import numpy as np, ml_dtypes
CORES = [9,25,41,57]
N = 4
BF = ml_dtypes.bfloat16
S, NM, L, RO, TAU = 2048, 4096, 256, 4, 5
ST, C0, LN = S // L, 16 - RO, NM.bit_length() - 1
def pack(nm, st, kd, ac, fu):
    return np.where(fu, 1 + 2048 * nm + 32 * st + 16 * kd + ac, 0)
def done(e, x, w, kp):
    return {"ent": np.ascontiguousarray(e.reshape(N, 128, S)).astype(np.int32), "feat": np.ascontiguousarray(x.reshape(N, 128, NM)).astype(np.float32).astype(BF),
            "wt": np.ascontiguousarray(w.reshape(N, 128, 1)).astype(np.int32), "kap": np.ascontiguousarray(kp.reshape(N, 128, 1)).astype(np.int32)}
def pooled(rng, n, other):
    pool = rng.integers(0, NM, (8, 16, n)); pool[..., 0] = rng.choice(np.array([0, NM - 1]), (8, 16))
    j = (n * rng.random((N, 8, 16, S)) ** 2).astype(np.int64)
    v = pool[np.arange(8)[:, None, None], np.arange(16)[None, :, None], j]
    return np.where(rng.random(v.shape) < other, rng.integers(0, NM, v.shape), v)
def parts(rng, n, other):
    sh = (N, 8, 16, S); nm = pooled(rng, n, other)
    st = rng.integers(0, 64, sh); kd = (rng.random(sh) < 0.45).astype(np.int64); ac = rng.integers(0, 16, sh); fu = rng.random(sh) < 0.8
    x = (64 * rng.random((N, 8, 16, NM)) ** 2).astype(np.int64)
    return nm, st, kd, ac, fu, x, rng.integers(0, 256, (N, 8, 16)), rng.integers(0, 256, (N, 8, 16))
def setup_inputs(rng):
    nm, st, kd, ac, fu, x, w, kp = parts(rng, 24, 0.3)
    return done(pack(nm, st, kd, ac, fu), x, w, kp)
def setup_inputs_spread(rng):
    sh = (N, 8, 16, S)
    nm = np.exp2(LN * rng.random(sh)).astype(np.int64) - 1; nm = np.where(rng.random((1, 8, 16, 1)) < 0.5, NM - 1 - nm, nm)
    st = np.exp2(6 * rng.random(sh)).astype(np.int64) - 1; st = np.where(rng.random(sh) < 0.5, 63 - st, st)
    kd = (rng.random(sh) < rng.choice(np.array([0.1, 0.4, 0.8]), (N, 8, 1, 1))).astype(np.int64)
    fu = rng.random(sh) < rng.random((N, 8, 1, S))
    x = (np.exp2(6 * rng.random((N, 8, 1, NM))) * rng.random((N, 8, 16, NM))).astype(np.int64)
    w = np.exp2(8 * rng.random((N, 8, 16))).astype(np.int64) - 1; kp = 256 - np.exp2(8 * rng.random((N, 8, 16))).astype(np.int64)
    return done(pack(nm, st, kd, rng.integers(0, 16, sh), fu), x, w, kp)
def at_ends(rng, hi):
    o = np.argsort(rng.random((N, 8, 16)), axis=-1)
    return np.where(o < 11, hi * rng.integers(0, 2, o.shape), rng.integers(0, hi + 1, o.shape))
def setup_inputs_ends(rng):
    sh = (N, 8, 16, S); top = 2048 * NM
    z = 32 * 63 * rng.integers(0, 2, sh) + 15 * rng.integers(0, 2, sh) + 1
    e = np.where(rng.random(sh) < 0.28, 2048 * rng.integers(0, NM, sh) + z, top * rng.integers(0, 2, sh))
    k = rng.random((N, 8, 1, S)); last = 2048 * (NM - 1) + z
    e = np.where(k < 0.41, 16 + z, e); e = np.where(k < 0.37, z, e); e = np.where(k < 0.33, last, e)
    e = np.where(k < 0.26, 0, e); e = np.where(k < 0.16, top, e)
    x = 63 * (rng.random((N, 8, 16, NM)) < 0.2).astype(np.int64); x[..., NM - 1] = 63; x[..., 0] = 0
    w = at_ends(rng, 255); kp = at_ends(rng, 255); w[0, 7] = 255; w[N - 1, 7] = 255
    for c in [0, ST] + list(range(S - ST, S)): e[:, 7, :, c] = last[:, 7, :, c]
    u = 16 * 63 * 255 & 4095
    for m in (8, 15): e[0, 7, :, ((u * u >> 5) + int(kp[N - 1, 7, m]) * u) & (S - 1)] = top
    return done(e, x, w, kp)
def setup_inputs_corners(rng):
    nm, st, kd, ac, fu, x, w, kp = parts(rng, 6, 0.1); sh = kd.shape
    o = rng.permutation(8); md = o[(np.arange(8)[None, :] + (np.arange(N)[:, None] & 1)) & 7]; m4 = md[:, :, None, None]
    kd = np.where(m4 == 0, 1, np.where(m4 == 1, 0, kd)); fu = fu | (m4 == 1)
    fu = np.where(m4 == 2, rng.random((N, 8, 1, S)) < 0.5, fu)
    ac = np.where(m4 == 3, C0 - TAU - 1 + rng.integers(0, RO + 1, sh), ac); kd = np.where(m4 == 3, (rng.random(sh) < 0.7).astype(np.int64), kd)
    st = np.where(m4 == 4, 63 * rng.integers(0, 2, sh), st); st = np.where(m4 == 7, 31, st)
    kd = np.where(m4 == 6, ((np.arange(S)[None, :] & 15) != np.arange(16)[:, None]).astype(np.int64), kd); fu = fu | (m4 == 6)
    x = np.where(m4 == 5, 63, x); m3 = md[:, :, None]
    w = np.where(m3 == 4, 0, np.where(m3 == 7, 255, w)); kp = np.where(m3 == 6, 0, np.where(m3 == 7, 255, kp))
    return done(pack(nm, st, kd, ac, fu), x, w, kp)
def setup_inputs_ties(rng):
    nm, st, kd, ac, fu, x, w, kp = parts(rng, 3, 0.02); sh = st.shape
    st = rng.integers(0, 63, (1, 8, 16, 1)) + rng.integers(0, 2, sh)
    ac = rng.choice(np.array([0, C0 - TAU - 1, C0 - TAU, C0 - TAU + 1, C0, 15]), sh); fu = rng.random(sh) < 0.9
    e = pack(nm, st, kd, ac, fu)
    w[..., 0] |= 1; kp = np.argsort(rng.random((N, 8, 256)), axis=-1)[..., :16]
    nn = rng.integers(0, NM, (N, 8, 16)); c = np.zeros((N, 8, 16), np.int64)
    for r in range(N):
        for g in range(8):
            n = int(nn[r, g, 0])
            if int(np.add.reduce(w[r, g] * x[r, g, :, n])) & 1 == 0: x[r, g, 0, n] ^= 1
            u = int(np.add.reduce(w[r, g] * x[r, g, :, n])) & 4095
            c[r, g] = ((u * u >> 5) + kp[r, g] * u) & (S - 1)
    for r in range(N):
        for g in range(8):
            q = (r + 1) % N; l = min(i for i in range(17) if not np.any(c[r - 1, g] == ST * i))
            s = rng.integers(0, 64, 16); own = pack(nn[r, g], s, (np.arange(16) > 0).astype(np.int64), rng.integers(0, 16, 16), True)
            e[r, g, :, ST * l] = own
            d = rng.integers(1, 4, 16); m = np.sort(rng.permutation(16)[:2]); d[m] = np.array([1, 0]) if (r + g) & 1 else np.array([0, 1])
            miss = np.argsort(rng.random((16, 16)), axis=0) < d[None, :]
            hit = pack(nn[r, g][:, None], s[:, None] ^ rng.integers(1, 64, (16, 16)), rng.integers(0, 2, (16, 16)), rng.integers(0, 16, (16, 16)), True)
            no = np.where(rng.random((16, 16)) < 0.5, 0, (((own - 1) >> 4) << 4)[:, None] + 1 + rng.integers(0, 16, (16, 16)))
            e[q, g][:, c[r, g]] = np.where(miss, no, hit)
    return done(e, x, w, kp)
def gone(v, c):
    return np.where((((37 * c + v) >> 3) & 7) == 0, v ^ 8, v)
def setup_inputs_crowd(rng):
    nm, st, kd, ac, fu, x, w, kp = parts(rng, 8, 0.2)
    e = np.take_along_axis(pack(nm, st, kd, ac, fu), rng.integers(0, 24, (N, 8, 1, S)), 3)
    kp[:, ::2] = kp[:, ::2, :1]
    h = int(rng.integers(0, 8)); kp[:, h] = 0; w[:, h] = 0; w[:, h, 0] = 1; w[:, h, 15] = 64
    cols = ST * np.arange(1, L); sh = (16, L - 1)
    for r in range(N):
        q = (r + 1) % N; o = rng.permutation(4096); c = (o * o >> 5) & (S - 1)
        first = np.unique(c, return_index=True)[1]; first = first[c[first] % ST != 0]
        u = o[rng.permutation(first)[:L - 1]]; p = (u * u >> 5) & (S - 1)
        names = rng.permutation(NM)[:L - 1]; x[r, h, 0, names] = u & 63; x[r, h, 15, names] = u >> 6
        it = rng.random(sh) < 0.4; it[0] = True; it[15] = True
        a = pack(np.where(it, names[None, :], rng.integers(0, NM, sh)), rng.integers(0, 64, sh), 1 - it.astype(np.int64), rng.integers(0, C0 - TAU, sh), True)
        b = pack(gone(rng.integers(0, NM, sh), p[None, :]), rng.integers(0, 64, sh), 1, rng.integers(0, C0 - TAU, sh), True)
        full = rng.random(L - 1) < 0.5; full[-1] = True
        e[r, h][:, cols] = a
        e[q, h][:, p] = np.where(full[None, :], b, a)
    e[:, h, :, 0] = pack(gone(rng.integers(0, NM, 16), 0), rng.integers(0, 64, 16), 1, rng.integers(0, C0 - TAU, 16), True)[None, :]
    return done(e, x, w, kp)
def check_inputs(d):
    bad = []
    for k, lo, hi in (("ent", 0, 2048 * NM), ("feat", 0, 63), ("wt", 0, 255), ("kap", 0, 255)):
        v = np.asarray(d[k]).astype(np.float64)
        if not (np.min(v) >= lo and np.max(v) <= hi): bad.append("range of " + k)
        elif np.any(v != np.floor(v)): bad.append("whole numbers in " + k)
    return bad
def item(a):
    return (a > 0) & ((((a - 1) >> 4) & 1) == 0)
def asleep(a, clock):
    return (a > 0) & ((((a - 1) >> 4) & 1) == 1) & (clock - ((a - 1) & 15) > TAU)
def stay(a, site, clock):
    return np.where(asleep(a, clock) & ((((37 * site + ((a - 1) >> 11)) >> 3) & 7) != 0), 0, a)
def meet(a, b, clock):
    same = (a > 0) & (b > 0) & (((a - 1) >> 11) == ((b - 1) >> 11)); big = np.maximum(a, b)
    wake = same & asleep(big, clock) & item(np.minimum(a, b))
    big = np.where(wake, (((big - 1) >> 4) << 4) + clock + 1, big)
    return np.where(same, big, np.where((a == 0) & ~asleep(b, clock), b, a)), np.where(same, big, np.where((b == 0) & ~asleep(a, clock), a, b))
def reference(ent, feat, wt, kap):
    E = ent.astype(np.int64).reshape(N, 8, 16, S); X = feat.astype(np.float32).astype(np.int64).reshape(N, 8, 16, NM)
    w = wt.astype(np.int64).reshape(N, 8, 16, 1); kp = kap.astype(np.int64).reshape(N, 8, 16, 1); A = [0] * N
    for t in range(RO):
        clock = C0 + t; lane = ST * np.arange(L) + t % ST; new = E.copy(); called = []
        for r in range(N):
            q = (r + 1 + t % (N - 1)) % N
            a = E[r][:, :, lane]
            x = np.take_along_axis(X[r], np.maximum((a - 1) >> 11, 0).reshape(8, 1, 16 * L), 2).reshape(8, 16, 16, L)
            y = np.max(np.where(item(a)[:, None], x, 0), axis=2)
            u = np.add.reduce(w[r] * y, axis=1)[:, None, :] & 4095
            e = ((u * u >> 5) + kp[r] * u + A[r]) & (S - 1)
            cand = np.take_along_axis(E[q], e.reshape(8, 1, 16 * L), 2).reshape(8, 16, 16, L) - 1
            own = a[:, :, None, :] - 1
            score = np.add.reduce((((cand >> 11) == (own >> 11)) & ((cand >> 4) != (own >> 4))).astype(np.int64), axis=1)
            p = np.take_along_axis(e, np.argmax(score, axis=1)[:, None, :], 1)
            win = np.zeros((8, L), bool)
            for g in range(8): win[g, np.unique(p[g, 0], return_index=True)[1]] = True
            b = np.take_along_axis(E[q], p, 2)
            na, nb = meet(stay(a, lane[None, None, :], clock), stay(b, p, clock), clock)
            new[r][:, :, lane] = np.where(win[:, None, :], na, a)
            called.append((q, p[:, 0], win, nb)); A[r] = int(np.count_nonzero(win)) & 31
        for q, p, win, nb in called:
            for g in range(8): new[q, g][:, p[g, win[g]]] = nb[g][:, win[g]]
        E = new
    return {"yent": E.reshape(N, 128, S).astype(np.float32)}

@@ -1,0 +1,633 @@
+from concourse.mybir import AluOpType as OP, ActivationFunctionType as AF
+
+L, S, NM, RO, C0 = 256, 2048, 4096, 4, 12
+SW_ = S + L
+NCH = 8
+CW = 4096 // NCH
+NV, WV = 3, 1
+AH1, AH2, AH3 = 6.0, 3.0, 3.0
+EQV = 9
+CY, WAKE, HOP, FX = 0.00083, 0.15, 3.5, 0.03
+
+F32, BF, I32, U16, F16 = "float32", "bfloat16", "int32", "uint16", "float16"
+SCRATCH = {}
+PART = {}
+for _buf, _d, _parts in (
+        ("KI", I32, (("pidx pm", 1), ("c64 c64b", 64), ("k4", L), ("k5", 16))),
+        ("KF", F32, (("wtF kapF pmF p0 kcol lc an aq", 1), ("wcol", 2), ("io16 io1 ucol LL P1 P1n t16 u16", 16))),
+        ("TI", I32, (("s1 lo1 lob sb ui um sq sq5 es e2 o1 o2", L),)),
+        ("TF", F32, (("nf fa fw fl sg sh lo wn wnb wf kc key TK PBf CP bx XH dd dq d2 sm na nb nbc", L),)),
+        ("TB", BF, (("Y lose junk", L),)), ("TU", U16, (("LS", L), ("pl PL", 16)))):
+    _o = 0
+    for _names, _w in _parts:
+        for _n in _names.split():
+            PART[_n] = (_buf, _o, _w)
+            _o += _w
+    SCRATCH[_buf] = ("sbuf", [128, _o], _d)
+for _names, _w, _d in (
+        ("ENT ENT2", S, I32), ("Np Ip Wp", SW_, F32), ("FA FB", NM + 16, BF), ("PI CC", S, F32),
+        ("wtS kapS", 1, I32), ("CT", 17 * 128, F32), ("ones SEL0", 128, F32), ("WL AC", 512, BF), ("BD", 128, BF), ("SC IX UT", 2048, BF),
+        ("SWP", 512, F16), ("IDH", 128, F16), ("PB idx TT", L, F16), ("ZE", L, BF), ("MK", 128, F32), ("pf", 16, F16), ("OR", 4096, F32), ("D A1 B1 IN", 4096, BF)):
+    for _n in _names.split():
+        SCRATCH[_n] = ("sbuf", [128, _w], _d)
+for _n, _m, _w, _d in (("EQ", 16, 256, BF), ("EA", 16 - EQV, 256 - 16 * EQV, BF), ("si", 2, L, I32),
+                       ("z", 2, L, I32), ("c", 2, L, F32), ("X1", 2, L, F32), ("e0", 2, L, F32), ("M", 2, L, F32)):
+    SCRATCH[_n] = ("sbuf", [128, _m, _w], _d)
+for _n in "ps_u ps_s0 ps_s1 ps_d".split():
+    SCRATCH[_n] = ("psum", [128, 512], F32)
+SCRATCH["ps_p"] = ("psum", [128, 32, 16], F32)
+SCRATCH["pA"] = SCRATCH["pB"] = ("psum", [128, 4, L // 2], F32)
+SCRATCH["pC"] = ("psum", [128, 2, L], F32)
+for _t in range(RO):
+    SCRATCH["ab%d" % _t] = ("sbuf", [128, L], F32)
+    SCRATCH["aL%d" % _t] = ("sbuf", [128, L], F32)
+    for _h in range(2):
+        SCRATCH["eb%d%d" % (_t, _h)] = ("sbuf", [128, 4, 32], U16)
+        SCRATCH["eL%d%d" % (_t, _h)] = ("sbuf", [128, L // 2], U16)
+    SCRATCH["nab%d" % _t] = ("sbuf", [128, L + 8], F32)
+    SCRATCH["naL%d" % _t] = ("sbuf", [128, L + 8], F32)
+SEMAPHORES = ["sV", "sS", "sT", "sG", "dEnt", "dFA", "dFB", "dW", "dK", "dY"]
+for _k in ("a%d", "e%d0", "e%d1", "n%d"):
+    for _t in range(RO):
+        SEMAPHORES += ["r" + _k % _t, "l" + _k % _t]
+
+
+def is_psum(b):
+    return b in SCRATCH and SCRATCH[b][0] == "psum"
+
+
+def make_tools(g, T):
+    queue = {"V": g.vector, "S": g.scalar, "T": g.tensor, "G": g, "Y": g.sync}
+    qsem = {"V": "sV", "S": "sS", "T": "sT", "G": "sG"}
+    nodes = []
+    log = {}
+    ahead = [0.0]
+
+    def touch(i, rg, wr):
+        q, comp, deps = nodes[i][0], nodes[i][7], nodes[i][6]
+        for (b, lo, hi) in rg:
+            for (l0, h0, w0, j) in log.get(b, []):
+                if j == i:
+                    continue
+                same = nodes[j][0] == q and comp and nodes[j][7]
+                if is_psum(b) and not same:
+                    deps[j] = True
+                elif is_psum(b) and q == "T":
+                    deps[j] = deps.get(j, False)
+                elif l0 < hi and lo < h0 and (w0 or wr):
+                    deps[j] = True
+
+    def note(i, rg, wr):
+        for (b, lo, hi) in rg:
+            ent = log.setdefault(b, [])
+            if wr and not is_psum(b):
+                ent[:] = [e for e in ent if not (lo <= e[0] and e[1] <= hi)]
+            ent.append((lo, hi, wr, i))
+
+    def run(q, fn, reads, writes, cost, sem=None, inc=1, lat=0.0):
+        nodes.append([q, fn, sem if sem else qsem[q], inc, cost, lat, {}, sem is None, ahead[0]])
+        i = len(nodes) - 1
+        touch(i, reads, False)
+        touch(i, writes, True)
+        note(i, reads, False)
+        note(i, writes, True)
+        return i
+
+    def landed(b, s, val, after, lat):
+        nodes.append([None, None, s, val, 0.0, lat, {after: True}, False, 0.0])
+        note(len(nodes) - 1, [(b, 0, 1 << 20)], True)
+
+    def plan():
+        n = len(nodes)
+        succ = [[] for _ in range(n)]
+        left = [len(nd[6]) for nd in nodes]
+        for i, nd in enumerate(nodes):
+            for j, w in nd[6].items():
+                succ[j].append((i, w))
+        way = [0.0] * n
+        for i in range(n - 1, -1, -1):
+            way[i] = nodes[i][4] + nodes[i][5] + max([way[k] + (WAKE if w else 0.0) for k, w in succ[i]] + [0.0])
+        for i, nd in enumerate(nodes):
+            way[i] += nd[8]
+        ready = {q: [] for q in queue}
+        free = {q: 0.0 for q in queue}
+        at = [0.0] * n
+        out = []
+
+        def opened(i):
+            if nodes[i][0] is None:
+                done(i, at[i])
+            else:
+                ready[nodes[i][0]].append(i)
+
+        def done(i, start):
+            fin = start + nodes[i][4]
+            for k, w in succ[i]:
+                if w:
+                    at[k] = max(at[k], fin + nodes[i][5] + (WAKE if nodes[k][0] is not None else 0.0))
+                left[k] -= 1
+                if left[k] == 0:
+                    opened(k)
+        for i in range(n):
+            if not nodes[i][6]:
+                opened(i)
+        while True:
+            best = None
+            for q, lst in ready.items():
+                if not lst:
+                    continue
+                first = min(max(at[i], free[q]) for i in lst)
+                i = max([i for i in lst if max(at[i], free[q]) <= first + 0.02], key=lambda i: (way[i], -i))
+                if best is None or first < best[0]:
+                    best = (first, q, i)
+            if best is None:
+                return out
+            q, i = best[1], best[2]
+            start = max(at[i], free[q])
+            free[q] = start + nodes[i][4]
+            ready[q].remove(i)
+            out.append(i)
+            done(i, start)
+
+    def issue():
+        total, val, know, known = {}, {}, {}, {q: {} for q in queue}
+        for i, nd in enumerate(nodes):
+            if nd[0] is None:
+                total[nd[2]] = total.get(nd[2], 0) + nd[3]
+                val[i], know[i] = total[nd[2]], {}
+        for i in plan():
+            q, fn, s, inc = nodes[i][:4]
+            deps = [j for j, w in nodes[i][6].items() if w]
+            best = {}
+            for j in deps:
+                sj = nodes[j][2]
+                if known[q].get(sj, 0) < val[j]:
+                    best[sj] = max(best.get(sj, 0), val[j])
+            for j in deps:
+                for sk, vk in know[j].items():
+                    if best.get(nodes[j][2]) == val[j] and sk in best and sk != nodes[j][2] and best[sk] <= vk:
+                        del best[sk]
+            for sk, vk in best.items():
+                queue[q].wait_ge(T.sem[sk], vk)
+                known[q][sk] = max(known[q].get(sk, 0), vk)
+            for j in deps:
+                for sk, vk in know[j].items():
+                    known[q][sk] = max(known[q].get(sk, 0), vk)
+            total[s] = total.get(s, 0) + inc
+            val[i] = total[s]
+            ins = fn(queue[q])
+            if ins is not None:
+                ins.then_inc(T.sem[s], inc)
+            know[i] = dict(known[q])
+        for s, x in total.items():
+            if known["G"].get(s, 0) < x:
+                g.wait_ge(T.sem[s], x)
+    return run, landed, issue, ahead
+
+
+def rank_program(g, core, T, topo):
+    rank = T.rank_of(core)
+    if rank is None:
+        return
+    run, landed, issue, ahead = make_tools(g, T)
+    cores = list(T.cores)
+
+    def size(b):
+        n = 1
+        for d in SCRATCH[b][1][1:]:
+            n *= d
+        return n
+
+    def v(b, lo=0, hi=None, st=1):
+        if b in PART:
+            b, o, w = PART[b]
+            lo, hi = o + lo, o + (w if hi is None else hi)
+        elif len(SCRATCH[b][1]) == 3:
+            return (T[b][:], [(b, 0, size(b))], size(b))
+        hi = size(b) if hi is None else hi
+        return (T[b][:, lo:hi] if st == 1 else T[b][:, lo:hi:st], [(b, lo, hi)], len(range(lo, hi, st)))
+
+    def v3(b, i, lo, hi):
+        m, w = SCRATCH[b][1][1:]
+        if not isinstance(i, int):
+            i0, i1 = (0, m) if i is None else i
+            return (T[b][:, i0:i1, lo:hi], [(b, k * w + lo, k * w + hi) for k in range(i0, i1)], (i1 - i0) * (hi - lo))
+        return (T[b][:, i, lo:hi], [(b, i * w + lo, i * w + hi)], hi - lo)
+
+    def vp(lo, hi, st=1):
+        return (T.ps_p[:, 0, lo:hi] if st == 1 else T.ps_p[:, 0, lo:hi:st], [("ps_p", lo, hi)], len(range(lo, hi, st)))
+
+    def at(b, o):
+        return (T[b][:].indirect(o[0]), [(b, 0, size(b))] + o[1], 16 * o[2], True)
+
+    def isv(x):
+        return isinstance(x, tuple)
+
+    def regs(*xs):
+        out = []
+        for x in xs:
+            if isv(x):
+                out += x[1]
+        return out
+
+    def ap(x):
+        return x[0] if isv(x) else x
+
+    def wide(*xs):
+        return any(SCRATCH[x[1][0][0]][2] in (F32, I32) for x in xs)
+
+    def ts(o, a, s1, op0, s2=None, op1=None):
+        if op1 is None:
+            f = lambda e: e.tensor_scalar(out=o[0], in0=a[0], scalar1=ap(s1), scalar2=None, op0=op0)
+        else:
+            f = lambda e: e.tensor_scalar(out=o[0], in0=a[0], scalar1=ap(s1), scalar2=ap(s2), op0=op0, op1=op1)
+        run("V", f, regs(a, s1, s2), regs(o), 0.05 + max(64, o[2] * (1.0 if wide(o, a) else 0.5)) * CY)
+
+    def tt(o, a, b, op):
+        k = 1.5 if len(a) > 3 else 1.0 if any(is_psum(x[1][0][0]) for x in (a, b)) else 2.0
+        run("V", lambda e: e.tensor_tensor(out=o[0], in0=a[0], in1=b[0], op=op), regs(a, b), regs(o), 0.05 + max(64, o[2] * k) * CY)
+
+    def tc(o, a):
+        f = lambda e: e.tensor_copy(out=o[0], in_=a[0])
+        if len(o) > 3:
+            run("V", f, regs(a) + o[1][1:], o[1][:1], 0.05 + 3.8 * o[2] * CY)
+        else:
+            k = 1.5 if len(a) > 3 else 1.0 if wide(o, a) else 0.5
+            run("V", f, regs(a), regs(o), 0.05 + max(64, o[2] * k) * CY)
+
+    def fill(o, c):
+        run("V", lambda e: e.memset(o[0], c), [], regs(o), 0.05 + o[2] * CY * (1.0 if wide(o) else 0.5))
+
+    def vtr(o, a):
+        run("V", lambda e: e.transpose(out=o[0], in_=a[0]), regs(a), regs(o), 0.05 + o[2] * CY)
+
+    def scan(o, m, a):
+        run("V", lambda e: e.tensor_tensor_scan(out=o[0], data0=m[0], data1=a[0], initial=0.0, op0=OP.mult, op1=OP.max), regs(m, a), regs(o), FX + o[2] * CY)
+
+    def act(o, a, func, scale=1.0, bias=0.0, accum=None):
+        b0, s0 = ap(bias), ap(scale)
+        if accum is None:
+            f = lambda e: e.activation(out=o[0], in_=a[0], func=func, bias=b0, scale=s0)
+        else:
+            f = lambda e: e.activation(out=o[0], in_=a[0], func=func, bias=b0, scale=s0, accum_out=accum[0])
+        run("S", f, regs(a, bias, scale), regs(o, accum), 0.065 + max(64, o[2] * (1.5 if len(a) > 3 else 1.0)) * CY)
+
+    def mm(o, lT, r, start, stop):
+        k = 4.0 if SCRATCH[lT[1][0][0]][2] == F32 else 1.0
+        run("T", lambda e: e.matmul(out=o[0], lhsT=lT[0], rhs=r[0], start=start, stop=stop), regs(lT, r), regs(o), 0.00071 * k * max(64, o[2]))
+
+    def iota(o, pattern, base, cm):
+        if SCRATCH[o[1][0][0]][2] != I32:
+            f = lambda e: e.iota(o[0], pattern, base, cm, allow_small_or_imprecise_dtypes=True)
+        else:
+            f = lambda e: e.iota(o[0], pattern, base, cm)
+        run("G", f, [], regs(o), 0.13 + 2 * o[2] * CY)
+
+    def asel(o, a, pattern, cmp, base, cm):
+        run("G", lambda e: e.affine_select(out=o[0], in_=a[0], pattern=pattern, compare_op=cmp, fill=0.0, base=base, channel_multiplier=cm), regs(a), regs(o), 0.17 + 2 * o[2] * CY)
+
+    def send(src, dst, to, frm, kind):
+        rid, pid = topo.addr(to)[:2]
+        m = topo.mask(core, to)
+        rs, ls = "r" + kind, "l" + kind
+
+        def f(e):
+            e.remote_dma(out_ap=T[dst][:], in_ap=T[src][:], remote_sem=T.sem[rs], local_sem=T.sem[ls], pid=pid, routing_id=rid, dma_engine_mask=m)
+        i = run("G", f, [(src, 0, size(src))], [], 0.1, sem=ls, inc=len(topo.engines(core, to)))
+        landed(dst, rs, len(topo.engines(frm, core)), i, HOP)
+
+    run("Y", lambda e: e.dma_start(T.ENT[:], T.ent[:]), [], regs(v("ENT")), 0.1, "dEnt", 16, 5.0)
+    run("S", lambda e: e.dma_start(T.wtS[:], T.wt[:]), [], regs(v("wtS")), 0.1, "dW", 16, 2.0)
+    run("S", lambda e: e.dma_start(T.kapS[:], T.kap[:]), [], regs(v("kapS")), 0.1, "dK", 16, 2.0)
+
+    def load(q, buf, par, sem):
+        def f(e):
+            for a in range(4):
+                for h in range(2):
+                    e.dma_start(T[buf][32 * a + 16 * h:32 * a + 16 * h + 16, 0:NM], T.feat[32 * a + 16 * par:32 * a + 16 * par + 16, :]).then_inc(T.sem[sem], 16)
+        run(q, f, [], [(buf, 0, NM)], 0.8, sem, 128, 8.0)
+    load("Y", "FA", 0, "dFA")
+    load("S", "FB", 1, "dFB")
+
+    fill(v("ones"), 1.0)
+    fill(v("FA", NM, NM + 16), 0.0)
+    fill(v("FB", NM, NM + 16), 0.0)
+    fill(v("Np", S, SW_), 0.0)
+    fill(v("Wp", S, SW_), 0.0)
+    fill(v("Ip", S, SW_), 0.0)
+    fill(v("ZE"), 0.0)
+    fill(v("MK"), 1.0)
+    fill(v("MK", 0, 128, 16), 0.0)
+    fill(v("SC"), 0.0)
+    fill(v("IX"), 0.0)
+    for t in range(RO):
+        fill(v("nab%d" % t, L, L + 8), 0.0)
+
+    def slot(k, n=1):
+        return v("CT", 128 * k, 128 * (k + n))
+    iota(v("pidx"), [[0, 1]], 0, 1)
+    iota(v("c64"), [[37, 64]], 0, 0)
+    iota(v("io1"), [[1, 16]], 0, 0)
+    iota(v("io16"), [[16, 16]], S, 0)
+    asel(slot(10), v("ones"), [[-16, 8], [0, 16]], OP.is_ge, 0, 1)
+    asel(slot(11), slot(10), [[16, 8], [0, 16]], OP.is_ge, 15, -1)
+    asel(slot(12), v("ones"), [[-1, 128]], OP.is_equal, 0, 1)
+    for p in range(2):
+        asel(slot(p), v("ones"), [[-32, 4], [0, 2], [-1, 16]], OP.is_equal, -16 * p, 1)
+    for p in range(2):
+        for h in range(2):
+            k = 2 + 2 * (2 * p + h)
+            asel(slot(k), v("ones"), [[-32, 4], [-1000 if p == 0 else 1000, 2], [0, 16]], OP.is_ge, -16 * h - (1000 if p else 0), 1)
+            asel(slot(k + 1), slot(k), [[32, 4], [0, 2], [0, 16]], OP.is_ge, 15 + 16 * h, -1)
+    for h in range(2):
+        for p in range(2):
+            asel(slot(13 + 2 * h + p), v("ones"), [[-32, 4], [984, 2], [-1, 16]], OP.is_equal, 16 * (p - h) - 1000 * p, 1)
+    iota(v("PI"), [[1, S]], 0, 0)
+    tc(v("wtF"), v("wtS"))
+    tc(v("kapF"), v("kapS"))
+    for p in range(2):
+        mm(vp(p, p + 1), slot(p), v("wtF"), True, True)
+    tc(v("wcol"), vp(0, 2))
+    for p in range(2):
+        for h in range(2):
+            k = 2 * p + h
+            ts(v("WL", 128 * k, 128 * k + 128), slot(2 + 2 * k + 1), v("wcol", p, p + 1), OP.mult)
+    ts(v("pm"), v("pidx"), 15, OP.bitwise_and)
+    tc(v("pmF"), v("pm"))
+    ts(v("p0"), v("pmF"), 0.0, OP.is_equal)
+    ts(v("kcol"), v("pmF"), -2048.0, OP.mult, 15.0 * 2048, OP.add)
+    ts(v("LL"), v("io16"), v("pmF"), OP.add)
+    ts(v("ucol"), v("io1"), v("pmF"), OP.is_gt)
+    for x in range(1, 16):
+        act(v("UT", 128 * x, 128 * x + 128), slot(11), AF.Copy, scale=v("ucol", x, x + 1))
+    ts(v("SEL0"), v("ones"), v("p0"), OP.mult)
+    tc(v("BD"), slot(11))
+    for q in range(8):
+        act(v("SC", 16 * q, 16 * q + 129 * 15 + 1, 129), v("CT", 128 * 11 + 16 * q, 128 * 11 + 16 * q + 16), AF.Copy, scale=32768.0)
+        tc(v("IX", 16 * q, 16 * q + 129 * 15 + 1, 129), v("CT", 128 * 12 + 16 * q, 128 * 12 + 16 * q + 16))
+    tc(v("SWP"), slot(13, 4))
+    tc(v("IDH"), slot(12))
+    ts(v("c64b"), v("c64"), 63, OP.bitwise_and)
+    ts(v("CC", 0, 64), v("c64b"), 4096.0, OP.mult, -262144.0 - 2033.0, OP.add)
+    n = 64
+    while n < S:
+        act(v("CC", n, 2 * n), v("CC", 0, n), AF.Copy)
+        n *= 2
+
+    def entries(o, x, tmp):
+        ts(tmp, x, 2047, OP.add)
+        ts(tmp, tmp, -2048, OP.bitwise_and)
+        tt(o, x, tmp, OP.add)
+    entries(v("ab0"), v("ENT", 0, S, 8), v("o1"))
+    for k in range(NV):
+        entries(v("Np", 512 * k, 512 * k + 512), v("ENT", 512 * k, 512 * k + 512), v("ENT2", 512 * k, 512 * k + 512))
+
+    BIG, MID = 12582912.0, 8387584.0
+
+    for k in range(NV, 4):
+        lo, hi = 512 * k, 512 * k + 512
+        num, quo, bank = v("OR", S + lo, S + hi), v("OR", lo, hi), v("ps_u" if k == 2 else "ps_d")
+        tc(num, v("ENT", lo, hi))
+        act(quo, num, AF.Identity, scale=2.0 ** -11, bias=2047 / 4096)
+        act(quo, quo, AF.Identity, bias=BIG)
+        act(bank, quo, AF.Identity, scale=2048.0, bias=-2048.0 * BIG)
+        tt(v("Np", lo, hi), num, bank, OP.add)
+
+    def mid(o, x):
+        act(o, x, AF.Identity, bias=-MID)
+
+    def w_of(o, x, tmp):
+        act(tmp, x, AF.Identity, scale=1 / 16, bias=-2056.5 / 16)
+        act(tmp, tmp, AF.Identity, bias=BIG)
+        act(o, tmp, AF.Identity, bias=MID / 16 - BIG)
+
+    def n32_of(o, x, tmp):
+        act(tmp, x, AF.Identity, scale=1 / 32, bias=-2048.5 / 32)
+        act(tmp, tmp, AF.Identity, bias=BIG)
+        act(tmp, tmp, AF.Identity, bias=-BIG)
+        act(o, tmp, AF.Identity, scale=32.0, bias=MID + 2033)
+
+    back = None
+    for t in range(RO):
+        clock = C0 + t
+        thr = clock - 5
+        d = 1 + t % 3
+        to, frm = cores[(rank + d) % 4], cores[(rank - d) % 4]
+        ab, aL, eb, eL, nab, naL = ["%s%d" % (x, t) for x in ("ab", "aL", "eb", "eL", "nab", "naL")]
+        prev = "naL%d" % (t - 1)
+
+        lanes = v("Np", t, S, 8) if t else v("ab0")
+        ts(v("s1"), lanes, -2033, OP.add)
+        act(v("nf"), lanes, AF.Identity, scale=2.0 ** -12, bias=BIG)
+        act(v("nf"), v("nf"), AF.Identity, bias=-BIG - 1 - 2048)
+        if t:
+            act(v(ab), lanes, AF.Copy)
+        send(ab, aL, to, frm, "a%d" % t)
+        ts(v("lo1"), v("s1"), 31, OP.bitwise_and)
+        dm = v3("pC", 0, 0, L)
+        ts(dm, v("lo1"), 16, OP.is_lt, 8192.0, OP.mult)
+        tt(v("idx"), v("nf"), dm, OP.add)
+        vtr(v("TT"), v("idx"))
+        for b in range(8):
+            mm(v("ps_s%d" % (b // 4), b % 4, 128, 4), v("IDH"), v("TT", 32 * b, 32 * b + 32), True, True)
+        for s in range(2):
+            ts(v("LS", 128 * s, 128 * s + 128), v("ps_s%d" % s, 0, 128), 2048.0, OP.add, 4096.0, OP.min)
+        if t:
+            back(t - 1)
+        for s in range(2):
+            lo, hi = 128 * s, 128 * s + 128
+            ahead[0] = AH1 if s == 0 else 0.0
+            for k in range(8):
+                for p in range(2):
+                    o = 256 * s + 128 * p
+                    acc = v("AC", o, o + 128)
+                    win = at("FB" if p else "FA", v("LS", lo + 64 * p + 8 * k, lo + 64 * p + 8 * k + 8))
+                    if k == 0:
+                        act(acc, win, AF.Copy)
+                    else:
+                        tt(acc, win, acc, OP.max)
+            for p in range(2):
+                o = 256 * s + 128 * p
+                tt(v("Y", lo + 64 * p, lo + 64 * p + 64), v("AC", o, o + 64), v("AC", o + 64, o + 128), OP.max)
+            for h in range(2):
+                for p in range(2):
+                    k = 2 * p + h
+                    mm(v("ps_u", lo + 64 * h, lo + 64 * h + 64), v("WL", 128 * k, 128 * k + 128), v("Y", lo + 64 * p, lo + 64 * p + 64), p == 0, p == 1)
+            tc(v("ui", lo, hi), v("ps_u", lo, hi))
+            ts(v("um", lo, hi), v("ui", lo, hi), 4095, OP.bitwise_and)
+            tt(v("sq", lo, hi), v("um", lo, hi), v("um", lo, hi), OP.mult)
+            ku = v3("pC", 0, lo, hi)
+            if t:
+                ts(ku, v("um", lo, hi), v("kapF", 0, 1), OP.mult, v(prev, L, L + 1), OP.add)
+            else:
+                ts(ku, v("um", lo, hi), v("kapF", 0, 1), OP.mult)
+            ts(v("sq5", lo, hi), v("sq", lo, hi), 5, OP.arith_shift_right)
+            tt(v("es", lo, hi), v("sq5", lo, hi), ku, OP.add)
+            ts(v("e2", lo, hi), v("es", lo, hi), 2047, OP.bitwise_and)
+            for h in range(2):
+                tc(v3("%s%d" % (eb, s), None, 16 * h, 16 * h + 16), v("e2", lo + 64 * h, lo + 64 * h + 64))
+            send("%s%d" % (eb, s), "%s%d" % (eL, s), to, frm, "e%d%d" % (t, s))
+            ahead[0] = 0.0
+
+        if t == 0:
+            for k in range(WV):
+                lo, hi = 512 * k, 512 * k + 512
+                ts(v("ENT", lo, hi), v("Np", lo, hi), -2049, OP.add)
+                ts(v("ENT2", lo, hi), v("ENT", lo, hi), 4, OP.arith_shift_right)
+                ts(v("Wp", lo, hi), v("ENT2", lo, hi), -128.0, OP.max)
+            for k in range(WV, 4):
+                lo, hi = 512 * k, 512 * k + 512
+                mid(v("OR", lo, hi), v("Np", lo, hi))
+                w_of(v("Wp", lo, hi), v("OR", lo, hi), v("OR", lo, hi))
+        else:
+            act(v("Np", t - 1, S, 8), v(prev, 0, L), AF.Copy)
+            mid(v("wn"), v(prev, 0, L))
+            w_of(v("Wp", t - 1, S, 8), v("wn"), v("wn"))
+            tc(at("Np", v("PL")), v("nb"))
+            tc(at("Wp", v("PL")), v("wnb"))
+        mid(v("fa"), v(aL))
+        w_of(v("wf"), v("fa"), v("fw"))
+        for m in range(16):
+            act(v("OR", m, 4096, 16), v("wf"), AF.Copy)
+
+        def side(x, k, s):
+            lo, hi = 128 * s, 128 * s + 128
+            far = v3("pB" if s else "pA", 1 - k, 0, 128)
+            tt(v3("pC", k, lo, hi), v3("z", k, lo, hi), far, OP.is_le)
+            tt(v3("X1", k, lo, hi), x, v3("pC", k, lo, hi), OP.mult)
+            tt(far, x, far, OP.mult)
+            act(v3("e0", k, lo, hi), v3("X1", k, lo, hi), AF.Relu, scale=-2.0 ** -18, bias=2.0 ** -18)
+
+        act(v("ps_s0", L, 2 * L), v("CC", t, S, 8), AF.Copy)
+        tt(v3("si", 0, 0, L), v(aL), v("ps_s0", L, 2 * L), OP.add)
+        ts(v3("z", 0, 0, L), v3("si", 0, 0, L), 7 << 15, OP.bitwise_and)
+        n32_of(v("ps_d", L, 2 * L), v("fa"), v("fl"))
+        tt(v("lo"), v(aL), v("ps_d", L, 2 * L), OP.subtract)
+        act(v("sg"), v("lo"), AF.Sign, bias=0.5 - thr)
+        act(v("sh"), v("lo"), AF.Sign, bias=-15.5)
+        act(v3("c", 0, 0, L), v("lo"), AF.Identity, scale=-1.0, bias=float(clock))
+        for s in range(2):
+            act(v3("pB" if s else "pA", 1, 0, 128), v("sg", 128 * s, 128 * s + 128), AF.Relu, scale=262144.0)
+            act(v3("pB" if s else "pA", 3, 0, 128), v("sh", 128 * s, 128 * s + 128), AF.Relu, scale=float(thr))
+            side(v(aL, 128 * s, 128 * s + 128), 0, s)
+        for s in range(2):
+            ts(v("kc", 128 * s, 128 * s + 128), v("%s%d" % (eL, s)), v("kcol", 0, 1), OP.add)
+        for k in range(NCH):
+            lo, hi, n = CW * k, CW * k + CW, CW // 16
+            q = k * n
+            ahead[0] = AH2 if k < NCH // 2 else 0.0
+            tt(v("D", lo, hi), at("Wp", v("%s%d" % (eL, q // 128), q % 128, q % 128 + n)), v("OR", lo, hi), OP.subtract)
+            act(v("A1", lo, hi), v("D", lo, hi), AF.Abs)
+            act(v("B1", lo, hi), v("A1", lo, hi), AF.Abs, bias=-64.0)
+            ts(v("IN", lo, hi), v("B1", lo, hi), 63.5, OP.is_lt)
+            for m in range(16):
+                mm(v("ps_s%d" % (q // 128), q % 128, q % 128 + n), v("SC", 128 * m, 128 * m + 128), v("IN", lo + m, hi, 16), m == 0, m == 15)
+        for s in range(2):
+            lo, hi = 128 * s, 128 * s + 128
+            ahead[0] = AH3 if s == 0 else 0.0
+
+            def f(b, n, o=0, st=1):
+                return v(b, n * s + o, n * s + n, st)
+            tt(f("key", 128), v("ps_s%d" % s, 0, 128), f("kc", 128), OP.add)
+            vtr(f("TK", 128), f("key", 128))
+            scan(f("k4", 128), v("MK"), f("TK", 128))
+            ts(f("k5", 8), f("k4", 128, 15, 16), 2047, OP.bitwise_and)
+            tc(f("pf", 8), f("k5", 8))
+            for h in range(2):
+                for p in range(2):
+                    k = 2 * h + p
+                    mm(vp(8 * s + h, 8 * s + 8, 2), v("SWP", 128 * k, 128 * k + 128), f("pf", 8, p, 2), p == 0, p == 1)
+            tc(f("pl", 8), vp(8 * s, 8 * s + 8))
+            act(f("P1", 8), vp(8 * s, 8 * s + 8), AF.Copy)
+            act(f("P1n", 8), f("P1", 8), AF.Copy, scale=-1.0)
+            act(f("CP", 128), at("CC", f("pl", 8)), AF.Copy)
+            act(f("bx", 128), at("Np", f("pl", 8)), AF.Copy)
+            tc(f("PB", 128), at("PI", f("pl", 8)))
+            P, low = "pB" if s else "pA", f("lob", 128)
+            tt(v3("si", 1, lo, hi), at("Np", f("pl", 8)), f("CP", 128), OP.add)
+            ts(low, v3("si", 1, lo, hi), 31, OP.bitwise_and)
+            ts(v3("z", 1, lo, hi), v3("si", 1, lo, hi), 7 << 15, OP.bitwise_and)
+            ts(v3(P, 0, 0, 128), low, thr, OP.is_ge, 262144.0, OP.mult)
+            ts(v3(P, 2, 0, 128), low, 16, OP.is_ge, float(thr), OP.mult)
+            ts(v3("c", 1, lo, hi), low, -1.0, OP.mult, float(clock), OP.add)
+            side(f("bx", 128), 1, s)
+            a = v3("X1", 0, lo, hi)
+            tt(f("dd", 128), a, f("bx", 128), OP.subtract)
+            act(f("dq", 128), f("dd", 128), AF.Square, scale=2.0 ** -11)
+            ts(f("sm", 128), f("dq", 128), 1.0, OP.is_lt)
+            tt(f("sm", 128), f("sm", 128), v3("pC", 1, lo, hi), OP.mult)
+            both, big = v3(P, (2, 4), 0, 128), v3(P, 3, 0, 128)
+            tt(v3(P, 2, 0, 128), f("lo", 128), v3(P, 2, 0, 128), OP.is_lt)
+            tt(big, low, big, OP.is_lt)
+            tt(both, v3("c", None, lo, hi), both, OP.mult)
+            tt(f("XH", 128), a, v3(P, 2, 0, 128), OP.add)
+            tt(big, f("bx", 128), big, OP.add)
+            tt(big, f("XH", 128), big, OP.max)
+            tt(big, f("sm", 128), big, OP.mult)
+            fil = v3(P, (0, 2), 0, 128)
+            tt(fil, v3("e0", None, lo, hi), fil, OP.mult)
+            tt(v3("M", None, lo, hi), v3("X1", None, lo, hi), fil, OP.max)
+            tt(f("nb", 128), v3("M", 1, lo, hi), big, OP.max)
+        ahead[0] = 0.0
+        act(v("PBf", 128, L), at("PI", v("pl", 8, 16)), AF.Copy)
+        for c in range(16):
+            n = 256 - 16 * c
+            if c < EQV:
+                ts(v3("EQ", c, 0, n), v("PB", 16 * c, 256), v("P1", c, c + 1), OP.is_equal)
+            else:
+                act(v3("EA", c - EQV, 0, n), v("PBf", 16 * c, 256), AF.Abs, bias=v("P1n", c, c + 1))
+                act(v3("EQ", c, 0, n), v3("EA", c - EQV, 0, n), AF.Relu, scale=-1.0, bias=1.0)
+        mm(v("ps_d", 0, 256), v("BD"), v("ZE"), True, False)
+        for c in range(15):
+            mm(v("ps_d", 16 * c + 16, 256), v("BD"), v3("EQ", c, 16, 256 - 16 * c), False, False)
+        for x in range(1, 16):
+            col = (T.EQ[:, 0:16, x], [("EQ", 256 * c + x, 256 * c + x + 1) for c in range(16)], 16)
+            mm(v("ps_d", x, 256, 16), v("UT", 128 * x, 128 * x + 128), col, False, x == 15)
+        act(v("lose"), v("ps_d", 0, 256), AF.Sign, accum=v("lc"))
+        for x in range(16):
+            mm(v("ps_d", 256, 272), v("IX", 128 * x, 128 * x + 128), v("lose", x, 256, 16), x == 0, x == 15)
+        tt(v("t16"), v("LL"), v("ps_d", 256, 272), OP.mult)
+        tt(v("u16"), v("t16"), v("P1"), OP.max)
+        tc(v("PL"), v("u16"))
+        if t < RO - 1:
+            mm(v3("ps_p", 2, 0, 1), v("SEL0"), v("lc"), True, True)
+
+        def back(t, aL=aL, nab=nab, to=to, frm=frm, naL=naL):
+            na, df = v3("pC", 0, 0, L), v3("pC", 1, 0, L)
+            for s in range(2):
+                tt(v3("pC", 0, 128 * s, 128 * s + 128), v3("M", 0, 128 * s, 128 * s + 128), v3("pB" if s else "pA", 3, 0, 128), OP.max)
+            tt(df, v(aL), na, OP.subtract)
+            tt(v("na"), v("lose"), df, OP.mult)
+            tt(v(nab, 0, L), v("na"), na, OP.add)
+            if t < RO - 1:
+                act(v("an"), v3("ps_p", 2, 0, 1), AF.Copy, scale=-1.0)
+                act(v("aq"), v("an"), AF.Identity, scale=1 / 32, bias=-15.5 / 32)
+                act(v("aq"), v("aq"), AF.Identity, bias=BIG)
+                act(v("aq"), v("aq"), AF.Identity, bias=-BIG)
+                act(v(nab, L, L + 1), v("aq"), AF.Identity, scale=-32.0, bias=v("an"))
+            send(nab, naL, frm, to, "n%d" % t)
+            if t < RO - 1:
+                mid(v("wn"), v("nb"))
+                w_of(v("wnb"), v("wn"), v("wn"))
+
+        if t == RO - 1:
+            back(t)
+        else:
+            tc(at("Np", v("PL")), v("nb"))
+
+    for k in range(4):
+        lo, hi = 512 * k, 512 * k + 512
+        bank = v(("ps_u", "ps_s0", "ps_s1", "ps_u")[k])
+        act(v("OR", lo, hi), v("Np", lo, hi), AF.Identity, scale=2.0 ** -12, bias=BIG)
+        act(bank, v("OR", lo, hi), AF.Identity, scale=2048.0, bias=-2048.0 * BIG)
+        tt(v("Ip", lo, hi), v("Np", lo, hi), bank, OP.subtract)
+
+    def number(o, x):
+        ts(v("o1"), x, 2047, OP.add)
+        ts(v("o2"), v("o1"), 1, OP.arith_shift_right, -2048, OP.bitwise_and)
+        tt(o, x, v("o2"), OP.subtract)
+    number(v("nbc"), v("nb"))
+    number(v("Ip", RO - 1, S, 8), v("naL%d" % (RO - 1), 0, L))
+    tc(at("Ip", v("PL")), v("nbc"))
+    run("Y", lambda e: e.dma_start(T.yent[:], T.Ip[:, 0:S]), regs(v("Ip", 0, S)), [("yent", 0, S)], 0.1, "dY", 16, 6.0)
+    issue()

@@ -1,23 +1,25 @@
+import numpy as np
 from concourse.mybir import AluOpType as OP, ActivationFunctionType as AF
 
-L, S, NM, RO, C0 = 256, 2048, 4096, 4, 12
+L, H, S, NM, RO, C0 = 256, 128, 2048, 4096, 4, 12
 SW_ = S + L
-NCH = 8
-CW = 4096 // NCH
-NV, WV = 3, 1
+VG = (0,)
+SG = ((1, 2, 3), (0, 1, 2, 3))
 AH1, AH2, AH3 = 6.0, 3.0, 3.0
-EQV = 9
-CY, WAKE, HOP, FX = 0.00083, 0.15, 3.5, 0.03
+CY, WAKE, HOP, RATE, FX, GAT, SCA = 0.00083, 0.1, 2.0, 50e3, 0.02, 1.56, 3.8
 
 F32, BF, I32, U16, F16 = "float32", "bfloat16", "int32", "uint16", "float16"
+WEIGHTS = [1.0, -1.0, -16.0, 8.0, 3.0 * 2 ** 25, 2.0 ** 26, -2.0 ** 25, 2.0 ** 24, -2.0 ** 27, -11.0 * 2 ** 24, 5.0 * 2 ** 23, 6.0 * 2 ** 23, 2.0 ** 21]
 SCRATCH = {}
 PART = {}
 for _buf, _d, _parts in (
-        ("KI", I32, (("pidx pm", 1), ("c64 c64b", 64), ("k4", L), ("k5", 16))),
-        ("KF", F32, (("wtF kapF pmF p0 kcol lc an aq", 1), ("wcol", 2), ("io16 io1 ucol LL P1 P1n t16 u16", 16))),
-        ("TI", I32, (("s1 lo1 lob sb ui um sq sq5 es e2 o1 o2", L),)),
-        ("TF", F32, (("nf fa fw fl sg sh lo wn wnb wf kc key TK PBf CP bx XH dd dq d2 sm na nb nbc", L),)),
-        ("TB", BF, (("Y lose junk", L),)), ("TU", U16, (("LS", L), ("pl PL", 16)))):
+        ("KI", I32, (("c64 c64b", 64), ("j4", 32), ("jj j1 j2 j3", 8), ("pidx pm", 1))),
+        ("KF", F32, (("xp colv DGm DG", L), ("P1 um16", 16), ("wtF kapF pmF p0 an aq", 1), ("lc", 2))),
+        ("TI", I32, (("s1 kd E2 E3 k4 sia za sib zb o1", L), ("ui um sq s5 k5", 16))),
+        ("TF", F32, (("n1 wi E1 sA c1 aN l1 a1c an1 anum CP bN l1b b1 b1c bnum d0 ah big TT wd sc", L), ("KK k0", H))),
+        ("TB", BF, (("same lose ow EQd", L), ("TRI ONEB BDk", H), ("KC", 192), ("KD", 16), ("TG", 4 * H))),
+        ("TH", F16, (("E16 PB", L), ("IDH", H))),
+        ("TU", U16, (("idx EL", L), ("pl PL", 16), ("RU RK", 8), ("RC", 32)))):
     _o = 0
     for _names, _w in _parts:
         for _n in _names.split():
@@ -25,31 +27,29 @@ for _buf, _d, _parts in (
             _o += _w
     SCRATCH[_buf] = ("sbuf", [128, _o], _d)
 for _names, _w, _d in (
-        ("ENT ENT2", S, I32), ("Np Ip Wp", SW_, F32), ("FA FB", NM + 16, BF), ("PI CC", S, F32),
-        ("wtS kapS", 1, I32), ("CT", 17 * 128, F32), ("ones SEL0", 128, F32), ("WL AC", 512, BF), ("BD", 128, BF), ("SC IX UT", 2048, BF),
-        ("SWP", 512, F16), ("IDH", 128, F16), ("PB idx TT", L, F16), ("ZE", L, BF), ("MK", 128, F32), ("pf", 16, F16), ("OR", 4096, F32), ("D A1 B1 IN", 4096, BF)):
+        ("ENT", S, I32), ("Xp Ip", SW_, F32), ("OWN", SW_, BF), ("FT", NM + 16, BF), ("PI CC W1", S, F32), ("GS", 4096, F32),
+        ("wtS kapS", 1, I32), ("ones B0 B1 ID SEL0 MK", 128, F32), ("SC WX", 2048, BF), ("GF YS", 4096, BF), ("MB", 512, BF),
+        ("ab0", H + 16, F32), ("ab1 nab0 nab1", H, F32), ("us0 us1", 16, F32), ("Ab", 4, F32)):
     for _n in _names.split():
         SCRATCH[_n] = ("sbuf", [128, _w], _d)
-for _n, _m, _w, _d in (("EQ", 16, 256, BF), ("EA", 16 - EQV, 256 - 16 * EQV, BF), ("si", 2, L, I32),
-                       ("z", 2, L, I32), ("c", 2, L, F32), ("X1", 2, L, F32), ("e0", 2, L, F32), ("M", 2, L, F32)):
-    SCRATCH[_n] = ("sbuf", [128, _m, _w], _d)
-for _n in "ps_u ps_s0 ps_s1 ps_d".split():
+for _n in "Q1 Q2".split():
+    SCRATCH[_n] = ("sbuf", [128, 16, 16, 16], BF)
+SCRATCH["D"] = ("sbuf", [128, 4096], BF)
+SCRATCH["OR"] = ("sbuf", [128, 1024], F32)
+SCRATCH["EQ"] = ("sbuf", [128, 16, H], BF)
+SCRATCH["WM"] = ("sbuf", [128, len(WEIGHTS), 128], BF)
+for _n in "LAM SIG IOT EM EM0".split():
+    SCRATCH[_n] = ("sbuf", [128, 2, 2, H], BF)
+for _n in "pU pA pW pZ pD pS0 pS1".split():
     SCRATCH[_n] = ("psum", [128, 512], F32)
-SCRATCH["ps_p"] = ("psum", [128, 32, 16], F32)
-SCRATCH["pA"] = SCRATCH["pB"] = ("psum", [128, 4, L // 2], F32)
-SCRATCH["pC"] = ("psum", [128, 2, L], F32)
+SCRATCH["pO"] = ("psum", [128, 8, 4, 16], F32)
+MSG = (("a0", H + 16), ("a1", H), ("u0", 16), ("u1", 16), ("n0", H), ("n1", H), ("A", 4))
+SEMAPHORES = ["sV", "sS", "sT", "sG", "dE0", "dE1", "dF", "dW", "dK", "dY0", "dY1"]
 for _t in range(RO):
-    SCRATCH["ab%d" % _t] = ("sbuf", [128, L], F32)
-    SCRATCH["aL%d" % _t] = ("sbuf", [128, L], F32)
-    for _h in range(2):
-        SCRATCH["eb%d%d" % (_t, _h)] = ("sbuf", [128, 4, 32], U16)
-        SCRATCH["eL%d%d" % (_t, _h)] = ("sbuf", [128, L // 2], U16)
-    SCRATCH["nab%d" % _t] = ("sbuf", [128, L + 8], F32)
-    SCRATCH["naL%d" % _t] = ("sbuf", [128, L + 8], F32)
-SEMAPHORES = ["sV", "sS", "sT", "sG", "dEnt", "dFA", "dFB", "dW", "dK", "dY"]
-for _k in ("a%d", "e%d0", "e%d1", "n%d"):
-    for _t in range(RO):
-        SEMAPHORES += ["r" + _k % _t, "l" + _k % _t]
+    for _n, _w in MSG:
+        if _n != "A" or _t < RO - 1:
+            SCRATCH["L%s%d" % (_n, _t)] = ("sbuf", [128, _w], F32)
+            SEMAPHORES += ["r%s%d" % (_n, _t), "l%s%d" % (_n, _t)]
 
 
 def is_psum(b):
@@ -60,19 +60,19 @@ def make_tools(g, T):
     queue = {"V": g.vector, "S": g.scalar, "T": g.tensor, "G": g, "Y": g.sync}
     qsem = {"V": "sV", "S": "sS", "T": "sT", "G": "sG"}
     nodes = []
-    log = {}
+    log, seen = {}, {}
     ahead = [0.0]
 
     def touch(i, rg, wr):
-        q, comp, deps = nodes[i][0], nodes[i][7], nodes[i][6]
+        q, deps = nodes[i][0], nodes[i][6]
         for (b, lo, hi) in rg:
-            for (l0, h0, w0, j) in log.get(b, []):
+            bank = is_psum(b)
+            for (l0, h0, w0, j) in log.get(b, []) + (seen.get(b, []) if wr else []):
                 if j == i:
                     continue
-                same = nodes[j][0] == q and comp and nodes[j][7]
-                if is_psum(b) and not same:
+                if bank and nodes[j][0] != q:
                     deps[j] = True
-                elif is_psum(b) and q == "T":
+                elif bank and q == "T":
                     deps[j] = deps.get(j, False)
                 elif l0 < hi and lo < h0 and (w0 or wr):
                     deps[j] = True
@@ -80,8 +80,18 @@ def make_tools(g, T):
     def note(i, rg, wr):
         for (b, lo, hi) in rg:
             ent = log.setdefault(b, [])
-            if wr and not is_psum(b):
+            if is_psum(b):
+                q = nodes[i][0]
+                if ent and nodes[ent[-1][3]][0] != q:
+                    p, k = nodes[ent[-1][3]][0], len(ent)
+                    while k and nodes[ent[k - 1][3]][0] == p:
+                        k -= 1
+                    del ent[:k]
+            elif wr:
                 ent[:] = [e for e in ent if not (lo <= e[0] and e[1] <= hi)]
+                seen[b] = [e for e in seen.get(b, []) if not (lo <= e[0] and e[1] <= hi)]
+            else:
+                ent = seen.setdefault(b, [])
             ent.append((lo, hi, wr, i))
 
     def run(q, fn, reads, writes, cost, sem=None, inc=1, lat=0.0):
@@ -202,23 +212,17 @@ def rank_program(g, core, T, topo):
         if b in PART:
             b, o, w = PART[b]
             lo, hi = o + lo, o + (w if hi is None else hi)
-        elif len(SCRATCH[b][1]) == 3:
-            return (T[b][:], [(b, 0, size(b))], size(b))
         hi = size(b) if hi is None else hi
         return (T[b][:, lo:hi] if st == 1 else T[b][:, lo:hi:st], [(b, lo, hi)], len(range(lo, hi, st)))
 
-    def v3(b, i, lo, hi):
-        m, w = SCRATCH[b][1][1:]
-        if not isinstance(i, int):
-            i0, i1 = (0, m) if i is None else i
-            return (T[b][:, i0:i1, lo:hi], [(b, k * w + lo, k * w + hi) for k in range(i0, i1)], (i1 - i0) * (hi - lo))
-        return (T[b][:, i, lo:hi], [(b, i * w + lo, i * w + hi)], hi - lo)
+    def w(b, *ix):
+        ix = tuple(slice(*k) if isinstance(k, tuple) else k for k in ix)
+        flat = np.arange(size(b)).reshape(SCRATCH[b][1][1:])[ix].reshape(-1)
+        cut = [0] + [int(k) + 1 for k in np.nonzero(np.diff(flat) > 16)[0]] + [len(flat)]
+        return (T[b][(slice(None),) + ix], [(b, int(flat[a]), int(flat[z - 1]) + 1) for a, z in zip(cut, cut[1:])], len(flat))
 
-    def vp(lo, hi, st=1):
-        return (T.ps_p[:, 0, lo:hi] if st == 1 else T.ps_p[:, 0, lo:hi:st], [("ps_p", lo, hi)], len(range(lo, hi, st)))
-
-    def at(b, o):
-        return (T[b][:].indirect(o[0]), [(b, 0, size(b))] + o[1], 16 * o[2], True)
+    def at(win, o):
+        return (win[0].indirect(o[0]), win[1] + o[1], 16 * o[2], True)
 
     def isv(x):
         return isinstance(x, tuple)
@@ -236,45 +240,48 @@ def rank_program(g, core, T, topo):
     def wide(*xs):
         return any(SCRATCH[x[1][0][0]][2] in (F32, I32) for x in xs)
 
+    def vec(f, o, ins, k):
+        if len(o) > 3:
+            run("V", f, regs(*ins) + o[1][1:], o[1][:1], 0.05 + SCA * o[2] * CY)
+        elif len(ins[0]) > 3:
+            run("V", f, regs(*ins), regs(o), 0.05 + GAT * o[2] * CY)
+        else:
+            run("V", f, regs(*ins), regs(o), FX + max(64, o[2] * k) * CY)
+
     def ts(o, a, s1, op0, s2=None, op1=None):
         if op1 is None:
             f = lambda e: e.tensor_scalar(out=o[0], in0=a[0], scalar1=ap(s1), scalar2=None, op0=op0)
         else:
             f = lambda e: e.tensor_scalar(out=o[0], in0=a[0], scalar1=ap(s1), scalar2=ap(s2), op0=op0, op1=op1)
-        run("V", f, regs(a, s1, s2), regs(o), 0.05 + max(64, o[2] * (1.0 if wide(o, a) else 0.5)) * CY)
+        vec(f, o, [a, s1, s2], 1.0 if wide(o, a) else 0.5)
 
     def tt(o, a, b, op):
-        k = 1.5 if len(a) > 3 else 1.0 if any(is_psum(x[1][0][0]) for x in (a, b)) else 2.0
-        run("V", lambda e: e.tensor_tensor(out=o[0], in0=a[0], in1=b[0], op=op), regs(a, b), regs(o), 0.05 + max(64, o[2] * k) * CY)
+        vec(lambda e: e.tensor_tensor(out=o[0], in0=a[0], in1=b[0], op=op), o, [a, b], 1.0 if any(is_psum(x[1][0][0]) for x in (a, b)) else 2.0)
 
     def tc(o, a):
-        f = lambda e: e.tensor_copy(out=o[0], in_=a[0])
-        if len(o) > 3:
-            run("V", f, regs(a) + o[1][1:], o[1][:1], 0.05 + 3.8 * o[2] * CY)
-        else:
-            k = 1.5 if len(a) > 3 else 1.0 if wide(o, a) else 0.5
-            run("V", f, regs(a), regs(o), 0.05 + max(64, o[2] * k) * CY)
+        vec(lambda e: e.tensor_copy(out=o[0], in_=a[0]), o, [a], 1.0 if wide(o, a) else 0.5)
 
     def fill(o, c):
-        run("V", lambda e: e.memset(o[0], c), [], regs(o), 0.05 + o[2] * CY * (1.0 if wide(o) else 0.5))
+        run("V", lambda e: e.memset(o[0], c), [], regs(o), FX + o[2] * CY * (1.0 if wide(o) else 0.5))
 
-    def vtr(o, a):
-        run("V", lambda e: e.transpose(out=o[0], in_=a[0]), regs(a), regs(o), 0.05 + o[2] * CY)
+    def scan(o, m, a, op=OP.mult):
+        vec(lambda e: e.tensor_tensor_scan(out=o[0], data0=m[0], data1=a[0], initial=0.0, op0=op, op1=OP.max), o, [m, a], 1.0 if wide(o, m, a) else 0.5)
 
-    def scan(o, m, a):
-        run("V", lambda e: e.tensor_tensor_scan(out=o[0], data0=m[0], data1=a[0], initial=0.0, op0=OP.mult, op1=OP.max), regs(m, a), regs(o), FX + o[2] * CY)
-
-    def act(o, a, func, scale=1.0, bias=0.0, accum=None):
+    def act(o, a, func=AF.Identity, scale=1.0, bias=0.0, accum=None):
         b0, s0 = ap(bias), ap(scale)
         if accum is None:
             f = lambda e: e.activation(out=o[0], in_=a[0], func=func, bias=b0, scale=s0)
         else:
             f = lambda e: e.activation(out=o[0], in_=a[0], func=func, bias=b0, scale=s0, accum_out=accum[0])
-        run("S", f, regs(a, bias, scale), regs(o, accum), 0.065 + max(64, o[2] * (1.5 if len(a) > 3 else 1.0)) * CY)
+        run("S", f, regs(a, bias, scale), regs(o, accum), 0.065 + o[2] * GAT * CY if len(a) > 3 else FX + max(64, o[2]) * CY)
 
     def mm(o, lT, r, start, stop):
         k = 4.0 if SCRATCH[lT[1][0][0]][2] == F32 else 1.0
         run("T", lambda e: e.matmul(out=o[0], lhsT=lT[0], rhs=r[0], start=start, stop=stop), regs(lT, r), regs(o), 0.00071 * k * max(64, o[2]))
+
+    def total(o, terms):
+        for k, (c, x) in enumerate(terms):
+            mm(o, w("WM", WEIGHTS.index(c)), x, k == 0, k == len(terms) - 1)
 
     def iota(o, pattern, base, cm):
         if SCRATCH[o[1][0][0]][2] != I32:
@@ -283,351 +290,322 @@ def rank_program(g, core, T, topo):
             f = lambda e: e.iota(o[0], pattern, base, cm)
         run("G", f, [], regs(o), 0.13 + 2 * o[2] * CY)
 
-    def asel(o, a, pattern, cmp, base, cm):
-        run("G", lambda e: e.affine_select(out=o[0], in_=a[0], pattern=pattern, compare_op=cmp, fill=0.0, base=base, channel_multiplier=cm), regs(a), regs(o), 0.17 + 2 * o[2] * CY)
+    def asel(o, a, pattern, cmp, base, cm, other=0.0):
+        run("G", lambda e: e.affine_select(out=o[0], in_=a[0], pattern=pattern, compare_op=cmp, fill=other, base=base, channel_multiplier=cm), regs(a), regs(o), 0.17 + 2 * o[2] * CY)
 
-    def send(src, dst, to, frm, kind):
+    def send(src, kind, t, to, frm):
         rid, pid = topo.addr(to)[:2]
         m = topo.mask(core, to)
-        rs, ls = "r" + kind, "l" + kind
+        dst, rs, ls = ["%s%s%d" % (x, kind, t) for x in "Lrl"]
 
         def f(e):
             e.remote_dma(out_ap=T[dst][:], in_ap=T[src][:], remote_sem=T.sem[rs], local_sem=T.sem[ls], pid=pid, routing_id=rid, dma_engine_mask=m)
         i = run("G", f, [(src, 0, size(src))], [], 0.1, sem=ls, inc=len(topo.engines(core, to)))
-        landed(dst, rs, len(topo.engines(frm, core)), i, HOP)
+        landed(dst, rs, len(topo.engines(frm, core)), i, HOP + 512 * size(src) / RATE)
 
-    run("Y", lambda e: e.dma_start(T.ENT[:], T.ent[:]), [], regs(v("ENT")), 0.1, "dEnt", 16, 5.0)
+    run("Y", lambda e: e.dma_start(T.ENT[:, 0:1024], T.ent[:, 0:1024]), [], regs(v("ENT", 0, 1024)), 0.1, "dE0", 16, 3.5)
+    run("Y", lambda e: e.dma_start(T.FT[:, 16:16 + NM], T.feat[:]), [], regs(v("FT", 16)), 0.1, "dF", 16, 6.5)
+    run("Y", lambda e: e.dma_start(T.ENT[:, 1024:S], T.ent[:, 1024:S]), [], regs(v("ENT", 1024, S)), 0.1, "dE1", 16, 8.0)
     run("S", lambda e: e.dma_start(T.wtS[:], T.wt[:]), [], regs(v("wtS")), 0.1, "dW", 16, 2.0)
     run("S", lambda e: e.dma_start(T.kapS[:], T.kap[:]), [], regs(v("kapS")), 0.1, "dK", 16, 2.0)
 
-    def load(q, buf, par, sem):
-        def f(e):
-            for a in range(4):
-                for h in range(2):
-                    e.dma_start(T[buf][32 * a + 16 * h:32 * a + 16 * h + 16, 0:NM], T.feat[32 * a + 16 * par:32 * a + 16 * par + 16, :]).then_inc(T.sem[sem], 16)
-        run(q, f, [], [(buf, 0, NM)], 0.8, sem, 128, 8.0)
-    load("Y", "FA", 0, "dFA")
-    load("S", "FB", 1, "dFB")
-
     fill(v("ones"), 1.0)
-    fill(v("FA", NM, NM + 16), 0.0)
-    fill(v("FB", NM, NM + 16), 0.0)
-    fill(v("Np", S, SW_), 0.0)
-    fill(v("Wp", S, SW_), 0.0)
-    fill(v("Ip", S, SW_), 0.0)
-    fill(v("ZE"), 0.0)
+    fill(v("ONEB"), 1.0)
+    fill(v("FT", 0, 16), 0.0)
+    fill(v("SC"), 0.0)
+    fill(v("WX"), 0.0)
+    fill(v("MB"), 1.0)
+    fill(v("MB", 0, 512, 16), 0.0)
     fill(v("MK"), 1.0)
     fill(v("MK", 0, 128, 16), 0.0)
-    fill(v("SC"), 0.0)
-    fill(v("IX"), 0.0)
+    fill(v("Xp", S, SW_), 0.0)
+    fill(v("Ip", S, SW_), 0.0)
+    fill(v("OWN"), 0.0)
+    fill(v("Ab"), 0.0)
     for t in range(RO):
-        fill(v("nab%d" % t, L, L + 8), 0.0)
-
-    def slot(k, n=1):
-        return v("CT", 128 * k, 128 * (k + n))
+        fill(v("TG", H * t, H * t + H), t + 1.0)
     iota(v("pidx"), [[0, 1]], 0, 1)
+    asel(v("B0"), v("ones"), [[-16, 8], [0, 16]], OP.is_ge, 0, 1)
+    asel(v("B1"), v("B0"), [[16, 8], [0, 16]], OP.is_ge, 15, -1)
+    asel(v("ID"), v("ones"), [[-1, 128]], OP.is_equal, 0, 1)
+    iota(v("xp"), [[0, 16], [1, 16]], 0, 0)
+    iota(v("jj"), [[16, 8]], 0, 0)
     iota(v("c64"), [[37, 64]], 0, 0)
-    iota(v("io1"), [[1, 16]], 0, 0)
-    iota(v("io16"), [[16, 16]], S, 0)
-    asel(slot(10), v("ones"), [[-16, 8], [0, 16]], OP.is_ge, 0, 1)
-    asel(slot(11), slot(10), [[16, 8], [0, 16]], OP.is_ge, 15, -1)
-    asel(slot(12), v("ones"), [[-1, 128]], OP.is_equal, 0, 1)
-    for p in range(2):
-        asel(slot(p), v("ones"), [[-32, 4], [0, 2], [-1, 16]], OP.is_equal, -16 * p, 1)
-    for p in range(2):
-        for h in range(2):
-            k = 2 + 2 * (2 * p + h)
-            asel(slot(k), v("ones"), [[-32, 4], [-1000 if p == 0 else 1000, 2], [0, 16]], OP.is_ge, -16 * h - (1000 if p else 0), 1)
-            asel(slot(k + 1), slot(k), [[32, 4], [0, 2], [0, 16]], OP.is_ge, 15 + 16 * h, -1)
-    for h in range(2):
-        for p in range(2):
-            asel(slot(13 + 2 * h + p), v("ones"), [[-32, 4], [984, 2], [-1, 16]], OP.is_equal, 16 * (p - h) - 1000 * p, 1)
-    iota(v("PI"), [[1, S]], 0, 0)
+    iota(v("colv"), [[1, L]], S, 0)
+    for k in range(2):
+        iota(v("KC", 64 * k, 64 * k + 64), [[0, 8], [-2048, 8]], 2048 * (15 - 8 * k), 0)
+    iota(v("KC", 128, 192), [[1, 8], [0, 8]], 0, 0)
+    for k in range(4):
+        iota(v("PI", 512 * k, 512 * k + 512), [[1, 512]], 512 * k, 0)
     tc(v("wtF"), v("wtS"))
     tc(v("kapF"), v("kapS"))
-    for p in range(2):
-        mm(vp(p, p + 1), slot(p), v("wtF"), True, True)
-    tc(v("wcol"), vp(0, 2))
-    for p in range(2):
-        for h in range(2):
-            k = 2 * p + h
-            ts(v("WL", 128 * k, 128 * k + 128), slot(2 + 2 * k + 1), v("wcol", p, p + 1), OP.mult)
     ts(v("pm"), v("pidx"), 15, OP.bitwise_and)
     tc(v("pmF"), v("pm"))
     ts(v("p0"), v("pmF"), 0.0, OP.is_equal)
-    ts(v("kcol"), v("pmF"), -2048.0, OP.mult, 15.0 * 2048, OP.add)
-    ts(v("LL"), v("io16"), v("pmF"), OP.add)
-    ts(v("ucol"), v("io1"), v("pmF"), OP.is_gt)
-    for x in range(1, 16):
-        act(v("UT", 128 * x, 128 * x + 128), slot(11), AF.Copy, scale=v("ucol", x, x + 1))
     ts(v("SEL0"), v("ones"), v("p0"), OP.mult)
-    tc(v("BD"), slot(11))
     for q in range(8):
-        act(v("SC", 16 * q, 16 * q + 129 * 15 + 1, 129), v("CT", 128 * 11 + 16 * q, 128 * 11 + 16 * q + 16), AF.Copy, scale=32768.0)
-        tc(v("IX", 16 * q, 16 * q + 129 * 15 + 1, 129), v("CT", 128 * 12 + 16 * q, 128 * 12 + 16 * q + 16))
-    tc(v("SWP"), slot(13, 4))
-    tc(v("IDH"), slot(12))
+        act(v("WX", 16 * q, 16 * q + 129 * 15 + 1, 129), v("B1", 16 * q, 16 * q + 16), AF.Copy, scale=v("wtF"))
+        act(v("SC", 16 * q, 16 * q + 129 * 15 + 1, 129), v("B1", 16 * q, 16 * q + 16), AF.Copy, scale=32768.0)
+    for k, c in enumerate(WEIGHTS):
+        act(w("WM", k), v("ID"), AF.Copy, scale=c)
+    act(v("BDk"), v("B1"), AF.Copy, scale=4096.0)
+    tc(v("IDH"), v("ID"))
+    ts(v("DGm"), v("xp"), v("pmF"), OP.is_equal)
+    tt(v("DG"), v("DGm"), v("colv"), OP.mult)
+    ts(v("TRI"), v("xp", 0, H), v("pmF"), OP.is_gt)
+    ts(v("KD"), v("DGm", 0, 16), v("kapF"), OP.mult)
+    mm(v("pZ", 0, 16), v("BDk"), v("KD"), True, True)
+    act(v("ab0", H, H + 16), v("pZ", 0, 16), AF.Copy, scale=2.0 ** -12)
+    ts(v("j1"), v("jj"), v("pmF"), OP.add)
+    ts(v("j2"), v("j1"), 2, OP.arith_shift_right, 7, OP.bitwise_and)
+    tc(v("RU"), v("j2"))
+    ts(v("j2"), v("j1"), 3, OP.arith_shift_right, -4, OP.bitwise_and)
+    ts(v("j3"), v("j1"), 3, OP.bitwise_and)
+    tt(v("j1"), v("j2"), v("j3"), OP.add)
+    tc(v("RK"), v("j1"))
+    iota(v("j4"), [[16, 8], [0, 4]], 0, 0)
+    ts(v("RC"), v("j4"), v("pmF"), OP.add)
     ts(v("c64b"), v("c64"), 63, OP.bitwise_and)
-    ts(v("CC", 0, 64), v("c64b"), 4096.0, OP.mult, -262144.0 - 2033.0, OP.add)
+    ts(v("CC", 0, 64), v("c64b"), 4096.0, OP.mult, -2049.0, OP.add)
     n = 64
     while n < S:
         act(v("CC", n, 2 * n), v("CC", 0, n), AF.Copy)
         n *= 2
 
-    def entries(o, x, tmp):
-        ts(tmp, x, 2047, OP.add)
-        ts(tmp, tmp, -2048, OP.bitwise_and)
-        tt(o, x, tmp, OP.add)
-    entries(v("ab0"), v("ENT", 0, S, 8), v("o1"))
-    for k in range(NV):
-        entries(v("Np", 512 * k, 512 * k + 512), v("ENT", 512 * k, 512 * k + 512), v("ENT2", 512 * k, 512 * k + 512))
+    BIG, MID, OUT = 12582912.0, 8388608.0, -33554432.0
 
-    BIG, MID = 12582912.0, 8387584.0
+    flat = v
 
-    for k in range(NV, 4):
+    def entries(o, x, tmp, bank):
+        ts(tmp, x, -1024.5, OP.add, 2048.0 * BIG, OP.add)
+        act(bank, tmp, bias=2048.0 - MID - 2048.0 * BIG)
+        tt(o, x, bank, OP.add)
+    for h in range(2):
+        ahead[0] = AH1 if h == 0 else 0.0
+        entries(v("ab%d" % h, 0, H), v("ENT", 1024 * h, 1024 * h + 1024, 8), v("n1", H * h, H * h + H), v("pA", H * h, H * h + H))
+    ahead[0] = 0.0
+    for k in range(4):
         lo, hi = 512 * k, 512 * k + 512
-        num, quo, bank = v("OR", S + lo, S + hi), v("OR", lo, hi), v("ps_u" if k == 2 else "ps_d")
-        tc(num, v("ENT", lo, hi))
-        act(quo, num, AF.Identity, scale=2.0 ** -11, bias=2047 / 4096)
-        act(quo, quo, AF.Identity, bias=BIG)
-        act(bank, quo, AF.Identity, scale=2048.0, bias=-2048.0 * BIG)
-        tt(v("Np", lo, hi), num, bank, OP.add)
+        entries(v("Xp", lo, hi), v("ENT", lo, hi), v("W1", lo, hi), (v("pW"), v("pD"), flat("pS0", 0, 512), flat("pS1", 0, 512))[k])
 
-    def mid(o, x):
-        act(o, x, AF.Identity, bias=-MID)
+    def number(o, x, tmp, bank):
+        act(tmp, x, scale=2.0 ** -12, bias=BIG)
+        act(bank, tmp, scale=2048.0, bias=-2048.0 * BIG - MID / 2)
+        tt(o, x, bank, OP.subtract)
 
-    def w_of(o, x, tmp):
-        act(tmp, x, AF.Identity, scale=1 / 16, bias=-2056.5 / 16)
-        act(tmp, tmp, AF.Identity, bias=BIG)
-        act(o, tmp, AF.Identity, bias=MID / 16 - BIG)
+    def settle(t, plane, h):
+        cur, bank = v(plane, t + 1024 * h, 1024 * h + 1024, 8), v("pD", L + H * h, L + H * h + H)
+        act(bank, cur, scale=-2.0, bias=OUT)
+        tt(bank, v("Ln%d%d" % (h, t)), bank, OP.min)
+        tt(cur, cur, bank, OP.max)
 
-    def n32_of(o, x, tmp):
-        act(tmp, x, AF.Identity, scale=1 / 32, bias=-2048.5 / 32)
-        act(tmp, tmp, AF.Identity, bias=BIG)
-        act(tmp, tmp, AF.Identity, bias=-BIG)
-        act(o, tmp, AF.Identity, scale=32.0, bias=MID + 2033)
-
-    back = None
     for t in range(RO):
         clock = C0 + t
         thr = clock - 5
+        last = t == RO - 1
+        plane = "Ip" if last else "Xp"
         d = 1 + t % 3
         to, frm = cores[(rank + d) % 4], cores[(rank - d) % 4]
-        ab, aL, eb, eL, nab, naL = ["%s%d" % (x, t) for x in ("ab", "aL", "eb", "eL", "nab", "naL")]
-        prev = "naL%d" % (t - 1)
 
-        lanes = v("Np", t, S, 8) if t else v("ab0")
-        ts(v("s1"), lanes, -2033, OP.add)
-        act(v("nf"), lanes, AF.Identity, scale=2.0 ** -12, bias=BIG)
-        act(v("nf"), v("nf"), AF.Identity, bias=-BIG - 1 - 2048)
-        if t:
-            act(v(ab), lanes, AF.Copy)
-        send(ab, aL, to, frm, "a%d" % t)
-        ts(v("lo1"), v("s1"), 31, OP.bitwise_and)
-        dm = v3("pC", 0, 0, L)
-        ts(dm, v("lo1"), 16, OP.is_lt, 8192.0, OP.mult)
-        tt(v("idx"), v("nf"), dm, OP.add)
-        vtr(v("TT"), v("idx"))
-        for b in range(8):
-            mm(v("ps_s%d" % (b // 4), b % 4, 128, 4), v("IDH"), v("TT", 32 * b, 32 * b + 32), True, True)
-        for s in range(2):
-            ts(v("LS", 128 * s, 128 * s + 128), v("ps_s%d" % s, 0, 128), 2048.0, OP.add, 4096.0, OP.min)
-        if t:
-            back(t - 1)
-        for s in range(2):
-            lo, hi = 128 * s, 128 * s + 128
-            ahead[0] = AH1 if s == 0 else 0.0
-            for k in range(8):
-                for p in range(2):
-                    o = 256 * s + 128 * p
-                    acc = v("AC", o, o + 128)
-                    win = at("FB" if p else "FA", v("LS", lo + 64 * p + 8 * k, lo + 64 * p + 8 * k + 8))
-                    if k == 0:
-                        act(acc, win, AF.Copy)
-                    else:
-                        tt(acc, win, acc, OP.max)
-            for p in range(2):
-                o = 256 * s + 128 * p
-                tt(v("Y", lo + 64 * p, lo + 64 * p + 64), v("AC", o, o + 64), v("AC", o + 64, o + 128), OP.max)
-            for h in range(2):
-                for p in range(2):
-                    k = 2 * p + h
-                    mm(v("ps_u", lo + 64 * h, lo + 64 * h + 64), v("WL", 128 * k, 128 * k + 128), v("Y", lo + 64 * p, lo + 64 * p + 64), p == 0, p == 1)
-            tc(v("ui", lo, hi), v("ps_u", lo, hi))
-            ts(v("um", lo, hi), v("ui", lo, hi), 4095, OP.bitwise_and)
-            tt(v("sq", lo, hi), v("um", lo, hi), v("um", lo, hi), OP.mult)
-            ku = v3("pC", 0, lo, hi)
+        def f(b, h, n=H, o=0, st=1):
+            return v(b, n * h + o, n * h + n, st)
+
+        for h in range(2):
+            ahead[0] = AH1 if h == 0 else 0.0
+            ab = v("ab%d" % h, 0, H)
+            lanes = v("Xp", t + 1024 * h, 1024 * h + 1024, 8) if t else ab
+            ts(f("s1", h), lanes if t else v("ENT", 1024 * h, 1024 * h + 1024, 8), -1.0, OP.add)
+            act(f("n1", h), lanes, scale=2.0 ** -12, bias=BIG)
+            act(f("pU", h), f("n1", h), scale=2.0 ** -9, bias=(2063 - BIG) / 512)
             if t:
-                ts(ku, v("um", lo, hi), v("kapF", 0, 1), OP.mult, v(prev, L, L + 1), OP.add)
-            else:
-                ts(ku, v("um", lo, hi), v("kapF", 0, 1), OP.mult)
-            ts(v("sq5", lo, hi), v("sq", lo, hi), 5, OP.arith_shift_right)
-            tt(v("es", lo, hi), v("sq5", lo, hi), ku, OP.add)
-            ts(v("e2", lo, hi), v("es", lo, hi), 2047, OP.bitwise_and)
-            for h in range(2):
-                tc(v3("%s%d" % (eb, s), None, 16 * h, 16 * h + 16), v("e2", lo + 64 * h, lo + 64 * h + 64))
-            send("%s%d" % (eb, s), "%s%d" % (eL, s), to, frm, "e%d%d" % (t, s))
-            ahead[0] = 0.0
-
-        if t == 0:
-            for k in range(WV):
-                lo, hi = 512 * k, 512 * k + 512
-                ts(v("ENT", lo, hi), v("Np", lo, hi), -2049, OP.add)
-                ts(v("ENT2", lo, hi), v("ENT", lo, hi), 4, OP.arith_shift_right)
-                ts(v("Wp", lo, hi), v("ENT2", lo, hi), -128.0, OP.max)
-            for k in range(WV, 4):
-                lo, hi = 512 * k, 512 * k + 512
-                mid(v("OR", lo, hi), v("Np", lo, hi))
-                w_of(v("Wp", lo, hi), v("OR", lo, hi), v("OR", lo, hi))
-        else:
-            act(v("Np", t - 1, S, 8), v(prev, 0, L), AF.Copy)
-            mid(v("wn"), v(prev, 0, L))
-            w_of(v("Wp", t - 1, S, 8), v("wn"), v("wn"))
-            tc(at("Np", v("PL")), v("nb"))
-            tc(at("Wp", v("PL")), v("wnb"))
-        mid(v("fa"), v(aL))
-        w_of(v("wf"), v("fa"), v("fw"))
-        for m in range(16):
-            act(v("OR", m, 4096, 16), v("wf"), AF.Copy)
-
-        def side(x, k, s):
-            lo, hi = 128 * s, 128 * s + 128
-            far = v3("pB" if s else "pA", 1 - k, 0, 128)
-            tt(v3("pC", k, lo, hi), v3("z", k, lo, hi), far, OP.is_le)
-            tt(v3("X1", k, lo, hi), x, v3("pC", k, lo, hi), OP.mult)
-            tt(far, x, far, OP.mult)
-            act(v3("e0", k, lo, hi), v3("X1", k, lo, hi), AF.Relu, scale=-2.0 ** -18, bias=2.0 ** -18)
-
-        act(v("ps_s0", L, 2 * L), v("CC", t, S, 8), AF.Copy)
-        tt(v3("si", 0, 0, L), v(aL), v("ps_s0", L, 2 * L), OP.add)
-        ts(v3("z", 0, 0, L), v3("si", 0, 0, L), 7 << 15, OP.bitwise_and)
-        n32_of(v("ps_d", L, 2 * L), v("fa"), v("fl"))
-        tt(v("lo"), v(aL), v("ps_d", L, 2 * L), OP.subtract)
-        act(v("sg"), v("lo"), AF.Sign, bias=0.5 - thr)
-        act(v("sh"), v("lo"), AF.Sign, bias=-15.5)
-        act(v3("c", 0, 0, L), v("lo"), AF.Identity, scale=-1.0, bias=float(clock))
-        for s in range(2):
-            act(v3("pB" if s else "pA", 1, 0, 128), v("sg", 128 * s, 128 * s + 128), AF.Relu, scale=262144.0)
-            act(v3("pB" if s else "pA", 3, 0, 128), v("sh", 128 * s, 128 * s + 128), AF.Relu, scale=float(thr))
-            side(v(aL, 128 * s, 128 * s + 128), 0, s)
-        for s in range(2):
-            ts(v("kc", 128 * s, 128 * s + 128), v("%s%d" % (eL, s)), v("kcol", 0, 1), OP.add)
-        for k in range(NCH):
-            lo, hi, n = CW * k, CW * k + CW, CW // 16
-            q = k * n
-            ahead[0] = AH2 if k < NCH // 2 else 0.0
-            tt(v("D", lo, hi), at("Wp", v("%s%d" % (eL, q // 128), q % 128, q % 128 + n)), v("OR", lo, hi), OP.subtract)
-            act(v("A1", lo, hi), v("D", lo, hi), AF.Abs)
-            act(v("B1", lo, hi), v("A1", lo, hi), AF.Abs, bias=-64.0)
-            ts(v("IN", lo, hi), v("B1", lo, hi), 63.5, OP.is_lt)
-            for m in range(16):
-                mm(v("ps_s%d" % (q // 128), q % 128, q % 128 + n), v("SC", 128 * m, 128 * m + 128), v("IN", lo + m, hi, 16), m == 0, m == 15)
-        for s in range(2):
-            lo, hi = 128 * s, 128 * s + 128
-            ahead[0] = AH3 if s == 0 else 0.0
-
-            def f(b, n, o=0, st=1):
-                return v(b, n * s + o, n * s + n, st)
-            tt(f("key", 128), v("ps_s%d" % s, 0, 128), f("kc", 128), OP.add)
-            vtr(f("TK", 128), f("key", 128))
-            scan(f("k4", 128), v("MK"), f("TK", 128))
-            ts(f("k5", 8), f("k4", 128, 15, 16), 2047, OP.bitwise_and)
-            tc(f("pf", 8), f("k5", 8))
-            for h in range(2):
-                for p in range(2):
-                    k = 2 * h + p
-                    mm(vp(8 * s + h, 8 * s + 8, 2), v("SWP", 128 * k, 128 * k + 128), f("pf", 8, p, 2), p == 0, p == 1)
-            tc(f("pl", 8), vp(8 * s, 8 * s + 8))
-            act(f("P1", 8), vp(8 * s, 8 * s + 8), AF.Copy)
-            act(f("P1n", 8), f("P1", 8), AF.Copy, scale=-1.0)
-            act(f("CP", 128), at("CC", f("pl", 8)), AF.Copy)
-            act(f("bx", 128), at("Np", f("pl", 8)), AF.Copy)
-            tc(f("PB", 128), at("PI", f("pl", 8)))
-            P, low = "pB" if s else "pA", f("lob", 128)
-            tt(v3("si", 1, lo, hi), at("Np", f("pl", 8)), f("CP", 128), OP.add)
-            ts(low, v3("si", 1, lo, hi), 31, OP.bitwise_and)
-            ts(v3("z", 1, lo, hi), v3("si", 1, lo, hi), 7 << 15, OP.bitwise_and)
-            ts(v3(P, 0, 0, 128), low, thr, OP.is_ge, 262144.0, OP.mult)
-            ts(v3(P, 2, 0, 128), low, 16, OP.is_ge, float(thr), OP.mult)
-            ts(v3("c", 1, lo, hi), low, -1.0, OP.mult, float(clock), OP.add)
-            side(f("bx", 128), 1, s)
-            a = v3("X1", 0, lo, hi)
-            tt(f("dd", 128), a, f("bx", 128), OP.subtract)
-            act(f("dq", 128), f("dd", 128), AF.Square, scale=2.0 ** -11)
-            ts(f("sm", 128), f("dq", 128), 1.0, OP.is_lt)
-            tt(f("sm", 128), f("sm", 128), v3("pC", 1, lo, hi), OP.mult)
-            both, big = v3(P, (2, 4), 0, 128), v3(P, 3, 0, 128)
-            tt(v3(P, 2, 0, 128), f("lo", 128), v3(P, 2, 0, 128), OP.is_lt)
-            tt(big, low, big, OP.is_lt)
-            tt(both, v3("c", None, lo, hi), both, OP.mult)
-            tt(f("XH", 128), a, v3(P, 2, 0, 128), OP.add)
-            tt(big, f("bx", 128), big, OP.add)
-            tt(big, f("XH", 128), big, OP.max)
-            tt(big, f("sm", 128), big, OP.mult)
-            fil = v3(P, (0, 2), 0, 128)
-            tt(fil, v3("e0", None, lo, hi), fil, OP.mult)
-            tt(v3("M", None, lo, hi), v3("X1", None, lo, hi), fil, OP.max)
-            tt(f("nb", 128), v3("M", 1, lo, hi), big, OP.max)
+                act(ab, lanes, AF.Copy)
+            send("ab%d" % h, "a%d" % h, t, to, frm)
+            ts(f("kd", h), f("s1", h), 16, OP.bitwise_and)
+            tt(f("wi", h), f("pU", h), f("kd", h), OP.subtract)
+            ts(f("idx", h), f("wi", h), 512.0, OP.mult, 0.0, OP.max)
+        for h in range(2):
+            ahead[0] = AH1 if h == 0 else 0.0
+            for q in range(4 * h, 4 * h + 4):
+                o, win = v("GF", 512 * q, 512 * q + 512), at(v("FT"), v("idx", 32 * q, 32 * q + 32))
+                if q in VG:
+                    tc(o, win)
+                else:
+                    act(o, win, AF.Copy)
+                scan(v("YS", 512 * q, 512 * q + 512), v("MB"), o)
+            u = v("pU", L + 8 * h, L + 8 * h + 8)
+            for x in range(16):
+                mm(u, v("WX", 128 * x, 128 * x + 128), v("YS", 2048 * h + 16 * x + 15, 2048 * h + 2048, 256), x == 0, x == 15)
+            tc(f("ui", h, 8), u)
+            ts(f("um", h, 8), f("ui", h, 8), 4095, OP.bitwise_and)
+            tt(f("sq", h, 8), f("um", h, 8), f("um", h, 8), OP.mult)
+            tc(v("us%d" % h, 0, 8), f("um", h, 8))
+            ts(f("s5", h, 8), f("sq", h, 8), 5, OP.arith_shift_right)
+            tc(v("us%d" % h, 8, 16), f("s5", h, 8))
+            send("us%d" % h, "u%d" % h, t, to, frm)
         ahead[0] = 0.0
-        act(v("PBf", 128, L), at("PI", v("pl", 8, 16)), AF.Copy)
-        for c in range(16):
-            n = 256 - 16 * c
-            if c < EQV:
-                ts(v3("EQ", c, 0, n), v("PB", 16 * c, 256), v("P1", c, c + 1), OP.is_equal)
+        if t:
+            for h in range(2):
+                settle(t - 1, "Xp", h)
+        if last:
+            for k in range(4):
+                lo, hi = 512 * k, 512 * k + 512
+                number(v("Ip", lo, hi), v("Xp", lo, hi), v("W1", lo, hi), flat("pS1", 0, 512) if k % 2 else v("pD"))
+
+        def flags(h, s, x, z, far, x1):
+            lam = w("LAM", h, s)
+            act(far, lam, AF.Relu, scale=262144.0, bias=262144.0 * (16 - thr))
+            tt(far, z, far, OP.is_le)
+            tt(x1, x, far, OP.mult)
+            act(w("SIG", h, s), lam, AF.Sign, bias=15.5 - thr)
+            act(w("IOT", h, 1 - s), lam, AF.Sign, bias=-0.5)
+            act(w("EM0", h, s), x, AF.Relu, scale=-1.0, bias=1.0)
+            act(w("EM", h, s), x1, AF.Relu, scale=-1.0, bias=1.0)
+
+        act(v("KK"), at(v("La0%d" % t, H, H + 16), v("RK")), AF.Copy)
+        for h in range(2):
+            ahead[0] = AH2 if h == 0 else 0.0
+            a = v("La%d%d" % (h, t), 0, H)
+            act(f("c1", h), a, scale=1 / 16, bias=7.5 / 16)
+            act(f("c1", h), f("c1", h), bias=BIG)
+            act(f("c1", h), f("c1", h), bias=-BIG)
+            if len(SG[h]) < 4:
+                act(f("OR", h, 512), at(f("c1", h), v("RC")), scale=16.0, bias=-7.5)
+            ahead[0] = 0.0
+            act(f("aN", h), a, bias=MID)
+            p0, p1, keep, a1 = v("pW", L * h, L * h + H), v("pW", L * h + H, L * h + L), v("pA", L * h, L * h + H), v("pA", L * h + H, L * h + L)
+            act(p0, v("CC", t + 1024 * h, 1024 * h + 1024, 8), AF.Copy)
+            act(f("l1", h), a, scale=1 / 32, bias=-0.5 / 32)
+            act(f("l1", h), f("l1", h), bias=BIG)
+            act(p1, f("l1", h), scale=32.0, bias=-32.0 * BIG)
+            tt(f("sia", h), a, p0, OP.add)
+            tt(w("LAM", h, 0), a, p1, OP.subtract)
+            ts(f("za", h), f("sia", h), 7 << 15, OP.bitwise_and)
+            flags(h, 0, f("aN", h), f("za", h), keep, a1)
+            if last:
+                number(f("anum", h), a, f("an1", h), p0)
+                tt(f("a1c", h), f("anum", h), keep, OP.mult)
             else:
-                act(v3("EA", c - EQV, 0, n), v("PBf", 16 * c, 256), AF.Abs, bias=v("P1n", c, c + 1))
-                act(v3("EQ", c, 0, n), v3("EA", c - EQV, 0, n), AF.Relu, scale=-1.0, bias=1.0)
-        mm(v("ps_d", 0, 256), v("BD"), v("ZE"), True, False)
-        for c in range(15):
-            mm(v("ps_d", 16 * c + 16, 256), v("BD"), v3("EQ", c, 16, 256 - 16 * c), False, False)
-        for x in range(1, 16):
-            col = (T.EQ[:, 0:16, x], [("EQ", 256 * c + x, 256 * c + x + 1) for c in range(16)], 16)
-            mm(v("ps_d", x, 256, 16), v("UT", 128 * x, 128 * x + 128), col, False, x == 15)
-        act(v("lose"), v("ps_d", 0, 256), AF.Sign, accum=v("lc"))
-        for x in range(16):
-            mm(v("ps_d", 256, 272), v("IX", 128 * x, 128 * x + 128), v("lose", x, 256, 16), x == 0, x == 15)
-        tt(v("t16"), v("LL"), v("ps_d", 256, 272), OP.mult)
-        tt(v("u16"), v("t16"), v("P1"), OP.max)
-        tc(v("PL"), v("u16"))
-        if t < RO - 1:
-            mm(v3("ps_p", 2, 0, 1), v("SEL0"), v("lc"), True, True)
+                act(f("a1c", h), a1, bias=-MID)
 
-        def back(t, aL=aL, nab=nab, to=to, frm=frm, naL=naL):
-            na, df = v3("pC", 0, 0, L), v3("pC", 1, 0, L)
-            for s in range(2):
-                tt(v3("pC", 0, 128 * s, 128 * s + 128), v3("M", 0, 128 * s, 128 * s + 128), v3("pB" if s else "pA", 3, 0, 128), OP.max)
-            tt(df, v(aL), na, OP.subtract)
-            tt(v("na"), v("lose"), df, OP.mult)
-            tt(v(nab, 0, L), v("na"), na, OP.add)
-            if t < RO - 1:
-                act(v("an"), v3("ps_p", 2, 0, 1), AF.Copy, scale=-1.0)
-                act(v("aq"), v("an"), AF.Identity, scale=1 / 32, bias=-15.5 / 32)
-                act(v("aq"), v("aq"), AF.Identity, bias=BIG)
-                act(v("aq"), v("aq"), AF.Identity, bias=-BIG)
-                act(v(nab, L, L + 1), v("aq"), AF.Identity, scale=-32.0, bias=v("an"))
-            send(nab, naL, frm, to, "n%d" % t)
-            if t < RO - 1:
-                mid(v("wn"), v("nb"))
-                w_of(v("wnb"), v("wn"), v("wn"))
+        for h in range(2):
+            bank = "pS%d" % h
+            ahead[0] = AH2 if h == 0 else 0.0
+            us = "Lu%d%d" % (h, t)
+            tt(f("E1", h), at(v(us, 0, 8), v("RU")), v("KK"), OP.mult)
+            if t:
+                act(f("sA", h), at(v(us, 8, 16), v("RU")), bias=v("LA%d" % (t - 1), 0, 1))
+                tt(f("E2", h), f("E1", h), f("sA", h), OP.add)
+            else:
+                tt(f("E2", h), at(v(us, 8, 16), v("RU")), f("E1", h), OP.add)
+            ts(f("E3", h), f("E2", h), 2047, OP.bitwise_and)
+            tc(f("EL", h), f("E3", h))
+            tc(f("E16", h), f("E3", h))
+            if SG[h]:
+                for m in range(4):
+                    act(w("pO", (0, 8), m), f("c1", h), scale=16.0, bias=-7.5)
+            blk = (8 * h, 8 * h + 8)
+            for k in range(2):
+                for q in (2 * k, 2 * k + 1):
+                    lo, ms = 2048 * h + 512 * q, (4 * q, 4 * q + 4)
+                    o, win = v("D", lo, lo + 512), at(v("Xp"), v("EL", H * h + 32 * q, H * h + 32 * q + 32))
+                    if q in SG[h]:
+                        act(v("GS", lo, lo + 512), win, AF.Copy)
+                        tt(o, v("GS", lo, lo + 512), w("pO"), OP.subtract)
+                    else:
+                        tt(o, win, f("OR", h, 512), OP.subtract)
+                    ts(w("Q1", blk, ms), o, 4096.0 * (BIG + 1), OP.add, 4096.0 * (BIG + 1), OP.is_equal)
+                    ts(w("Q2", blk, ms), o, 16.0 * BIG, OP.add, 16.0 * BIG, OP.not_equal)
+                ms = (8 * k, 8 * k + 8)
+                key = v(bank, 64 * k, 64 * k + 64)
+                mm(key, w("WM", 0), v("KC", 64 * k, 64 * k + 64), True, False)
+                mm(key, w("WM", WEIGHTS.index(2.0 ** 21)), v("KC", 128, 192), False, False)
+                for m in range(8):
+                    lo = H * h + 64 * k + 32 * (m // 4)
+                    mm(v(bank, 64 * k + m, 64 * k + 64, 8), v("IDH"), v("E16", lo + m % 4, lo + 32, 4), False, False)
+                for Q in ("Q1", "Q2"):
+                    for x in range(16):
+                        mm(key, v("SC", 128 * x, 128 * x + 128), w(Q, blk, ms, x), False, Q == "Q2" and x == 15)
+                if k == 0:
+                    act(f("k0", h, 64), key, AF.Copy)
+            ahead[0] = AH3 if h == 0 else 0.0
+            scan(f("k4", h, 64), f("k0", h, 64), v(bank, 64, H), OP.max)
+            ts(f("k5", h, 8), f("k4", h, 64, 7, 8), 2047, OP.bitwise_and)
+            pl = f("pl", h, 8)
+            tc(pl, f("k5", h, 8))
+            tc(f("P1", h, 8), f("k5", h, 8))
+            tc(f("PB", h), at(v("PI"), pl))
+            act(f("l1b", h), at(v("Xp"), pl), scale=1 / 32, bias=-0.5 / 32)
+            act(f("CP", h), at(v("CC"), pl), AF.Copy)
+            act(f("bN", h), at(v("Xp"), pl), bias=MID)
+            tt(f("sib", h), at(v("Xp"), pl), f("CP", h), OP.add)
+            if last:
+                act(f("bnum", h), at(v("Ip"), pl), AF.Copy)
+            if h:
+                act(f("ow", h), at(v("OWN"), pl), AF.Relu, bias=-float(t))
+            for c in range(8):
+                ts(w("EQ", 8 * h + c, (0, H - 16 * c)), f("PB", h, H, 16 * c), v("P1", 8 * h + c, 8 * h + c + 1), OP.is_equal)
+            tt(f("EQd", h), w("EQ", blk, (0, 16)), v("TRI"), OP.mult)
+            cnt = f("pD", h)
+            mm(cnt, v("IDH"), f("PB", h), True, False)
+            if h:
+                mm(cnt, v("BDk"), f("ow", h), False, False)
+            for c in range(7):
+                mm(f("pD", h, H, 16 * c + 16), v("BDk"), w("EQ", 8 * h + c, (16, H - 16 * c)), False, False)
+            mm(cnt, v("BDk"), f("EQd", h), False, True)
+            tt(f("wd", h), cnt, f("DG", h), OP.min)
+            act(f("lose", h), cnt, AF.Sign, bias=-2047.5, accum=v("lc", h, h + 1))
+            scan(f("sc", h), v("MK"), f("wd", h))
+            tc(f("PL", h, 8), f("sc", h, H, 15, 16))
+            if h == 0:
+                tc(at(v("OWN"), f("PL", h, 8)), f("TG", t))
+            r, keep = flat(bank, H, 2 * H), flat(bank, 2 * H, 3 * H)
+            act(f("l1b", h), f("l1b", h), bias=BIG)
+            act(r, f("l1b", h), scale=32.0, bias=MID - 32.0 * BIG)
+            tt(w("LAM", h, 1), f("bN", h), r, OP.subtract)
+            ts(f("zb", h), f("sib", h), 7 << 15, OP.bitwise_and)
+            flags(h, 1, f("bN", h), f("zb", h), keep, f("b1", h))
+            if last:
+                tt(f("b1c", h), f("bnum", h), keep, OP.mult)
+            else:
+                act(f("b1c", h), f("b1", h), bias=-MID)
+            tt(f("d0", h), f("b1", h), v("pA", L * h + H, L * h + L), OP.subtract)
+            ts(f("same", h), f("d0", h), 4096.0 * BIG, OP.add, 4096.0 * BIG, OP.is_equal)
+            om = f("pW", h, L)
+            total(om, [(-1.0, w("LAM", h)), (-16.0, w("SIG", h)), (8.0, w("IOT", h))] + [(-16.0, w("EM", h))] * last)
+            act(om, om, AF.Relu, bias=clock - 39.0)
+            oa, ob = v("pW", L * h, L * h + H), v("pW", L * h + H, L * h + L)
+            tt(f("ah", h), f("a1c", h), oa, OP.add)
+            tt(ob, f("b1c", h), ob, OP.add)
+            tt(f("big", h), f("ah", h), ob, OP.max)
+            zz, zk = v("pZ", L * h, L * h + H), v("pZ", L * h + H, L * h + L)
+            total(zz, [(-11.0 * 2 ** 24, v("ONEB")), (2.0 ** 26, w("EM", h, 0)), (-2.0 ** 25, w("EM0", h, 0)), (2.0 ** 24, w("SIG", h, 0)),
+                       (-2.0 ** 25, w("EM0", h, 1)), (2.0 ** 24, w("SIG", h, 1)), (2.0 ** 26, w("EM", h, 1)),
+                       (3.0 * 2 ** 25, f("same", h)), (-2.0 ** 27, f("lose", h))])
+            tt(f("TT", h), f("big", h), zz, OP.min)
+            total(zk, [((6.0 if last else 5.0) * 2 ** 23, v("ONEB")), (-2.0 ** 25, w("EM", h, 0)), (2.0 ** 24, w("EM0", h, 0)), (2.0 ** 24, w("EM0", h, 0)),
+                       (2.0 ** 24, f("lose", h))])
+            tt(zk, f("anum", h) if last else v("La%d%d" % (h, t), 0, H), zk, OP.min)
+            tt(v("nab%d" % h), f("TT", h), zk, OP.max)
+            send("nab%d" % h, "n%d" % h, t, frm, to)
+        ahead[0] = 0.0
+        mine = v(plane, t, S, 8)
+        asel(mine, mine, [[0, L]], OP.is_gt, 0, 0, OUT)
+        for h in range(2):
+            tt(at(v(plane), f("PL", h, 8)), f("b1c", h), f("TT", h), OP.max)
+        if not last:
+            col = v("pU", 300, 301)
+            for h in range(2):
+                mm(col, v("SEL0"), v("lc", h, h + 1), h == 0, h == 1)
+            act(v("an"), col, AF.Copy, scale=-0.5)
+            act(v("aq"), v("an"), scale=1 / 32, bias=-15.5 / 32)
+            act(v("aq"), v("aq"), bias=BIG)
+            act(v("aq"), v("aq"), bias=-BIG)
+            act(v("Ab", 0, 1), v("aq"), scale=-32.0, bias=v("an"))
+            dn = 1 + (t + 1) % 3
+            send("Ab", "A", t, cores[(rank - d + dn) % 4], cores[(rank - dn + d) % 4])
 
-        if t == RO - 1:
-            back(t)
-        else:
-            tc(at("Np", v("PL")), v("nb"))
-
-    for k in range(4):
-        lo, hi = 512 * k, 512 * k + 512
-        bank = v(("ps_u", "ps_s0", "ps_s1", "ps_u")[k])
-        act(v("OR", lo, hi), v("Np", lo, hi), AF.Identity, scale=2.0 ** -12, bias=BIG)
-        act(bank, v("OR", lo, hi), AF.Identity, scale=2048.0, bias=-2048.0 * BIG)
-        tt(v("Ip", lo, hi), v("Np", lo, hi), bank, OP.subtract)
-
-    def number(o, x):
-        ts(v("o1"), x, 2047, OP.add)
-        ts(v("o2"), v("o1"), 1, OP.arith_shift_right, -2048, OP.bitwise_and)
-        tt(o, x, v("o2"), OP.subtract)
-    number(v("nbc"), v("nb"))
-    number(v("Ip", RO - 1, S, 8), v("naL%d" % (RO - 1), 0, L))
-    tc(at("Ip", v("PL")), v("nbc"))
-    run("Y", lambda e: e.dma_start(T.yent[:], T.Ip[:, 0:S]), regs(v("Ip", 0, S)), [("yent", 0, S)], 0.1, "dY", 16, 6.0)
+    for h in range(2):
+        settle(RO - 1, "Ip", h)
+        lo, hi = 1024 * h, 1024 * h + 1024
+        run("Y", lambda e, lo=lo, hi=hi: e.dma_start(T.yent[:, lo:hi], T.Ip[:, lo:hi]), regs(v("Ip", lo, hi)), [("yent", lo, hi)], 0.1, "dY%d" % h, 16, 4.0)
     issue()

@@ -3,21 +3,28 @@ from concourse.mybir import AluOpType as OP, ActivationFunctionType as AF
 
 L, H, S, NM, RO, C0 = 256, 128, 2048, 4096, 4, 12
 SW_ = S + L
-VG = (0,)
+VG = (0, 2)
 SG = ((1, 2, 3), (0, 1, 2, 3))
-AH1, AH2, AH3 = 6.0, 3.0, 3.0
-CY, WAKE, HOP, RATE, FX, GAT, SCA = 0.00083, 0.1, 2.0, 50e3, 0.02, 1.56, 3.8
+EQS, SAME = (), (0, 0)
+PE1, PE2, PE3, GAB, E16U = (0, 0), (0, 0, 0, 0), (0, 0), 0, 0
+CY, WAKE, HOP, RATE, FX, GAT, SCA = 0.00083, 0.23, 2.0, 60e3, 0.0, 1.5, 3.6
+PASSES, NOISE, WIN, PEC = 500, 2.0, 1.5, 0.00055
+SPANS = []
+ORDER = []
 
+BIG, MID, OUT = 12582912.0, 8388608.0, -33554432.0
 F32, BF, I32, U16, F16 = "float32", "bfloat16", "int32", "uint16", "float16"
-WEIGHTS = [1.0, -1.0, -16.0, 8.0, 3.0 * 2 ** 25, 2.0 ** 26, -2.0 ** 25, 2.0 ** 24, -2.0 ** 27, -11.0 * 2 ** 24, 5.0 * 2 ** 23, 6.0 * 2 ** 23, 2.0 ** 21]
+WEIGHTS = {BF: [1.0, -1.0, -8.0, -16.0, 8.0, 16.0, 2.0 ** 21, 2.0 ** 23, -2.0 ** 23, 2.0 ** 24, 2.0 ** 25, -2.0 ** 26, -2.0 ** 27,
+                3.0 * 2 ** 24, -3.0 * 2 ** 24, 3.0 * 2 ** 25, 32 * BIG],
+           F32: [1.0, -1.0, -32.0]}
 SCRATCH = {}
 PART = {}
 for _buf, _d, _parts in (
         ("KI", I32, (("c64 c64b", 64), ("j4", 32), ("jj j1 j2 j3", 8), ("pidx pm", 1))),
-        ("KF", F32, (("xp colv DGm DG", L), ("P1 um16", 16), ("wtF kapF pmF p0 an aq", 1), ("lc", 2))),
-        ("TI", I32, (("s1 kd E2 E3 k4 sia za sib zb o1", L), ("ui um sq s5 k5", 16))),
-        ("TF", F32, (("n1 wi E1 sA c1 aN l1 a1c an1 anum CP bN l1b b1 b1c bnum d0 ah big TT wd sc", L), ("KK k0", H))),
-        ("TB", BF, (("same lose ow EQd", L), ("TRI ONEB BDk", H), ("KC", 192), ("KD", 16), ("TG", 4 * H))),
+        ("KF", F32, (("xp colv DGm DG", L), ("P1", 16), ("wtF kapF pmF p0 an aq", 1), ("lc", 2))),
+        ("TI", I32, (("s1 kd E2 E3 k4 sia za sib zb", L), ("ui sq s5 k5", 16))),
+        ("TF", F32, (("n1 wi E1 PBf c1 l1 a1c a1n an1 anum CP bX l1b b1c b1n bnum d0 ah big TT wd sc", L), ("KK k0", H))),
+        ("TB", BF, (("same lose ow EQd oa pen", L), ("ONEB BDk", H), ("KC", 192), ("KD", 16), ("TG", 4 * H))),
         ("TH", F16, (("E16 PB", L), ("IDH", H))),
         ("TU", U16, (("idx EL", L), ("pl PL", 16), ("RU RK", 8), ("RC", 32)))):
     _o = 0
@@ -28,28 +35,25 @@ for _buf, _d, _parts in (
     SCRATCH[_buf] = ("sbuf", [128, _o], _d)
 for _names, _w, _d in (
         ("ENT", S, I32), ("Xp Ip", SW_, F32), ("OWN", SW_, BF), ("FT", NM + 16, BF), ("PI CC W1", S, F32), ("GS", 4096, F32),
-        ("wtS kapS", 1, I32), ("ones B0 B1 ID SEL0 MK", 128, F32), ("SC WX", 2048, BF), ("GF YS", 4096, BF), ("MB", 512, BF),
-        ("ab0", H + 16, F32), ("ab1 nab0 nab1", H, F32), ("us0 us1", 16, F32), ("Ab", 4, F32)):
+        ("wtS kapS", 1, I32), ("ones B0 B1 ID SEL0 MK", 128, F32), ("SC WX", 2048, BF), ("GF YS D", 4096, BF), ("MB", 512, BF),
+        ("OR", 1024, F32), ("LAM SIG IOT KP EM0", 2 * L, BF)):
     for _n in _names.split():
         SCRATCH[_n] = ("sbuf", [128, _w], _d)
 for _n in "Q1 Q2".split():
     SCRATCH[_n] = ("sbuf", [128, 16, 16, 16], BF)
-SCRATCH["D"] = ("sbuf", [128, 4096], BF)
-SCRATCH["OR"] = ("sbuf", [128, 1024], F32)
 SCRATCH["EQ"] = ("sbuf", [128, 16, H], BF)
-SCRATCH["WM"] = ("sbuf", [128, len(WEIGHTS), 128], BF)
-for _n in "LAM SIG IOT EM EM0".split():
-    SCRATCH[_n] = ("sbuf", [128, 2, 2, H], BF)
+for _d in WEIGHTS:
+    SCRATCH["W" + _d] = ("sbuf", [128, len(WEIGHTS[_d]), 128], _d)
 for _n in "pU pA pW pZ pD pS0 pS1".split():
     SCRATCH[_n] = ("psum", [128, 512], F32)
 SCRATCH["pO"] = ("psum", [128, 8, 4, 16], F32)
-MSG = (("a0", H + 16), ("a1", H), ("u0", 16), ("u1", 16), ("n0", H), ("n1", H), ("A", 4))
 SEMAPHORES = ["sV", "sS", "sT", "sG", "dE0", "dE1", "dF", "dW", "dK", "dY0", "dY1"]
-for _t in range(RO):
-    for _n, _w in MSG:
-        if _n != "A" or _t < RO - 1:
-            SCRATCH["L%s%d" % (_n, _t)] = ("sbuf", [128, _w], F32)
-            SEMAPHORES += ["r%s%d" % (_n, _t), "l%s%d" % (_n, _t)]
+for _n, _w, _d in (("a", 16 + L, F32), ("u", 32, I32), ("n", L, F32), ("A", 4, F32)):
+    SCRATCH["O" + _n] = ("sbuf", [128, _w], _d)
+    for _t in range(RO - (_n == "A")):
+        SCRATCH["L%s%d" % (_n, _t)] = ("sbuf", [128, _w], _d)
+        for _h in range(2 - (_n == "A")):
+            SEMAPHORES += ["r%s%d%d" % (_n, _t, _h), "l%s%d%d" % (_n, _t, _h)]
 
 
 def is_psum(b):
@@ -61,103 +65,116 @@ def make_tools(g, T):
     qsem = {"V": "sV", "S": "sS", "T": "sT", "G": "sG"}
     nodes = []
     log, seen = {}, {}
-    ahead = [0.0]
+    lastmm = {}
+    kin, kinds, count = [], {}, {}
+    now = [-1]
 
     def touch(i, rg, wr):
         q, deps = nodes[i][0], nodes[i][6]
         for (b, lo, hi) in rg:
-            bank = is_psum(b)
-            for (l0, h0, w0, j) in log.get(b, []) + (seen.get(b, []) if wr else []):
-                if j == i:
-                    continue
-                if bank and nodes[j][0] != q:
-                    deps[j] = True
-                elif bank and q == "T":
-                    deps[j] = deps.get(j, False)
-                elif l0 < hi and lo < h0 and (w0 or wr):
+            if is_psum(b):
+                nodes[i][7].add(b)
+                if q == "T":
+                    if lastmm.get(b, i) != i:
+                        deps[lastmm[b]] = deps.get(lastmm[b], False)
+                    lastmm[b] = i
+            for (l0, h0, j) in log.get(b, []) + (seen.get(b, []) if wr else []):
+                if j != i and l0 < hi and lo < h0 and not (q == "T" and nodes[j][0] == "T"):
                     deps[j] = True
 
     def note(i, rg, wr):
         for (b, lo, hi) in rg:
-            ent = log.setdefault(b, [])
-            if is_psum(b):
-                q = nodes[i][0]
-                if ent and nodes[ent[-1][3]][0] != q:
-                    p, k = nodes[ent[-1][3]][0], len(ent)
-                    while k and nodes[ent[k - 1][3]][0] == p:
-                        k -= 1
-                    del ent[:k]
-            elif wr:
-                ent[:] = [e for e in ent if not (lo <= e[0] and e[1] <= hi)]
-                seen[b] = [e for e in seen.get(b, []) if not (lo <= e[0] and e[1] <= hi)]
-            else:
-                ent = seen.setdefault(b, [])
-            ent.append((lo, hi, wr, i))
+            if wr:
+                for d in (log, seen):
+                    d[b] = [e for e in d.get(b, []) if not (lo <= e[0] and e[1] <= hi)]
+            (log if wr else seen).setdefault(b, []).append((lo, hi, i))
 
-    def run(q, fn, reads, writes, cost, sem=None, inc=1, lat=0.0):
-        nodes.append([q, fn, sem if sem else qsem[q], inc, cost, lat, {}, sem is None, ahead[0]])
+    def run(q, fn, reads, writes, cost, sem=None, inc=1, lat=0.0, behind=None):
+        nodes.append([q, fn, sem if sem else qsem[q], inc, cost, lat, {} if behind is None else {behind: False}, set()])
         i = len(nodes) - 1
+        name = (q, cost, tuple((b[:2], lo // 8, hi // 8) for b, lo, hi in writes[:1] + reads[:1]))
+        count[name, now[0]] = count.get((name, now[0]), 0) + 1
+        kin.append(kinds.setdefault((name, count[name, now[0]]), len(kinds)))
         touch(i, reads, False)
         touch(i, writes, True)
         note(i, reads, False)
         note(i, writes, True)
         return i
 
-    def landed(b, s, val, after, lat):
-        nodes.append([None, None, s, val, 0.0, lat, {after: True}, False, 0.0])
-        note(len(nodes) - 1, [(b, 0, 1 << 20)], True)
+    def landed(rg, s, val, after, cost):
+        nodes.append([None, None, s, val, cost, 0.0, {after: True}, set()])
+        kin.append(kin[after])
+        note(len(nodes) - 1, rg, True)
 
     def plan():
         n = len(nodes)
-        succ = [[] for _ in range(n)]
-        left = [len(nd[6]) for nd in nodes]
-        for i, nd in enumerate(nodes):
-            for j, w in nd[6].items():
-                succ[j].append((i, w))
+        before = [[(j, nodes[j][5] + (WAKE if nd[0] else 0.0) if w else 0.0) for j, w in nd[6].items()] for nd in nodes]
+        after = [[] for _ in range(n)]
+        for i in range(n):
+            for j, d in before[i]:
+                after[j].append((i, d))
+        lat = [nd[5] for nd in nodes]
         way = [0.0] * n
         for i in range(n - 1, -1, -1):
-            way[i] = nodes[i][4] + nodes[i][5] + max([way[k] + (WAKE if w else 0.0) for k, w in succ[i]] + [0.0])
-        for i, nd in enumerate(nodes):
-            way[i] += nd[8]
-        ready = {q: [] for q in queue}
-        free = {q: 0.0 for q in queue}
-        at = [0.0] * n
-        out = []
+            way[i] = nodes[i][4] + max([way[k] + d for k, d in after[i]] + [lat[i]])
 
-        def opened(i):
-            if nodes[i][0] is None:
-                done(i, at[i])
+        SPANS.append(max(way))
+
+        def first(lst, s):
+            lo, hi = 0, len(lst)
+            while lo < hi:
+                m = (lo + hi) // 2
+                if lst[m][1] <= s:
+                    lo = m + 1
+                else:
+                    hi = m
+            return lo
+
+        def place(key, pre, post, tail):
+            left, at, end = [len(p) for p in pre], list(tail), [0.0] * n
+            taken = {}
+            ready = [i for i in range(n) if not left[i]]
+            while ready:
+                i = min(ready, key=lambda k: (key[k], k))
+                ready.remove(i)
+                q, c, s, t = nodes[i][0], nodes[i][4], at[i], -1.0
+                lists = [taken.setdefault(x, []) for x in [q] + sorted(nodes[i][7])]
+                while s > t:
+                    t = s
+                    for lst in lists:
+                        k = first(lst, s - WAKE)
+                        while k < len(lst) and lst[k][0] < s + c + WAKE:
+                            pad = 0.0 if lst[k][2] == q else WAKE
+                            if lst[k][0] < s + c + pad - 1e-9 and lst[k][1] + pad > s + 1e-9:
+                                s = lst[k][1] + pad
+                            k += 1
+                for lst in lists:
+                    lst.insert(first(lst, s + 1e-9), (s, s + c, q))
+                end[i] = s + c
+                for k, d in post[i]:
+                    at[k] = max(at[k], end[i] + d)
+                    left[k] -= 1
+                    if not left[k]:
+                        ready.append(k)
+            return end
+        rng = np.random.default_rng(1)
+        key, best = [-x for x in way], None
+        for p in range(PASSES):
+            end = place(key, before, after, [0.0] * n)
+            span = max(e + d for e, d in zip(end, lat))
+            if best is None or span <= best[0]:
+                best = (span, end)
+            SPANS.append(round(span, 1))
+            if p < 3 or p % 8 == 0:
+                key = [-x for x in place([-x for x in best[1]], after, before, lat)]
             else:
-                ready[nodes[i][0]].append(i)
-
-        def done(i, start):
-            fin = start + nodes[i][4]
-            for k, w in succ[i]:
-                if w:
-                    at[k] = max(at[k], fin + nodes[i][5] + (WAKE if nodes[k][0] is not None else 0.0))
-                left[k] -= 1
-                if left[k] == 0:
-                    opened(k)
-        for i in range(n):
-            if not nodes[i][6]:
-                opened(i)
-        while True:
-            best = None
-            for q, lst in ready.items():
-                if not lst:
-                    continue
-                first = min(max(at[i], free[q]) for i in lst)
-                i = max([i for i in lst if max(at[i], free[q]) <= first + 0.02], key=lambda i: (way[i], -i))
-                if best is None or first < best[0]:
-                    best = (first, q, i)
-            if best is None:
-                return out
-            q, i = best[1], best[2]
-            start = max(at[i], free[q])
-            free[q] = start + nodes[i][4]
-            ready[q].remove(i)
-            out.append(i)
-            done(i, start)
+                pick = kin[int(n * rng.random())]
+                mids = [best[1][i] for i in range(n) if kin[i] == pick]
+                if p % 3 == 0:
+                    mids = mids[p // 3 % len(mids):][:1]
+                x = NOISE * rng.random() * (rng.random(n) - 0.5)
+                key = [e - nd[4] + (x[k] if min(abs(e - m) for m in mids) < WIN else 0.0) for e, nd, k in zip(best[1], nodes, kin)]
+        return sorted((i for i in range(n) if nodes[i][0]), key=lambda i: (best[1][i] - nodes[i][4], i))
 
     def issue():
         total, val, know, known = {}, {}, {}, {q: {} for q in queue}
@@ -165,8 +182,16 @@ def make_tools(g, T):
             if nd[0] is None:
                 total[nd[2]] = total.get(nd[2], 0) + nd[3]
                 val[i], know[i] = total[nd[2]], {}
-        for i in plan():
+        if not ORDER:
+            ORDER.extend(plan())
+        turn = {}
+        for i in ORDER:
             q, fn, s, inc = nodes[i][:4]
+            for b in nodes[i][7]:
+                for p, j in turn.setdefault(b, {}).items():
+                    if p != q:
+                        nodes[i][6][j] = True
+                turn[b][q] = i
             deps = [j for j, w in nodes[i][6].items() if w]
             best = {}
             for j in deps:
@@ -192,14 +217,14 @@ def make_tools(g, T):
         for s, x in total.items():
             if known["G"].get(s, 0) < x:
                 g.wait_ge(T.sem[s], x)
-    return run, landed, issue, ahead
+    return run, landed, issue, now
 
 
 def rank_program(g, core, T, topo):
     rank = T.rank_of(core)
     if rank is None:
         return
-    run, landed, issue, ahead = make_tools(g, T)
+    run, landed, issue, now = make_tools(g, T)
     cores = list(T.cores)
 
     def size(b):
@@ -214,6 +239,9 @@ def rank_program(g, core, T, topo):
             lo, hi = o + lo, o + (w if hi is None else hi)
         hi = size(b) if hi is None else hi
         return (T[b][:, lo:hi] if st == 1 else T[b][:, lo:hi:st], [(b, lo, hi)], len(range(lo, hi, st)))
+
+    def f(b, h, n=H, o=0, st=1):
+        return v(b, n * h + o, n * h + n, st)
 
     def w(b, *ix):
         ix = tuple(slice(*k) if isinstance(k, tuple) else k for k in ix)
@@ -237,23 +265,26 @@ def rank_program(g, core, T, topo):
     def ap(x):
         return x[0] if isv(x) else x
 
-    def wide(*xs):
-        return any(SCRATCH[x[1][0][0]][2] in (F32, I32) for x in xs)
+    def dtype(x):
+        return SCRATCH[x[1][0][0]][2]
 
-    def vec(f, o, ins, k):
+    def wide(*xs):
+        return any(dtype(x) in (F32, I32) for x in xs)
+
+    def vec(fn, o, ins, k):
         if len(o) > 3:
-            run("V", f, regs(*ins) + o[1][1:], o[1][:1], 0.05 + SCA * o[2] * CY)
+            run("V", fn, regs(*ins) + o[1][1:], o[1][:1], 0.05 + SCA * o[2] * CY)
         elif len(ins[0]) > 3:
-            run("V", f, regs(*ins), regs(o), 0.05 + GAT * o[2] * CY)
+            run("V", fn, regs(*ins), regs(o), 0.05 + GAT * o[2] * CY)
         else:
-            run("V", f, regs(*ins), regs(o), FX + max(64, o[2] * k) * CY)
+            run("V", fn, regs(*ins), regs(o), FX + max(64, o[2] * k) * CY)
 
     def ts(o, a, s1, op0, s2=None, op1=None):
         if op1 is None:
-            f = lambda e: e.tensor_scalar(out=o[0], in0=a[0], scalar1=ap(s1), scalar2=None, op0=op0)
+            fn = lambda e: e.tensor_scalar(out=o[0], in0=a[0], scalar1=ap(s1), scalar2=None, op0=op0)
         else:
-            f = lambda e: e.tensor_scalar(out=o[0], in0=a[0], scalar1=ap(s1), scalar2=ap(s2), op0=op0, op1=op1)
-        vec(f, o, [a, s1, s2], 1.0 if wide(o, a) else 0.5)
+            fn = lambda e: e.tensor_scalar(out=o[0], in0=a[0], scalar1=ap(s1), scalar2=ap(s2), op0=op0, op1=op1)
+        vec(fn, o, [a, s1, s2], 1.0 if wide(o, a) else 0.5)
 
     def tt(o, a, b, op):
         vec(lambda e: e.tensor_tensor(out=o[0], in0=a[0], in1=b[0], op=op), o, [a, b], 1.0 if any(is_psum(x[1][0][0]) for x in (a, b)) else 2.0)
@@ -270,42 +301,51 @@ def rank_program(g, core, T, topo):
     def act(o, a, func=AF.Identity, scale=1.0, bias=0.0, accum=None):
         b0, s0 = ap(bias), ap(scale)
         if accum is None:
-            f = lambda e: e.activation(out=o[0], in_=a[0], func=func, bias=b0, scale=s0)
+            fn = lambda e: e.activation(out=o[0], in_=a[0], func=func, bias=b0, scale=s0)
         else:
-            f = lambda e: e.activation(out=o[0], in_=a[0], func=func, bias=b0, scale=s0, accum_out=accum[0])
-        run("S", f, regs(a, bias, scale), regs(o, accum), 0.065 + o[2] * GAT * CY if len(a) > 3 else FX + max(64, o[2]) * CY)
+            fn = lambda e: e.activation(out=o[0], in_=a[0], func=func, bias=b0, scale=s0, accum_out=accum[0])
+        run("S", fn, regs(a, bias, scale), regs(o, accum), 0.065 + o[2] * GAT * CY if len(a) > 3 else FX + max(64, o[2]) * CY)
 
     def mm(o, lT, r, start, stop):
-        k = 4.0 if SCRATCH[lT[1][0][0]][2] == F32 else 1.0
-        run("T", lambda e: e.matmul(out=o[0], lhsT=lT[0], rhs=r[0], start=start, stop=stop), regs(lT, r), regs(o), 0.00071 * k * max(64, o[2]))
+        k = 4.0 if dtype(lT) == F32 else 1.0
+        run("T", lambda e: e.matmul(out=o[0], lhsT=lT[0], rhs=r[0], start=start, stop=stop), regs(lT, r), regs(o), PEC * k * max(64, o[2]))
+
+    used = set()
+
+    def diag(c, d=BF):
+        k = WEIGHTS[d].index(c)
+        if (k, d) not in used:
+            used.add((k, d))
+            act(w("W" + d, k), v("ID"), AF.Copy, scale=c)
+        return w("W" + d, k)
 
     def total(o, terms):
         for k, (c, x) in enumerate(terms):
-            mm(o, w("WM", WEIGHTS.index(c)), x, k == 0, k == len(terms) - 1)
+            mm(o, diag(c, dtype(x)), x, k == 0, k == len(terms) - 1)
 
     def iota(o, pattern, base, cm):
-        if SCRATCH[o[1][0][0]][2] != I32:
-            f = lambda e: e.iota(o[0], pattern, base, cm, allow_small_or_imprecise_dtypes=True)
+        if dtype(o) != I32:
+            fn = lambda e: e.iota(o[0], pattern, base, cm, allow_small_or_imprecise_dtypes=True)
         else:
-            f = lambda e: e.iota(o[0], pattern, base, cm)
-        run("G", f, [], regs(o), 0.13 + 2 * o[2] * CY)
+            fn = lambda e: e.iota(o[0], pattern, base, cm)
+        run("G", fn, [], regs(o), 0.13 + 2 * o[2] * CY)
 
     def asel(o, a, pattern, cmp, base, cm, other=0.0):
         run("G", lambda e: e.affine_select(out=o[0], in_=a[0], pattern=pattern, compare_op=cmp, fill=other, base=base, channel_multiplier=cm), regs(a), regs(o), 0.17 + 2 * o[2] * CY)
 
-    def send(src, kind, t, to, frm):
+    def send(kind, t, h, lo, hi, to, frm):
         rid, pid = topo.addr(to)[:2]
         m = topo.mask(core, to)
-        dst, rs, ls = ["%s%s%d" % (x, kind, t) for x in "Lrl"]
+        src, dst, rs, ls = v("O" + kind, lo, hi), v("L%s%d" % (kind, t), lo, hi), "r%s%d%d" % (kind, t, h), "l%s%d%d" % (kind, t, h)
 
-        def f(e):
-            e.remote_dma(out_ap=T[dst][:], in_ap=T[src][:], remote_sem=T.sem[rs], local_sem=T.sem[ls], pid=pid, routing_id=rid, dma_engine_mask=m)
-        i = run("G", f, [(src, 0, size(src))], [], 0.1, sem=ls, inc=len(topo.engines(core, to)))
-        landed(dst, rs, len(topo.engines(frm, core)), i, HOP + 512 * size(src) / RATE)
+        def fn(e):
+            e.remote_dma(out_ap=dst[0], in_ap=src[0], remote_sem=T.sem[rs], local_sem=T.sem[ls], pid=pid, routing_id=rid, dma_engine_mask=m)
+        i = run("G", fn, src[1], [], 0.1, sem=ls, inc=len(topo.engines(core, to)), lat=HOP)
+        landed(dst[1], rs, len(topo.engines(frm, core)), i, 512 * (hi - lo) / RATE)
 
-    run("Y", lambda e: e.dma_start(T.ENT[:, 0:1024], T.ent[:, 0:1024]), [], regs(v("ENT", 0, 1024)), 0.1, "dE0", 16, 3.5)
-    run("Y", lambda e: e.dma_start(T.FT[:, 16:16 + NM], T.feat[:]), [], regs(v("FT", 16)), 0.1, "dF", 16, 6.5)
-    run("Y", lambda e: e.dma_start(T.ENT[:, 1024:S], T.ent[:, 1024:S]), [], regs(v("ENT", 1024, S)), 0.1, "dE1", 16, 8.0)
+    i = run("Y", lambda e: e.dma_start(T.ENT[:, 0:1024], T.ent[:, 0:1024]), [], regs(v("ENT", 0, 1024)), 0.05, "dE0", 16, 3.7)
+    i = run("Y", lambda e: e.dma_start(T.FT[:, 16:16 + NM], T.feat[:]), [], regs(v("FT", 16)), 0.05, "dF", 16, 7.2, i)
+    run("Y", lambda e: e.dma_start(T.ENT[:, 1024:S], T.ent[:, 1024:S]), [], regs(v("ENT", 1024, S)), 0.05, "dE1", 16, 9.0, i)
     run("S", lambda e: e.dma_start(T.wtS[:], T.wt[:]), [], regs(v("wtS")), 0.1, "dW", 16, 2.0)
     run("S", lambda e: e.dma_start(T.kapS[:], T.kap[:]), [], regs(v("kapS")), 0.1, "dK", 16, 2.0)
 
@@ -317,13 +357,13 @@ def rank_program(g, core, T, topo):
     fill(v("MB"), 1.0)
     fill(v("MB", 0, 512, 16), 0.0)
     fill(v("MK"), 1.0)
-    fill(v("MK", 0, 128, 16), 0.0)
+    fill(v("MK", 0, H, 16), 0.0)
     fill(v("Xp", S, SW_), 0.0)
     fill(v("Ip", S, SW_), 0.0)
+    fill(v("OA"), 0.0)
     fill(v("OWN"), 0.0)
-    fill(v("Ab"), 0.0)
     for t in range(RO):
-        fill(v("TG", H * t, H * t + H), t + 1.0)
+        fill(f("TG", t), t + 1.0)
     iota(v("pidx"), [[0, 1]], 0, 1)
     asel(v("B0"), v("ones"), [[-16, 8], [0, 16]], OP.is_ge, 0, 1)
     asel(v("B1"), v("B0"), [[16, 8], [0, 16]], OP.is_ge, 15, -1)
@@ -333,10 +373,10 @@ def rank_program(g, core, T, topo):
     iota(v("c64"), [[37, 64]], 0, 0)
     iota(v("colv"), [[1, L]], S, 0)
     for k in range(2):
-        iota(v("KC", 64 * k, 64 * k + 64), [[0, 8], [-2048, 8]], 2048 * (15 - 8 * k), 0)
-    iota(v("KC", 128, 192), [[1, 8], [0, 8]], 0, 0)
+        iota(f("KC", k, 64), [[0, 8], [-2048, 8]], 2048 * (15 - 8 * k), 0)
+    iota(f("KC", 2, 64), [[1, 8], [0, 8]], 0, 0)
     for k in range(4):
-        iota(v("PI", 512 * k, 512 * k + 512), [[1, 512]], 512 * k, 0)
+        iota(f("PI", k, 512), [[1, 512]], 512 * k, 0)
     tc(v("wtF"), v("wtS"))
     tc(v("kapF"), v("kapS"))
     ts(v("pm"), v("pidx"), 15, OP.bitwise_and)
@@ -344,18 +384,17 @@ def rank_program(g, core, T, topo):
     ts(v("p0"), v("pmF"), 0.0, OP.is_equal)
     ts(v("SEL0"), v("ones"), v("p0"), OP.mult)
     for q in range(8):
-        act(v("WX", 16 * q, 16 * q + 129 * 15 + 1, 129), v("B1", 16 * q, 16 * q + 16), AF.Copy, scale=v("wtF"))
-        act(v("SC", 16 * q, 16 * q + 129 * 15 + 1, 129), v("B1", 16 * q, 16 * q + 16), AF.Copy, scale=32768.0)
-    for k, c in enumerate(WEIGHTS):
-        act(w("WM", k), v("ID"), AF.Copy, scale=c)
+        act(v("WX", 16 * q, 16 * q + 129 * 15 + 1, 129), f("B1", q, 16), AF.Copy, scale=v("wtF"))
+        act(v("SC", 16 * q, 16 * q + 129 * 15 + 1, 129), f("B1", q, 16), AF.Copy, scale=32768.0)
     act(v("BDk"), v("B1"), AF.Copy, scale=4096.0)
     tc(v("IDH"), v("ID"))
     ts(v("DGm"), v("xp"), v("pmF"), OP.is_equal)
     tt(v("DG"), v("DGm"), v("colv"), OP.mult)
-    ts(v("TRI"), v("xp", 0, H), v("pmF"), OP.is_gt)
+    tri = v("pU", 384, 512)
+    ts(tri, v("xp", 0, H), v("pmF"), OP.is_gt)
     ts(v("KD"), v("DGm", 0, 16), v("kapF"), OP.mult)
     mm(v("pZ", 0, 16), v("BDk"), v("KD"), True, True)
-    act(v("ab0", H, H + 16), v("pZ", 0, 16), AF.Copy, scale=2.0 ** -12)
+    act(v("Oa", 0, 16), v("pZ", 0, 16), AF.Copy, scale=2.0 ** -12)
     ts(v("j1"), v("jj"), v("pmF"), OP.add)
     ts(v("j2"), v("j1"), 2, OP.arith_shift_right, 7, OP.bitwise_and)
     tc(v("RU"), v("j2"))
@@ -371,22 +410,16 @@ def rank_program(g, core, T, topo):
     while n < S:
         act(v("CC", n, 2 * n), v("CC", 0, n), AF.Copy)
         n *= 2
-
-    BIG, MID, OUT = 12582912.0, 8388608.0, -33554432.0
-
-    flat = v
+    one = v("ONEB")
 
     def entries(o, x, tmp, bank):
         ts(tmp, x, -1024.5, OP.add, 2048.0 * BIG, OP.add)
         act(bank, tmp, bias=2048.0 - MID - 2048.0 * BIG)
         tt(o, x, bank, OP.add)
     for h in range(2):
-        ahead[0] = AH1 if h == 0 else 0.0
-        entries(v("ab%d" % h, 0, H), v("ENT", 1024 * h, 1024 * h + 1024, 8), v("n1", H * h, H * h + H), v("pA", H * h, H * h + H))
-    ahead[0] = 0.0
+        entries(v("Oa", 16 + H * h, 16 + H * h + H), f("ENT", h, 1024, 0, 8), f("n1", h), f("pA", h))
     for k in range(4):
-        lo, hi = 512 * k, 512 * k + 512
-        entries(v("Xp", lo, hi), v("ENT", lo, hi), v("W1", lo, hi), (v("pW"), v("pD"), flat("pS0", 0, 512), flat("pS1", 0, 512))[k])
+        entries(f("Xp", k, 512), f("ENT", k, 512), f("W1", k, 512), v(("pW", "pD", "pS0", "pS1")[k]))
 
     def number(o, x, tmp, bank):
         act(tmp, x, scale=2.0 ** -12, bias=BIG)
@@ -394,141 +427,139 @@ def rank_program(g, core, T, topo):
         tt(o, x, bank, OP.subtract)
 
     def settle(t, plane, h):
-        cur, bank = v(plane, t + 1024 * h, 1024 * h + 1024, 8), v("pD", L + H * h, L + H * h + H)
-        act(bank, cur, scale=-2.0, bias=OUT)
-        tt(bank, v("Ln%d%d" % (h, t)), bank, OP.min)
+        cur, bank, new = f(plane, h, 1024, t, 8), f("pD", 2 + h), f("Ln%d" % t, h)
+        if PE1[h]:
+            act(f("pen", h), cur, AF.Relu, bias=2 * MID)
+            total(bank, [(-8.0, f("pen", h)), (1.0, new)])
+        else:
+            act(bank, cur, scale=-2.0, bias=OUT)
+            tt(bank, new, bank, OP.min)
         tt(cur, cur, bank, OP.max)
 
     for t in range(RO):
         clock = C0 + t
+        now[0] = t
         thr = clock - 5
         last = t == RO - 1
         plane = "Ip" if last else "Xp"
         d = 1 + t % 3
         to, frm = cores[(rank + d) % 4], cores[(rank - d) % 4]
 
-        def f(b, h, n=H, o=0, st=1):
-            return v(b, n * h + o, n * h + n, st)
-
         for h in range(2):
-            ahead[0] = AH1 if h == 0 else 0.0
-            ab = v("ab%d" % h, 0, H)
-            lanes = v("Xp", t + 1024 * h, 1024 * h + 1024, 8) if t else ab
-            ts(f("s1", h), lanes if t else v("ENT", 1024 * h, 1024 * h + 1024, 8), -1.0, OP.add)
+            ab = v("Oa", 16 + H * h, 16 + H * h + H)
+            lanes = f("Xp", h, 1024, t, 8) if t else ab
+            ts(f("s1", h), lanes if t else f("ENT", h, 1024, 0, 8), -1.0, OP.add)
             act(f("n1", h), lanes, scale=2.0 ** -12, bias=BIG)
             act(f("pU", h), f("n1", h), scale=2.0 ** -9, bias=(2063 - BIG) / 512)
-            if t:
+            if t and GAB:
+                asel(ab, lanes, [[0, H]], OP.is_ge, 0, 0)
+            elif t:
                 act(ab, lanes, AF.Copy)
-            send("ab%d" % h, "a%d" % h, t, to, frm)
+            send("a", t, h, (16 + H) * h, 16 + H * h + H, to, frm)
             ts(f("kd", h), f("s1", h), 16, OP.bitwise_and)
             tt(f("wi", h), f("pU", h), f("kd", h), OP.subtract)
             ts(f("idx", h), f("wi", h), 512.0, OP.mult, 0.0, OP.max)
         for h in range(2):
-            ahead[0] = AH1 if h == 0 else 0.0
             for q in range(4 * h, 4 * h + 4):
-                o, win = v("GF", 512 * q, 512 * q + 512), at(v("FT"), v("idx", 32 * q, 32 * q + 32))
+                o, win = f("GF", q, 512), at(v("FT"), f("idx", q, 32))
                 if q in VG:
                     tc(o, win)
                 else:
                     act(o, win, AF.Copy)
-                scan(v("YS", 512 * q, 512 * q + 512), v("MB"), o)
+                scan(f("YS", q, 512), v("MB"), o)
             u = v("pU", L + 8 * h, L + 8 * h + 8)
             for x in range(16):
-                mm(u, v("WX", 128 * x, 128 * x + 128), v("YS", 2048 * h + 16 * x + 15, 2048 * h + 2048, 256), x == 0, x == 15)
+                mm(u, f("WX", x), f("YS", h, 2048, 16 * x + 15, 256), x == 0, x == 15)
             tc(f("ui", h, 8), u)
-            ts(f("um", h, 8), f("ui", h, 8), 4095, OP.bitwise_and)
-            tt(f("sq", h, 8), f("um", h, 8), f("um", h, 8), OP.mult)
-            tc(v("us%d" % h, 0, 8), f("um", h, 8))
-            ts(f("s5", h, 8), f("sq", h, 8), 5, OP.arith_shift_right)
-            tc(v("us%d" % h, 8, 16), f("s5", h, 8))
-            send("us%d" % h, "u%d" % h, t, to, frm)
-        ahead[0] = 0.0
+            um, s5 = f("Ou", 2 * h, 8), f("Ou", 2 * h + 1, 8)
+            ts(um, f("ui", h, 8), 4095, OP.bitwise_and)
+            tt(f("sq", h, 8), um, um, OP.mult)
+            ts(f("s5", h, 8) if t else s5, f("sq", h, 8), 5, OP.arith_shift_right)
+            if t:
+                ts(s5, f("s5", h, 8), v("LA%d" % (t - 1), 0, 1), OP.add)
+            send("u", t, h, 16 * h, 16 * h + 16, to, frm)
         if t:
             for h in range(2):
                 settle(t - 1, "Xp", h)
         if last:
             for k in range(4):
-                lo, hi = 512 * k, 512 * k + 512
-                number(v("Ip", lo, hi), v("Xp", lo, hi), v("W1", lo, hi), flat("pS1", 0, 512) if k % 2 else v("pD"))
+                number(f("Ip", k, 512), f("Xp", k, 512), f("W1", k, 512), v("pS1" if k % 2 else "pD"))
 
-        def flags(h, s, x, z, far, x1):
-            lam = w("LAM", h, s)
-            act(far, lam, AF.Relu, scale=262144.0, bias=262144.0 * (16 - thr))
-            tt(far, z, far, OP.is_le)
-            tt(x1, x, far, OP.mult)
-            act(w("SIG", h, s), lam, AF.Sign, bias=15.5 - thr)
-            act(w("IOT", h, 1 - s), lam, AF.Sign, bias=-0.5)
-            act(w("EM0", h, s), x, AF.Relu, scale=-1.0, bias=1.0)
-            act(w("EM", h, s), x1, AF.Relu, scale=-1.0, bias=1.0)
+        def alone(h, s, x, l2, z, p0, p1, x1, num, n1, k0, k1):
+            lam, keep = f("LAM", 2 * h + s), f("KP", 2 * h + s)
+            if PE2[2 * h + s]:
+                total(p0, [(32 * BIG, one), (-32.0, l2), (1.0, x)])
+                act(p1, p0, AF.Relu, scale=262144.0, bias=262144.0 * (16 - thr))
+                act(lam, p0, AF.Copy)
+            else:
+                act(p0, l2, scale=32.0, bias=-32.0 * BIG)
+                tt(lam, x, p0, OP.subtract)
+                act(p1, lam, AF.Relu, scale=262144.0, bias=262144.0 * (16 - thr))
+            tt(keep, z, p1, OP.is_le)
+            total(k0, [(-MID, one), (2.0 ** 25, keep)])
+            tt(x1, x, k0, OP.min)
+            if last:
+                total(k1, [(2.0 ** 25, keep)])
+                tt(n1, num, k1, OP.min)
+            act(f("SIG", 2 * h + s), lam, AF.Sign, bias=15.5 - thr)
+            act(f("IOT", 2 * h + 1 - s), lam, AF.Sign, bias=-0.5)
+            act(f("EM0", 2 * h + s), x, AF.Relu, scale=-1.0, bias=1.0 - MID)
 
-        act(v("KK"), at(v("La0%d" % t, H, H + 16), v("RK")), AF.Copy)
+        act(v("KK"), at(v("La%d" % t, 0, 16), v("RK")), AF.Copy)
+        lane = [v("La%d" % t, 16 + H * h, 16 + H * h + H) for h in range(2)]
+        a1c = [f("a1c", h) if PE3[h] else f("pA", h) for h in range(2)]
+        a1n = [(f("a1n", h) if PE3[h] else f("pA", 2 + h)) if last else a1c[h] for h in range(2)]
         for h in range(2):
-            ahead[0] = AH2 if h == 0 else 0.0
-            a = v("La%d%d" % (h, t), 0, H)
+            a = lane[h]
             act(f("c1", h), a, scale=1 / 16, bias=7.5 / 16)
             act(f("c1", h), f("c1", h), bias=BIG)
             act(f("c1", h), f("c1", h), bias=-BIG)
             if len(SG[h]) < 4:
                 act(f("OR", h, 512), at(f("c1", h), v("RC")), scale=16.0, bias=-7.5)
-            ahead[0] = 0.0
-            act(f("aN", h), a, bias=MID)
-            p0, p1, keep, a1 = v("pW", L * h, L * h + H), v("pW", L * h + H, L * h + L), v("pA", L * h, L * h + H), v("pA", L * h + H, L * h + L)
-            act(p0, v("CC", t + 1024 * h, 1024 * h + 1024, 8), AF.Copy)
+            p0, p1 = f("pW", 2 * h), f("pW", 2 * h + 1)
+            act(p1, f("CC", h, 1024, t, 8), AF.Copy)
             act(f("l1", h), a, scale=1 / 32, bias=-0.5 / 32)
             act(f("l1", h), f("l1", h), bias=BIG)
-            act(p1, f("l1", h), scale=32.0, bias=-32.0 * BIG)
-            tt(f("sia", h), a, p0, OP.add)
-            tt(w("LAM", h, 0), a, p1, OP.subtract)
+            tt(f("sia", h), a, p1, OP.add)
             ts(f("za", h), f("sia", h), 7 << 15, OP.bitwise_and)
-            flags(h, 0, f("aN", h), f("za", h), keep, a1)
             if last:
-                number(f("anum", h), a, f("an1", h), p0)
-                tt(f("a1c", h), f("anum", h), keep, OP.mult)
-            else:
-                act(f("a1c", h), a1, bias=-MID)
+                number(f("anum", h), a, f("an1", h), f("pA", 2 + h))
+            alone(h, 0, a, f("l1", h), f("za", h), p0, p1, a1c[h], f("anum", h), a1n[h], f("pA", h), f("pA", 2 + h))
 
         for h in range(2):
             bank = "pS%d" % h
-            ahead[0] = AH2 if h == 0 else 0.0
-            us = "Lu%d%d" % (h, t)
-            tt(f("E1", h), at(v(us, 0, 8), v("RU")), v("KK"), OP.mult)
-            if t:
-                act(f("sA", h), at(v(us, 8, 16), v("RU")), bias=v("LA%d" % (t - 1), 0, 1))
-                tt(f("E2", h), f("E1", h), f("sA", h), OP.add)
-            else:
-                tt(f("E2", h), at(v(us, 8, 16), v("RU")), f("E1", h), OP.add)
+            tt(f("E1", h), at(f("Lu%d" % t, 2 * h, 8), v("RU")), v("KK"), OP.mult)
+            tt(f("E2", h), at(f("Lu%d" % t, 2 * h + 1, 8), v("RU")), f("E1", h), OP.add)
             ts(f("E3", h), f("E2", h), 2047, OP.bitwise_and)
             tc(f("EL", h), f("E3", h))
-            tc(f("E16", h), f("E3", h))
+            tc(f("E16", h), f("EL" if E16U else "E3", h))
             if SG[h]:
                 for m in range(4):
                     act(w("pO", (0, 8), m), f("c1", h), scale=16.0, bias=-7.5)
             blk = (8 * h, 8 * h + 8)
             for k in range(2):
                 for q in (2 * k, 2 * k + 1):
-                    lo, ms = 2048 * h + 512 * q, (4 * q, 4 * q + 4)
-                    o, win = v("D", lo, lo + 512), at(v("Xp"), v("EL", H * h + 32 * q, H * h + 32 * q + 32))
+                    ms = (4 * q, 4 * q + 4)
+                    o, win = f("D", 4 * h + q, 512), at(v("Xp"), f("EL", 4 * h + q, 32))
                     if q in SG[h]:
-                        act(v("GS", lo, lo + 512), win, AF.Copy)
-                        tt(o, v("GS", lo, lo + 512), w("pO"), OP.subtract)
+                        act(f("GS", 4 * h + q, 512), win, AF.Copy)
+                        tt(o, f("GS", 4 * h + q, 512), w("pO"), OP.subtract)
                     else:
                         tt(o, win, f("OR", h, 512), OP.subtract)
                     ts(w("Q1", blk, ms), o, 4096.0 * (BIG + 1), OP.add, 4096.0 * (BIG + 1), OP.is_equal)
                     ts(w("Q2", blk, ms), o, 16.0 * BIG, OP.add, 16.0 * BIG, OP.not_equal)
                 ms = (8 * k, 8 * k + 8)
-                key = v(bank, 64 * k, 64 * k + 64)
-                mm(key, w("WM", 0), v("KC", 64 * k, 64 * k + 64), True, False)
-                mm(key, w("WM", WEIGHTS.index(2.0 ** 21)), v("KC", 128, 192), False, False)
+                key = f(bank, k, 64)
+                mm(key, diag(1.0), f("KC", k, 64), True, False)
+                mm(key, diag(2.0 ** 21), f("KC", 2, 64), False, False)
                 for m in range(8):
-                    lo = H * h + 64 * k + 32 * (m // 4)
-                    mm(v(bank, 64 * k + m, 64 * k + 64, 8), v("IDH"), v("E16", lo + m % 4, lo + 32, 4), False, False)
+                    mm(f(bank, k, 64, m, 8), v("IDH"), f("E16", 4 * h + 2 * k + m // 4, 32, m % 4, 4), False, False)
                 for Q in ("Q1", "Q2"):
                     for x in range(16):
-                        mm(key, v("SC", 128 * x, 128 * x + 128), w(Q, blk, ms, x), False, Q == "Q2" and x == 15)
+                        mm(key, f("SC", x), w(Q, blk, ms, x), False, Q == "Q2" and x == 15)
                 if k == 0:
                     act(f("k0", h, 64), key, AF.Copy)
-            ahead[0] = AH3 if h == 0 else 0.0
-            scan(f("k4", h, 64), f("k0", h, 64), v(bank, 64, H), OP.max)
+            scan(f("k4", h, 64), f("k0", h, 64), f(bank, 1, 64), OP.max)
             ts(f("k5", h, 8), f("k4", h, 64, 7, 8), 2047, OP.bitwise_and)
             pl = f("pl", h, 8)
             tc(pl, f("k5", h, 8))
@@ -536,73 +567,87 @@ def rank_program(g, core, T, topo):
             tc(f("PB", h), at(v("PI"), pl))
             act(f("l1b", h), at(v("Xp"), pl), scale=1 / 32, bias=-0.5 / 32)
             act(f("CP", h), at(v("CC"), pl), AF.Copy)
-            act(f("bN", h), at(v("Xp"), pl), bias=MID)
+            act(f("bX", h), at(v("Xp"), pl), AF.Copy)
             tt(f("sib", h), at(v("Xp"), pl), f("CP", h), OP.add)
             if last:
                 act(f("bnum", h), at(v("Ip"), pl), AF.Copy)
             if h:
                 act(f("ow", h), at(v("OWN"), pl), AF.Relu, bias=-float(t))
-            for c in range(8):
-                ts(w("EQ", 8 * h + c, (0, H - 16 * c)), f("PB", h, H, 16 * c), v("P1", 8 * h + c, 8 * h + c + 1), OP.is_equal)
-            tt(f("EQd", h), w("EQ", blk, (0, 16)), v("TRI"), OP.mult)
+            hi = H * h + H
+            mine = [c for c in range(*blk) if c in EQS]
+            if mine:
+                act(v("PBf", 16 * mine[0], hi), at(v("PI"), v("pl", mine[0], blk[1])), AF.Copy)
+            for c in range(*blk):
+                eq = w("EQ", c, (0, hi - 16 * c))
+                if c in mine:
+                    act(eq, v("PBf", 16 * c, hi), AF.Abs, scale=-1.0, bias=f("P1", c, 1))
+                    act(eq, eq, AF.Relu, scale=-1.0, bias=1.0)
+                else:
+                    ts(eq, v("PB", 16 * c, hi), f("P1", c, 1), OP.is_equal)
+            tt(f("EQd", h), w("EQ", blk, (0, 16)), tri, OP.mult)
             cnt = f("pD", h)
             mm(cnt, v("IDH"), f("PB", h), True, False)
             if h:
                 mm(cnt, v("BDk"), f("ow", h), False, False)
-            for c in range(7):
-                mm(f("pD", h, H, 16 * c + 16), v("BDk"), w("EQ", 8 * h + c, (16, H - 16 * c)), False, False)
+            for c in range(blk[0], blk[1] - 1):
+                mm(v("pD", 16 * c + 16, hi), v("BDk"), w("EQ", c, (16, hi - 16 * c)), False, False)
             mm(cnt, v("BDk"), f("EQd", h), False, True)
             tt(f("wd", h), cnt, f("DG", h), OP.min)
-            act(f("lose", h), cnt, AF.Sign, bias=-2047.5, accum=v("lc", h, h + 1))
+            act(f("lose", h), cnt, AF.Sign, bias=-2047.5, accum=f("lc", h, 1))
             scan(f("sc", h), v("MK"), f("wd", h))
             tc(f("PL", h, 8), f("sc", h, H, 15, 16))
             if h == 0:
                 tc(at(v("OWN"), f("PL", h, 8)), f("TG", t))
-            r, keep = flat(bank, H, 2 * H), flat(bank, 2 * H, 3 * H)
+            b1c, b1n = f("b1c", h), f("b1n" if last else "b1c", h)
             act(f("l1b", h), f("l1b", h), bias=BIG)
-            act(r, f("l1b", h), scale=32.0, bias=MID - 32.0 * BIG)
-            tt(w("LAM", h, 1), f("bN", h), r, OP.subtract)
             ts(f("zb", h), f("sib", h), 7 << 15, OP.bitwise_and)
-            flags(h, 1, f("bN", h), f("zb", h), keep, f("b1", h))
-            if last:
-                tt(f("b1c", h), f("bnum", h), keep, OP.mult)
+            alone(h, 1, f("bX", h), f("l1b", h), f("zb", h), f(bank, 1), f(bank, 2), b1c, f("bnum", h), b1n, f(bank, 1), f(bank, 2))
+            if PE3[h]:
+                d0 = f(bank, 3)
+                total(d0, [(-1.0, a1c[h]), (1.0, b1c)])
             else:
-                act(f("b1c", h), f("b1", h), bias=-MID)
-            tt(f("d0", h), f("b1", h), v("pA", L * h + H, L * h + L), OP.subtract)
-            ts(f("same", h), f("d0", h), 4096.0 * BIG, OP.add, 4096.0 * BIG, OP.is_equal)
-            om = f("pW", h, L)
-            total(om, [(-1.0, w("LAM", h)), (-16.0, w("SIG", h)), (8.0, w("IOT", h))] + [(-16.0, w("EM", h))] * last)
-            act(om, om, AF.Relu, bias=clock - 39.0)
-            oa, ob = v("pW", L * h, L * h + H), v("pW", L * h + H, L * h + L)
-            tt(f("ah", h), f("a1c", h), oa, OP.add)
-            tt(ob, f("b1c", h), ob, OP.add)
-            tt(f("big", h), f("ah", h), ob, OP.max)
-            zz, zk = v("pZ", L * h, L * h + H), v("pZ", L * h + H, L * h + L)
-            total(zz, [(-11.0 * 2 ** 24, v("ONEB")), (2.0 ** 26, w("EM", h, 0)), (-2.0 ** 25, w("EM0", h, 0)), (2.0 ** 24, w("SIG", h, 0)),
-                       (-2.0 ** 25, w("EM0", h, 1)), (2.0 ** 24, w("SIG", h, 1)), (2.0 ** 26, w("EM", h, 1)),
-                       (3.0 * 2 ** 25, f("same", h)), (-2.0 ** 27, f("lose", h))])
+                d0 = f("d0", h)
+                tt(d0, b1c, a1c[h], OP.subtract)
+            if SAME[h]:
+                act(d0, d0, AF.Abs)
+                act(f("same", h), d0, AF.Sign, scale=-1.0, bias=2048.0)
+            else:
+                ts(f("same", h), d0, 4096.0 * BIG, OP.add, 4096.0 * BIG, OP.is_equal)
+            total(f("pW", h, L), [(c, f(b, h, L)) for c, b in [(-1.0, "LAM"), (-16.0, "SIG"), (8.0, "IOT")] + [(16.0, "KP")] * last])
+            oa, ob = f("pW", 2 * h), f("pW", 2 * h + 1)
+            act(f("oa", h), oa, AF.Relu, bias=clock - 39.0 - 16 * last)
+            act(ob, ob, AF.Relu, bias=clock - 39.0 - 16 * last)
+            if PE3[h]:
+                total(f("pA", h), [(1.0, a1n[h]), (1.0, f("oa", h))])
+                tt(f("ah", h), b1n, ob, OP.add)
+                tt(f("big", h), f("ah", h), f("pA", h), OP.max)
+            else:
+                tt(f("ah", h), f("oa", h), a1n[h], OP.add)
+                tt(ob, b1n, ob, OP.add)
+                tt(f("big", h), f("ah", h), ob, OP.max)
+            zz, zk = f("pZ", 2 * h), f("pZ", 2 * h + 1)
+            total(zz, [(-3.0 * 2 ** 24, one)] * (not SAME[h])
+                  + [(c, f(b, 2 * h + s)) for s in range(2) for c, b in ((2.0 ** 25, "EM0"), (2.0 ** 24, "SIG"), (-2.0 ** 26, "KP"))]
+                  + [(3.0 * 2 ** (24 if SAME[h] else 25), f("same", h)), (-2.0 ** 27, f("lose", h))])
             tt(f("TT", h), f("big", h), zz, OP.min)
-            total(zk, [((6.0 if last else 5.0) * 2 ** 23, v("ONEB")), (-2.0 ** 25, w("EM", h, 0)), (2.0 ** 24, w("EM0", h, 0)), (2.0 ** 24, w("EM0", h, 0)),
-                       (2.0 ** 24, f("lose", h))])
-            tt(zk, f("anum", h) if last else v("La%d%d" % (h, t), 0, H), zk, OP.min)
-            tt(v("nab%d" % h), f("TT", h), zk, OP.max)
-            send("nab%d" % h, "n%d" % h, t, frm, to)
-        ahead[0] = 0.0
+            total(zk, [(2.0 ** (24 if last else 23), one), (2.0 ** 25, f("KP", 2 * h)), (2.0 ** 24, f("lose", h))])
+            tt(zk, f("anum", h) if last else lane[h], zk, OP.min)
+            tt(f("On", h), f("TT", h), zk, OP.max)
+            send("n", t, h, H * h, H * h + H, frm, to)
         mine = v(plane, t, S, 8)
         asel(mine, mine, [[0, L]], OP.is_gt, 0, 0, OUT)
         for h in range(2):
-            tt(at(v(plane), f("PL", h, 8)), f("b1c", h), f("TT", h), OP.max)
+            tt(at(v(plane), f("PL", h, 8)), f("b1n" if last else "b1c", h), f("TT", h), OP.max)
         if not last:
             col = v("pU", 300, 301)
             for h in range(2):
-                mm(col, v("SEL0"), v("lc", h, h + 1), h == 0, h == 1)
+                mm(col, v("SEL0"), f("lc", h, 1), h == 0, h == 1)
             act(v("an"), col, AF.Copy, scale=-0.5)
             act(v("aq"), v("an"), scale=1 / 32, bias=-15.5 / 32)
             act(v("aq"), v("aq"), bias=BIG)
             act(v("aq"), v("aq"), bias=-BIG)
-            act(v("Ab", 0, 1), v("aq"), scale=-32.0, bias=v("an"))
-            dn = 1 + (t + 1) % 3
-            send("Ab", "A", t, cores[(rank - d + dn) % 4], cores[(rank - dn + d) % 4])
+            act(v("OA", 0, 1), v("aq"), scale=-32.0, bias=v("an"))
+            send("A", t, 0, 0, 4, frm, to)
 
     for h in range(2):
         settle(RO - 1, "Ip", h)

@@ -6,27 +6,31 @@ SW_ = S + L
 VG = (0, 2)
 SG = ((1, 2, 3), (0, 1, 2, 3))
 EQS, SAME = (), (0, 0)
-PE1, PE2, PE3, GAB, E16U = (0, 0), (0, 0, 0, 0), (0, 0), 0, 0
-CY, WAKE, HOP, RATE, FX, GAT, SCA = 0.00083, 0.23, 2.0, 60e3, 0.0, 1.5, 3.6
-PASSES, NOISE, WIN, PEC = 500, 2.0, 1.5, 0.00055
-SPANS = []
+PARTS = MP = AMSG = NMSG = IDX = ((0, 128), (128, 256))
+VD, FAST, LATE, Q2S = ((0,), (), (), ()), (0, 1), (1, 0, 0), ()
+CY, WAKE, HOP, RATE, FX, GAT, SCA = 0.00083, 0.23, 1.7, 60e3, 0.0, 1.5, 3.6
+PASSES, NOISE, WIN, PEC = 2000, 2.0, 1.5, 0.00055
+SPANS, DBG, SLACK, MEAN = [], [], 0.1, 0.3
+FASTA, FIRST = (1, 1), (0,)
+LOADS, HALF = (0, "F", 1), 1.4
+NLAST = ((0, 128), (128, 192), (192, 256))
 ORDER = []
 
 BIG, MID, OUT = 12582912.0, 8388608.0, -33554432.0
 F32, BF, I32, U16, F16 = "float32", "bfloat16", "int32", "uint16", "float16"
-WEIGHTS = {BF: [1.0, -1.0, -8.0, -16.0, 8.0, 16.0, 2.0 ** 21, 2.0 ** 23, -2.0 ** 23, 2.0 ** 24, 2.0 ** 25, -2.0 ** 26, -2.0 ** 27,
-                3.0 * 2 ** 24, -3.0 * 2 ** 24, 3.0 * 2 ** 25, 32 * BIG],
+WEIGHTS = {BF: [1.0, -1.0, -16.0, 8.0, 16.0, 2.0 ** 21, 2.0 ** 23, -2.0 ** 23, 2.0 ** 24, 2.0 ** 25, -2.0 ** 25, 2.0 ** 26, -2.0 ** 26,
+                -2.0 ** 27, -7.0 * 2 ** 24, 3.0 * 2 ** 25],
            F32: [1.0, -1.0, -32.0]}
 SCRATCH = {}
 PART = {}
 for _buf, _d, _parts in (
         ("KI", I32, (("c64 c64b", 64), ("j4", 32), ("jj j1 j2 j3", 8), ("pidx pm", 1))),
-        ("KF", F32, (("xp colv DGm DG", L), ("P1", 16), ("wtF kapF pmF p0 an aq", 1), ("lc", 2))),
-        ("TI", I32, (("s1 kd E2 E3 k4 sia za sib zb", L), ("ui sq s5 k5", 16))),
-        ("TF", F32, (("n1 wi E1 PBf c1 l1 a1c a1n an1 anum CP bX l1b b1c b1n bnum d0 ah big TT wd sc", L), ("KK k0", H))),
-        ("TB", BF, (("same lose ow EQd oa pen", L), ("ONEB BDk", H), ("KC", 192), ("KD", 16), ("TG", 4 * H))),
+        ("KF", F32, (("DG", L), ("xp", H), ("P1 DGm LL l16", 16), ("wtF kapF pmF p0 an aq", 1), ("lc", 4))),
+        ("TI", I32, (("s1 kd E2 E3 k4 sia za sib zb loa lob U1 U2 U3", L), ("ui sq s5 k5", 16))),
+        ("TF", F32, (("n1 wi E1 c1 l1 an1 anum CP bN l1b b1 b1c bnum d0 ah big TT wd sc k0 PBf", L), ("KK128", H), ("KK64", 64))),
+        ("TB", BF, (("same lose ow EQd oa KP EM", L), ("ONEB BDk", H), ("KC", 256), ("KD", 16), ("TG", 4 * H))),
         ("TH", F16, (("E16 PB", L), ("IDH", H))),
-        ("TU", U16, (("idx EL", L), ("pl PL", 16), ("RU RK", 8), ("RC", 32)))):
+        ("TU", U16, (("idx EL", L), ("pl PL", 16), ("RU128 RK128", 8), ("RU64 RK64", 4), ("RC", 32)))):
     _o = 0
     for _names, _w in _parts:
         for _n in _names.split():
@@ -35,8 +39,8 @@ for _buf, _d, _parts in (
     SCRATCH[_buf] = ("sbuf", [128, _o], _d)
 for _names, _w, _d in (
         ("ENT", S, I32), ("Xp Ip", SW_, F32), ("OWN", SW_, BF), ("FT", NM + 16, BF), ("PI CC W1", S, F32), ("GS", 4096, F32),
-        ("wtS kapS", 1, I32), ("ones B0 B1 ID SEL0 MK", 128, F32), ("SC WX", 2048, BF), ("GF YS D", 4096, BF), ("MB", 512, BF),
-        ("OR", 1024, F32), ("LAM SIG IOT KP EM0", 2 * L, BF)):
+        ("wtS kapS", 1, I32), ("ones B0 B1 ID SEL0 MK", 128, F32), ("SC SH WX", 2048, BF), ("GF YS D AB", 4096, BF), ("MB", 512, BF),
+        ("OR", 1024, F32), ("LAM SIG IOT EM0", 2 * L, BF)):
     for _n in _names.split():
         SCRATCH[_n] = ("sbuf", [128, _w], _d)
 for _n in "Q1 Q2".split():
@@ -47,12 +51,12 @@ for _d in WEIGHTS:
 for _n in "pU pA pW pZ pD pS0 pS1".split():
     SCRATCH[_n] = ("psum", [128, 512], F32)
 SCRATCH["pO"] = ("psum", [128, 8, 4, 16], F32)
-SEMAPHORES = ["sV", "sS", "sT", "sG", "dE0", "dE1", "dF", "dW", "dK", "dY0", "dY1"]
-for _n, _w, _d in (("a", 16 + L, F32), ("u", 32, I32), ("n", L, F32), ("A", 4, F32)):
+SEMAPHORES = ["sV", "sS", "sT", "sG", "dE0", "dE1", "dF", "dW", "dK", "dY0", "dY1", "dY2", "dY3"]
+for _n, _w, _d in (("a", 16 + L, F32), ("u", 64, I32), ("n", L, F32), ("A", 4, F32)):
     SCRATCH["O" + _n] = ("sbuf", [128, _w], _d)
     for _t in range(RO - (_n == "A")):
         SCRATCH["L%s%d" % (_n, _t)] = ("sbuf", [128, _w], _d)
-        for _h in range(2 - (_n == "A")):
+        for _h in range(1 if _n == "A" else 4):
             SEMAPHORES += ["r%s%d%d" % (_n, _t, _h), "l%s%d%d" % (_n, _t, _h)]
 
 
@@ -67,7 +71,7 @@ def make_tools(g, T):
     log, seen = {}, {}
     lastmm = {}
     kin, kinds, count = [], {}, {}
-    now = [-1]
+    now, early = [-1, 3], []
 
     def touch(i, rg, wr):
         q, deps = nodes[i][0], nodes[i][6]
@@ -92,6 +96,8 @@ def make_tools(g, T):
     def run(q, fn, reads, writes, cost, sem=None, inc=1, lat=0.0, behind=None):
         nodes.append([q, fn, sem if sem else qsem[q], inc, cost, lat, {} if behind is None else {behind: False}, set()])
         i = len(nodes) - 1
+        if now[1]:
+            early.append((i, now[1]))
         name = (q, cost, tuple((b[:2], lo // 8, hi // 8) for b, lo, hi in writes[:1] + reads[:1]))
         count[name, now[0]] = count.get((name, now[0]), 0) + 1
         kin.append(kinds.setdefault((name, count[name, now[0]]), len(kinds)))
@@ -119,6 +125,7 @@ def make_tools(g, T):
             way[i] = nodes[i][4] + max([way[k] + d for k, d in after[i]] + [lat[i]])
 
         SPANS.append(max(way))
+        DBG[:] = [nodes, after, way, kinds, kin]
 
         def first(lst, s):
             lo, hi = 0, len(lst)
@@ -131,49 +138,80 @@ def make_tools(g, T):
             return lo
 
         def place(key, pre, post, tail):
-            left, at, end = [len(p) for p in pre], list(tail), [0.0] * n
-            taken = {}
-            ready = [i for i in range(n) if not left[i]]
-            while ready:
-                i = min(ready, key=lambda k: (key[k], k))
-                ready.remove(i)
+            key = list(key)
+            if pre is before:
+                for i, k in early:
+                    key[i] = -way[i] - 1000.0 * k
+            for i in (range(n) if pre is before else range(n - 1, -1, -1)):
+                for j, d in pre[i]:
+                    if key[i] <= key[j]:
+                        key[i] = key[j] + 1e-7
+            at, end, why = list(tail), [0.0] * n, [(-1, False)] * n
+            taken = {x: [] for x in places}
+            for i in sorted(range(n), key=lambda k: key[k]):
                 q, c, s, t = nodes[i][0], nodes[i][4], at[i], -1.0
-                lists = [taken.setdefault(x, []) for x in [q] + sorted(nodes[i][7])]
+                lists = [taken[x] for x in uses[i]]
                 while s > t:
                     t = s
                     for lst in lists:
-                        k = first(lst, s - WAKE)
-                        while k < len(lst) and lst[k][0] < s + c + WAKE:
-                            pad = 0.0 if lst[k][2] == q else WAKE
-                            if lst[k][0] < s + c + pad - 1e-9 and lst[k][1] + pad > s + 1e-9:
-                                s = lst[k][1] + pad
-                            k += 1
+                        if lst and lst[-1][1] > s - WAKE:
+                            k = first(lst, s - WAKE)
+                            while k < len(lst) and lst[k][0] < s + c + WAKE:
+                                pad = 0.0 if lst[k][2] == q else WAKE
+                                if lst[k][0] < s + c + pad - 1e-9 and lst[k][1] + pad > s + 1e-9:
+                                    s = lst[k][1] + pad
+                                    why[i] = (lst[k][3], True)
+                                k += 1
                 for lst in lists:
-                    lst.insert(first(lst, s + 1e-9), (s, s + c, q))
+                    if not lst or lst[-1][0] <= s:
+                        lst.append((s, s + c, q, i))
+                    else:
+                        lst.insert(first(lst, s + 1e-9), (s, s + c, q, i))
                 end[i] = s + c
                 for k, d in post[i]:
-                    at[k] = max(at[k], end[i] + d)
-                    left[k] -= 1
-                    if not left[k]:
-                        ready.append(k)
-            return end
+                    if end[i] + d > at[k]:
+                        at[k] = end[i] + d
+                        why[k] = (i, False)
+            return end, why
+        uses = [[nd[0]] + sorted(nd[7]) for nd in nodes]
+        places = {x for u in uses for x in u}
+        like = {}
+        for i in range(n):
+            like.setdefault(kin[i], []).append(i)
         rng = np.random.default_rng(1)
-        key, best = [-x for x in way], None
+        key, best, cur = [-x for x in way], None, None
         for p in range(PASSES):
-            end = place(key, before, after, [0.0] * n)
-            span = max(e + d for e, d in zip(end, lat))
+            end, why = place(key, before, after, [0.0] * n)
+            span = max(e + d for e, d in zip(end, lat)) + MEAN * sum(end) / n
+            if cur is None or span <= cur[0] + SLACK * (1 - p / PASSES) * rng.random():
+                cur = (span, end, why)
             if best is None or span <= best[0]:
                 best = (span, end)
             SPANS.append(round(span, 1))
-            if p < 3 or p % 8 == 0:
-                key = [-x for x in place([-x for x in best[1]], after, before, lat)]
-            else:
-                pick = kin[int(n * rng.random())]
-                mids = [best[1][i] for i in range(n) if kin[i] == pick]
-                if p % 3 == 0:
-                    mids = mids[p // 3 % len(mids):][:1]
+            key = [e - nd[4] for e, nd in zip(cur[1], nodes)]
+            if p < 3 or p % 16 == 0:
+                key = [-x for x in place([-x for x in cur[1]], after, before, lat)[0]]
+            elif p % 4 == 0:
+                mids = [cur[1][i] for i in like[kin[int(n * rng.random())]]]
                 x = NOISE * rng.random() * (rng.random(n) - 0.5)
-                key = [e - nd[4] + (x[k] if min(abs(e - m) for m in mids) < WIN else 0.0) for e, nd, k in zip(best[1], nodes, kin)]
+                key = [e + (x[k] if min(abs(e - m) for m in mids) < WIN else 0.0) for e, k in zip(key, kin)]
+            else:
+                i, held = max(range(n), key=lambda k: cur[1][k] + lat[k]), []
+                while i >= 0:
+                    j, by = cur[2][i]
+                    if by:
+                        held.append((i, j))
+                    i = j
+                i, j = held[int(len(held) * rng.random())]
+                back = key[i] - key[j] + 1e-3 + rng.random() ** 2
+                pull = rng.random() < 0.6
+                for k in (like[kin[i if pull else j]] if rng.random() < 0.7 else [i if pull else j]):
+                    key[k] += -back if pull else back
+                if pull:
+                    for k in range(n - 1, -1, -1):
+                        for j, d in before[k]:
+                            if key[j] >= key[k]:
+                                key[j] = key[k] - 1e-7
         return sorted((i for i in range(n) if nodes[i][0]), key=lambda i: (best[1][i] - nodes[i][4], i))
 
     def issue():
@@ -238,7 +276,8 @@ def rank_program(g, core, T, topo):
             b, o, w = PART[b]
             lo, hi = o + lo, o + (w if hi is None else hi)
         hi = size(b) if hi is None else hi
-        return (T[b][:, lo:hi] if st == 1 else T[b][:, lo:hi:st], [(b, lo, hi)], len(range(lo, hi, st)))
+        rg = [(b, lo, hi)] if st <= 16 else [(b, k, k + 1) for k in range(lo, hi, st)]
+        return (T[b][:, lo:hi] if st == 1 else T[b][:, lo:hi:st], rg, len(range(lo, hi, st)))
 
     def f(b, h, n=H, o=0, st=1):
         return v(b, n * h + o, n * h + n, st)
@@ -340,43 +379,34 @@ def rank_program(g, core, T, topo):
 
         def fn(e):
             e.remote_dma(out_ap=dst[0], in_ap=src[0], remote_sem=T.sem[rs], local_sem=T.sem[ls], pid=pid, routing_id=rid, dma_engine_mask=m)
-        i = run("G", fn, src[1], [], 0.1, sem=ls, inc=len(topo.engines(core, to)), lat=HOP)
-        landed(dst[1], rs, len(topo.engines(frm, core)), i, 512 * (hi - lo) / RATE)
+        i = run("G", fn, src[1], [], max(0.1, 512 * (hi - lo) / RATE), sem=ls, inc=len(topo.engines(core, to)), lat=HOP)
+        landed(dst[1], rs, len(topo.engines(frm, core)), i, 0.0)
 
-    i = run("Y", lambda e: e.dma_start(T.ENT[:, 0:1024], T.ent[:, 0:1024]), [], regs(v("ENT", 0, 1024)), 0.05, "dE0", 16, 3.7)
-    i = run("Y", lambda e: e.dma_start(T.FT[:, 16:16 + NM], T.feat[:]), [], regs(v("FT", 16)), 0.05, "dF", 16, 7.2, i)
-    run("Y", lambda e: e.dma_start(T.ENT[:, 1024:S], T.ent[:, 1024:S]), [], regs(v("ENT", 1024, S)), 0.05, "dE1", 16, 9.0, i)
-    run("S", lambda e: e.dma_start(T.wtS[:], T.wt[:]), [], regs(v("wtS")), 0.1, "dW", 16, 2.0)
-    run("S", lambda e: e.dma_start(T.kapS[:], T.kap[:]), [], regs(v("kapS")), 0.1, "dK", 16, 2.0)
+    i = run("Y", lambda e: e.dma_start(T.kapS[:], T.kap[:]), [], regs(v("kapS")), 0.05, "dK", 16, 2.0)
+    i = run("Y", lambda e: e.dma_start(T.wtS[:], T.wt[:]), [], regs(v("wtS")), 0.05, "dW", 16, 2.0, i)
+    mb = 0
+    for b in LOADS:
+        mb += 2 if b == "F" else 1
+        o, x = (v("FT", 16), T.feat[:]) if b == "F" else (f("ENT", b, 1024), T.ent[:, 1024 * b:1024 * b + 1024])
+        i = run("Y", lambda e, o=o, x=x: e.dma_start(o[0], x), [], o[1], 0.05, "dF" if b == "F" else "dE%d" % b, 16, 2.0 + mb * HALF, i)
 
     fill(v("ones"), 1.0)
     fill(v("ONEB"), 1.0)
     fill(v("FT", 0, 16), 0.0)
     fill(v("SC"), 0.0)
     fill(v("WX"), 0.0)
+    if Q2S:
+        fill(v("SH"), 0.0)
     fill(v("MB"), 1.0)
     fill(v("MB", 0, 512, 16), 0.0)
-    fill(v("MK"), 1.0)
-    fill(v("MK", 0, H, 16), 0.0)
-    fill(v("Xp", S, SW_), 0.0)
-    fill(v("Ip", S, SW_), 0.0)
     fill(v("OA"), 0.0)
-    fill(v("OWN"), 0.0)
-    for t in range(RO):
-        fill(f("TG", t), t + 1.0)
     iota(v("pidx"), [[0, 1]], 0, 1)
     asel(v("B0"), v("ones"), [[-16, 8], [0, 16]], OP.is_ge, 0, 1)
     asel(v("B1"), v("B0"), [[16, 8], [0, 16]], OP.is_ge, 15, -1)
     asel(v("ID"), v("ones"), [[-1, 128]], OP.is_equal, 0, 1)
-    iota(v("xp"), [[0, 16], [1, 16]], 0, 0)
+    iota(v("xp"), [[0, 8], [1, 16]], 0, 0)
     iota(v("jj"), [[16, 8]], 0, 0)
     iota(v("c64"), [[37, 64]], 0, 0)
-    iota(v("colv"), [[1, L]], S, 0)
-    for k in range(2):
-        iota(f("KC", k, 64), [[0, 8], [-2048, 8]], 2048 * (15 - 8 * k), 0)
-    iota(f("KC", 2, 64), [[1, 8], [0, 8]], 0, 0)
-    for k in range(4):
-        iota(f("PI", k, 512), [[1, 512]], 512 * k, 0)
     tc(v("wtF"), v("wtS"))
     tc(v("kapF"), v("kapS"))
     ts(v("pm"), v("pidx"), 15, OP.bitwise_and)
@@ -386,45 +416,347 @@ def rank_program(g, core, T, topo):
     for q in range(8):
         act(v("WX", 16 * q, 16 * q + 129 * 15 + 1, 129), f("B1", q, 16), AF.Copy, scale=v("wtF"))
         act(v("SC", 16 * q, 16 * q + 129 * 15 + 1, 129), f("B1", q, 16), AF.Copy, scale=32768.0)
+        if Q2S:
+            act(v("SH", 16 * q, 16 * q + 129 * 15 + 1, 129), f("B1", q, 16), AF.Copy, scale=16384.0)
     act(v("BDk"), v("B1"), AF.Copy, scale=4096.0)
     tc(v("IDH"), v("ID"))
-    ts(v("DGm"), v("xp"), v("pmF"), OP.is_equal)
-    tt(v("DG"), v("DGm"), v("colv"), OP.mult)
+    ts(v("DGm"), v("xp", 0, 16), v("pmF"), OP.is_equal)
     tri = v("pU", 384, 512)
     ts(tri, v("xp", 0, H), v("pmF"), OP.is_gt)
     ts(v("KD"), v("DGm", 0, 16), v("kapF"), OP.mult)
     mm(v("pZ", 0, 16), v("BDk"), v("KD"), True, True)
     act(v("Oa", 0, 16), v("pZ", 0, 16), AF.Copy, scale=2.0 ** -12)
+    now[1] = 1
     ts(v("j1"), v("jj"), v("pmF"), OP.add)
-    ts(v("j2"), v("j1"), 2, OP.arith_shift_right, 7, OP.bitwise_and)
-    tc(v("RU"), v("j2"))
-    ts(v("j2"), v("j1"), 3, OP.arith_shift_right, -4, OP.bitwise_and)
     ts(v("j3"), v("j1"), 3, OP.bitwise_and)
-    tt(v("j1"), v("j2"), v("j3"), OP.add)
-    tc(v("RK"), v("j1"))
+    for n in sorted({hi - lo for lo, hi in PARTS}):
+        j1, j2, j3 = [v(b, 0, n // 16) for b in ("j1", "j2", "j3")]
+        ts(j2, j1, 2, OP.arith_shift_right, n // 16 - 1, OP.bitwise_and)
+        tc(v("RU%d" % n), j2)
+        ts(j2, j1, 1 + n // 64, OP.arith_shift_right, -4, OP.bitwise_and)
+        tt(j2, j2, j3, OP.add)
+        tc(v("RK%d" % n), j2)
+    fill(v("Ou"), 0)
     iota(v("j4"), [[16, 8], [0, 4]], 0, 0)
     ts(v("RC"), v("j4"), v("pmF"), OP.add)
     ts(v("c64b"), v("c64"), 63, OP.bitwise_and)
-    ts(v("CC", 0, 64), v("c64b"), 4096.0, OP.mult, -2049.0, OP.add)
+    ts(v("CC", 0, 64), v("c64b"), 4096.0, OP.mult, -2033.0, OP.add)
     n = 64
     while n < S:
         act(v("CC", n, 2 * n), v("CC", 0, n), AF.Copy)
         n *= 2
-    one = v("ONEB")
+    for c in WEIGHTS[BF]:
+        diag(c)
+    for b in ("Xp", "Ip"):
+        for h in range(2):
+            act(v(b, S + H * h, S + H * h + H), v("ones"), AF.Copy)
+    ts(v("MK"), v("xp"), 1.0, OP.min)
+    iota(v("l16"), [[16, 16]], S, 0)
+    ts(v("LL"), v("l16"), v("pmF"), OP.add)
+    for k in range(2):
+        iota(f("KC", k, 64), [[0, 8], [-2048, 8]], 2048 * (15 - 8 * k), 0)
+    iota(f("KC", 2, 64), [[1, 8], [0, 8]], 0, 0)
+    if any(hi - lo < H for lo, hi in PARTS):
+        iota(f("KC", 3, 64), [[0, 4], [-2048, 16]], 2048 * 15, 0)
+    now[1] = 0
+    for c in range(16):
+        act(f("DG", c, 16), v("DGm"), AF.Copy, scale=f("LL", c, 1))
+    for k in range(3):
+        act(f("OWN", k, 768), f("FT", k, 768), AF.Copy, scale=0.0)
+    for t in range(RO):
+        act(f("TG", t), v("ONEB"), AF.Copy, scale=t + 1.0)
+    for k in range(8):
+        iota(f("PI", k, 256), [[1, 256]], 256 * k, 0)
 
     def entries(o, x, tmp, bank):
         ts(tmp, x, -1024.5, OP.add, 2048.0 * BIG, OP.add)
         act(bank, tmp, bias=2048.0 - MID - 2048.0 * BIG)
         tt(o, x, bank, OP.add)
+    now[1] = 2
     for h in range(2):
         entries(v("Oa", 16 + H * h, 16 + H * h + H), f("ENT", h, 1024, 0, 8), f("n1", h), f("pA", h))
+    now[1] = 0
     for k in range(4):
-        entries(f("Xp", k, 512), f("ENT", k, 512), f("W1", k, 512), v(("pW", "pD", "pS0", "pS1")[k]))
+        entries(f("Xp", k, 512), f("ENT", k, 512), f("W1", k, 512), v(("pW", "pD", "pZ", "pD")[k]))
 
     def number(o, x, tmp, bank):
         act(tmp, x, scale=2.0 ** -12, bias=BIG)
         act(bank, tmp, scale=2048.0, bias=-2048.0 * BIG - MID / 2)
         tt(o, x, bank, OP.subtract)
+
+    def settle(t, plane, lo, hi):
+        cur, bank = v(plane, 8 * lo + t, 8 * hi, 8), v("pD", L + lo, L + hi)
+        act(bank, cur, scale=-2.0, bias=OUT)
+        tt(bank, v("Ln%d" % t, lo, hi), bank, OP.min)
+        tt(cur, cur, bank, OP.max)
+
+    for t in range(RO):
+        clock = C0 + t
+        now[0] = t
+        thr = clock - 5
+        last = t == RO - 1
+        plane = "Ip" if last else "Xp"
+        d = 1 + t % 3
+        to, frm = cores[(rank + d) % 4], cores[(rank - d) % 4]
+
+        now[1] = 2 * (t in FIRST)
+        for k, (lo, hi) in enumerate(AMSG):
+            if t:
+                act(v("Oa", 16 + lo, 16 + hi), v("Xp", 8 * lo + t, 8 * hi, 8), AF.Copy)
+            send("a", t, k, 16 + lo if lo else 0, 16 + hi, to, frm)
+        for lo, hi in IDX:
+            lanes = v("Xp", 8 * lo + t, 8 * hi, 8) if t else v("Oa", 16 + lo, 16 + hi)
+            ts(v("s1", lo, hi), lanes if t else v("ENT", 8 * lo, 8 * hi, 8), -1.0, OP.add)
+            act(v("n1", lo, hi), lanes, scale=2.0 ** -12, bias=BIG)
+            act(v("pU", lo, hi), v("n1", lo, hi), scale=2.0 ** -9, bias=(2063 - BIG) / 512)
+            ts(v("kd", lo, hi), v("s1", lo, hi), 16, OP.bitwise_and)
+            tt(v("wi", lo, hi), v("pU", lo, hi), v("kd", lo, hi), OP.subtract)
+            ts(v("idx", lo, hi), v("wi", lo, hi), 512.0, OP.mult, 0.0, OP.max)
+        for p, (lo, hi) in enumerate(PARTS):
+            c0, c1 = lo // 16, hi // 16
+            for q in range(lo // 32, hi // 32):
+                o, win = f("GF", q, 512), at(v("FT"), f("idx", q, 32))
+                if q in VG:
+                    tc(o, win)
+                else:
+                    act(o, win, AF.Copy)
+                scan(f("YS", q, 512), v("MB"), o)
+            u = v("pS%d" % (p % 2), 448 + c0, 448 + c1)
+            for x in range(16):
+                mm(u, f("WX", x), v("YS", 16 * lo + 16 * x + 15, 16 * hi, 256), x == 0, x == 15)
+            um, s5 = v("Ou", 16 * p, 16 * p + c1 - c0), v("Ou", 16 * p + 8, 16 * p + 8 + c1 - c0)
+            if LATE[p]:
+                tc(um, u)
+            else:
+                tc(v("ui", c0, c1), u)
+                ts(um, v("ui", c0, c1), 4095, OP.bitwise_and)
+                tt(v("sq", c0, c1), um, um, OP.mult)
+                ts(s5, v("sq", c0, c1), 5, OP.arith_shift_right)
+            send("u", t, p, 16 * p, 16 * p + (8 if LATE[p] else 16), to, frm)
+            now[1] = 0
+        if t:
+            for lo, hi in NMSG:
+                settle(t - 1, "Xp", lo, hi)
+        if last:
+            for k in range(4):
+                number(f("Ip", k, 512), f("Xp", k, 512), f("W1", k, 512), v("pS1" if k % 2 else "pD"))
+
+        def side(b, lo, hi, s):
+            return v(b, 2 * lo + s * (hi - lo), 2 * lo + (s + 1) * (hi - lo))
+
+        for n in sorted({hi - lo for lo, hi in PARTS}):
+            act(v("KK%d" % n), at(v("La%d" % t, 0, 16), v("RK%d" % n)), AF.Copy)
+        for p, (lo, hi) in enumerate(PARTS):
+            a, c1, l1 = v("La%d" % t, 16 + lo, 16 + hi), v("c1", lo, hi), v("l1", lo, hi)
+            act(c1, a, scale=1 / 16, bias=7.5 / 16)
+            act(c1, c1, bias=BIG)
+            act(c1, c1, bias=-BIG)
+            if VD[p]:
+                act(v("OR", 4 * lo, 4 * hi), at(c1, v("RC", 0, (hi - lo) // 4)), scale=16.0, bias=-7.5)
+        for lo, hi in MP:
+            a, l1 = v("La%d" % t, 16 + lo, 16 + hi), v("l1", lo, hi)
+            p0, p1, lam, keep = side("pW", lo, hi, 0), side("pW", lo, hi, 1), side("LAM", lo, hi, 0), v("KP", lo, hi)
+            act(p1, v("CC", 8 * lo + t, 8 * hi, 8), AF.Copy)
+            tt(v("sia", lo, hi), a, p1, OP.add)
+            ts(v("za", lo, hi), v("sia", lo, hi), 7 << 15, OP.bitwise_and)
+            if FASTA[lo // H]:
+                ts(v("loa", lo, hi), v("sia", lo, hi), 31, OP.bitwise_and)
+                ts(p1, v("loa", lo, hi), thr, OP.is_ge, 262144.0, OP.mult)
+                ts(lam, v("loa", lo, hi), -15.0, OP.add)
+            else:
+                act(l1, a, scale=1 / 32, bias=-0.5 / 32)
+                act(l1, l1, bias=BIG)
+                act(p0, l1, scale=32.0, bias=-32.0 * BIG)
+                tt(lam, a, p0, OP.subtract)
+                act(p1, lam, AF.Relu, scale=262144.0, bias=262144.0 * (16 - thr))
+            tt(keep, v("za", lo, hi), p1, OP.is_le)
+            a1, a1N, one = v("pA", lo, hi), v("pA", L + lo, L + hi), v("ONEB", 0, hi - lo)
+            total(a1, [(-MID, one), (2.0 ** 25, keep)])
+            tt(a1, a, a1, OP.min)
+            act(a1N, a1, bias=MID)
+            if last:
+                number(v("anum", lo, hi), a, v("an1", lo, hi), p0)
+                total(a1, [(2.0 ** 25, keep)])
+                tt(a1, v("anum", lo, hi), a1, OP.min)
+            act(side("SIG", lo, hi, 0), lam, AF.Sign, bias=15.5 - thr)
+            act(side("IOT", lo, hi, 1), lam, AF.Sign, bias=-0.5)
+            act(side("EM0", lo, hi, 0), a, AF.Relu, scale=-1.0, bias=1.0 - MID)
+
+        for p, (lo, hi) in enumerate(PARTS):
+            bank, n, c0, c1 = "pS%d" % (p % 2), hi - lo, lo // 16, hi // 16
+
+            def r(b, o=0, st=1):
+                return v(b, lo + o, hi, st)
+            um, s5 = at(f("Lu%d" % t, 2 * p, 8), v("RU%d" % n)), at(f("Lu%d" % t, 2 * p + 1, 8), v("RU%d" % n))
+            if LATE[p]:
+                ts(r("U1"), um, 4095, OP.bitwise_and)
+                um, s5 = r("U1"), r("U3")
+                tt(r("U2"), um, um, OP.mult)
+                ts(s5, r("U2"), 5, OP.arith_shift_right)
+            tt(r("E1"), um, v("KK%d" % n), OP.mult)
+            e1 = r("E1")
+            if t:
+                e1 = v("pZ", 2 * lo, lo + hi) if LATE[p] else e1
+                act(e1, r("E1"), bias=v("LA%d" % (t - 1), 0, 1))
+            tt(r("E2"), s5, e1, OP.add)
+            ts(r("E3"), r("E2"), 2047, OP.bitwise_and)
+            tc(r("EL"), r("E3"))
+            tc(r("E16"), r("E3"))
+            rows = (0, 8) if n == H else (4 * (p % 2), 4 * (p % 2) + 4)
+            if len(VD[p]) < 4:
+                for m in range(4):
+                    act(w("pO", rows, m), r("c1"), scale=16.0, bias=-7.5)
+            step = 512 // (4 * n)
+            for q in range(4):
+                a = 16 * lo + 4 * n * q
+                if q not in VD[p] and (q % step == 0 or q - 1 in VD[p]):
+                    k = step - q % step
+                    act(v("GS", a, a + 4 * n * k), at(v("Xp"), v("EL", lo + n * q // 4, lo + n * (q + k) // 4)), AF.Copy)
+            for k in range(n // 64):
+                g0, gm = 1024 // n * k, 1024 // n
+                for q in range(g0 // 4, (g0 + gm) // 4):
+                    a, ms = 16 * lo + 4 * n * q, (4 * q, 4 * q + 4)
+                    o = v("D", a, a + 4 * n)
+                    if q in VD[p]:
+                        tt(o, at(v("Xp"), v("EL", lo + n * q // 4, lo + n * (q + 1) // 4)), v("OR", 4 * lo, 4 * hi), OP.subtract)
+                    else:
+                        tt(o, v("GS", a, a + 4 * n), w("pO", rows), OP.subtract)
+                    ts(w("Q1", (c0, c1), ms), o, 4096.0 * (BIG + 1), OP.add, 4096.0 * (BIG + 1), OP.is_equal)
+                    if (p, k) in Q2S:
+                        act(v("AB", a, a + 4 * n), o, AF.Abs)
+                        act(w("Q2", (c0, c1), ms), v("AB", a, a + 4 * n), AF.Sign, bias=-8.25)
+                    else:
+                        ts(w("Q2", (c0, c1), ms), o, 16.0 * BIG, OP.add, 16.0 * BIG, OP.not_equal)
+                key = f(bank, k, 64)
+                mm(key, diag(1.0), f("KC", k if n == H else 3, 64), True, False)
+                if n == H:
+                    mm(key, diag(2.0 ** 21), f("KC", 2, 64), False, False)
+                for m in range(g0, g0 + gm):
+                    a = lo + n // 4 * (m // 4)
+                    mm(f(bank, k, 64, m - g0, gm), v("IDH"), v("E16", a + m % 4, a + n // 4, 4), False, False)
+                if (p, k) in Q2S:
+                    mm(key, diag(2.0 ** 18), v("ONEB", 0, 64), False, False)
+                for Q in ("Q1", "Q2"):
+                    for x in range(16):
+                        mm(key, f("SH" if Q == "Q2" and (p, k) in Q2S else "SC", x), w(Q, (c0, c1), (g0, g0 + gm), x), False, Q == "Q2" and x == 15)
+                if n == H and k == 0:
+                    act(f("k0", p, 64), key, AF.Copy)
+            if n == H:
+                scan(f("k4", p, 64), f("k0", p, 64), f(bank, 1, 64), OP.max)
+            else:
+                scan(f("k4", p, 64), v("MK", 0, 64), f(bank, 0, 64))
+            ts(v("k5", c0, c1), f("k4", p, 64, gm - 1, gm), 2047, OP.bitwise_and)
+            if hi not in [b for a, b in MP]:
+                continue
+            p = [b for a, b in MP].index(hi)
+            lo = MP[p][0]
+            bank, n, c0 = "pS%d" % (p % 2), hi - lo, lo // 16
+            pl = v("pl", c0, c1)
+            tc(pl, v("k5", c0, c1))
+            tc(v("P1", c0, c1), v("k5", c0, c1))
+            tc(r("PB"), at(v("PI"), pl))
+            act(r("CP"), at(v("CC"), pl), AF.Copy)
+            act(r("bN"), at(v("Xp"), pl), bias=MID)
+            tt(r("sib"), at(v("Xp"), pl), r("CP"), OP.add)
+            if last:
+                act(r("bnum"), at(v("Ip"), pl), AF.Copy)
+            if p:
+                act(r("ow"), at(v("OWN"), pl), AF.Relu, bias=-float(t))
+            mine = [c for c in range(c0, c1) if c in EQS]
+            if mine:
+                act(v("PBf", 16 * mine[0], hi), at(v("PI"), v("pl", mine[0], c1)), AF.Copy)
+            for c in range(c0, c1):
+                eq = w("EQ", c, (0, hi - 16 * c))
+                if c in mine:
+                    act(eq, v("PBf", 16 * c, hi), AF.Abs, scale=-1.0, bias=f("P1", c, 1))
+                    act(eq, eq, AF.Relu, scale=-1.0, bias=1.0)
+                else:
+                    ts(eq, v("PB", 16 * c, hi), f("P1", c, 1), OP.is_equal)
+            tt(r("EQd"), w("EQ", (c0, c1), (0, 16)), v("pU", 384, 384 + n), OP.mult)
+            cnt = r("pD")
+            mm(cnt, v("IDH"), r("PB"), True, False)
+            for c in range(c0, c1 - 1):
+                mm(v("pD", 16 * c + 16, hi), v("BDk"), w("EQ", c, (16, hi - 16 * c)), False, False)
+            if p:
+                mm(cnt, v("BDk"), r("ow"), False, False)
+            mm(cnt, v("BDk"), r("EQd"), False, True)
+            tt(r("wd"), cnt, r("DG"), OP.min)
+            act(r("lose"), cnt, AF.Sign, bias=-2047.5, accum=f("lc", p, 1))
+            scan(r("sc"), v("MK", 0, n), r("wd"))
+            tc(v("PL", c0, c1), r("sc", 15, 16))
+            if hi < L:
+                tc(at(v("OWN"), v("PL", c0, c1)), v("TG", H * t, H * t + n))
+            lam, keep = side("LAM", lo, hi, 1), v(bank, 2 * H, 2 * H + n)
+            ts(r("zb"), r("sib"), 7 << 15, OP.bitwise_and)
+            if FAST[p]:
+                ts(r("lob"), r("sib"), 31, OP.bitwise_and)
+                ts(keep, r("lob"), thr, OP.is_ge, 262144.0, OP.mult)
+                ts(lam, r("lob"), -15.0, OP.add)
+            else:
+                act(r("l1b"), at(v("Xp"), pl), scale=1 / 32, bias=-0.5 / 32)
+                act(r("l1b"), r("l1b"), bias=BIG)
+                act(v(bank, H, H + n), r("l1b"), scale=32.0, bias=MID - 32.0 * BIG)
+                tt(lam, r("bN"), v(bank, H, H + n), OP.subtract)
+                act(keep, lam, AF.Relu, scale=262144.0, bias=262144.0 * (16 - thr))
+            tt(keep, r("zb"), keep, OP.is_le)
+            tt(r("b1"), r("bN"), keep, OP.mult)
+            if last:
+                tt(r("b1c"), r("bnum"), keep, OP.mult)
+            else:
+                act(r("b1c"), r("b1"), bias=-MID)
+            act(side("SIG", lo, hi, 1), lam, AF.Sign, bias=15.5 - thr)
+            act(side("IOT", lo, hi, 0), lam, AF.Sign, bias=-0.5)
+            act(side("EM0", lo, hi, 1), r("bN"), AF.Relu, scale=-1.0, bias=1.0)
+            act(r("EM"), r("b1"), AF.Relu, scale=-1.0, bias=1.0)
+            tt(r("d0"), r("b1"), v("pA", L + lo, L + hi), OP.subtract)
+            if SAME[p]:
+                act(r("d0"), r("d0"), AF.Abs)
+                act(r("same"), r("d0"), AF.Sign, scale=-1.0, bias=2048.0)
+            else:
+                ts(r("same"), r("d0"), 4096.0 * BIG, OP.add, 4096.0 * BIG, OP.is_equal)
+            oa, ob = side("pW", lo, hi, 0), side("pW", lo, hi, 1)
+            for k, (c, b) in enumerate(((-1.0, "LAM"), (-16.0, "SIG"), (8.0, "IOT"))):
+                mm(v("pW", 2 * lo, 2 * hi), diag(c), v(b, 2 * lo, 2 * hi), k == 0, k == 2 and not last)
+            if last:
+                mm(oa, diag(16.0), r("KP"), False, False)
+                mm(ob, diag(-16.0), r("EM"), False, True)
+            act(r("oa"), oa, AF.Relu, bias=clock - 39.0 - 16 * last)
+            act(ob, ob, AF.Relu, bias=clock - 39.0)
+            tt(r("ah"), r("oa"), r("pA"), OP.add)
+            tt(ob, r("b1c"), ob, OP.add)
+            tt(r("big"), r("ah"), ob, OP.max)
+            zz, zk, one = side("pZ", lo, hi, 0), side("pZ", lo, hi, 1), v("ONEB", 0, n)
+            total(zz, [(-2.0 ** 26 if SAME[p] else -7.0 * 2 ** 24, one), (2.0 ** 25, side("EM0", lo, hi, 0)), (2.0 ** 24, side("SIG", lo, hi, 0)), (-2.0 ** 26, r("KP")),
+                       (-2.0 ** 25, side("EM0", lo, hi, 1)), (2.0 ** 24, side("SIG", lo, hi, 1)), (2.0 ** 26, r("EM")),
+                       (3.0 * 2 ** (24 if SAME[p] else 25), r("same")), (-2.0 ** 27, r("lose"))])
+            tt(r("TT"), r("big"), zz, OP.min)
+            total(zk, [(2.0 ** (24 if last else 23), one), (2.0 ** 25, r("KP")), (2.0 ** 24, r("lose"))])
+            tt(zk, r("anum") if last else v("La%d" % t, 16 + lo, 16 + hi), zk, OP.min)
+            tt(r("On"), r("TT"), zk, OP.max)
+        for k, (lo, hi) in enumerate(NLAST if last else NMSG):
+            send("n", t, k, lo, hi, frm, to)
+        mine = v(plane, t, S, 8)
+        asel(mine, mine, [[0, L]], OP.is_gt, 0, 0, OUT)
+        for lo, hi in MP:
+            tt(at(v(plane), v("PL", lo // 16, hi // 16)), v("b1c", lo, hi), v("TT", lo, hi), OP.max)
+        if not last:
+            col = v("pU", 300, 301)
+            for p in range(len(MP)):
+                mm(col, v("SEL0"), f("lc", p, 1), p == 0, p == len(MP) - 1)
+            act(v("an"), col, AF.Copy, scale=-0.5)
+            act(v("aq"), v("an"), scale=1 / 32, bias=-15.5 / 32)
+            act(v("aq"), v("aq"), bias=BIG)
+            act(v("aq"), v("aq"), bias=-BIG)
+            act(v("OA", 0, 1), v("aq"), scale=-32.0, bias=v("an"))
+            dn = 1 + (t + 1) % 3
+            send("A", t, 0, 0, 4, cores[(rank - d + dn) % 4], cores[(rank - dn + d) % 4])
+
+    for k, (lo, hi) in enumerate(NLAST):
+        settle(RO - 1, "Ip", lo, hi)
+        o = v("Ip", 8 * lo, 8 * hi)
+        run("Y", lambda e, o=o, lo=lo, hi=hi: e.dma_start(T.yent[:, 8 * lo:8 * hi], o[0]), o[1], [("yent", 8 * lo, 8 * hi)], 0.1, "dY%d" % k, 16, 2.0 + (hi - lo) / 80)
+    issue()
+    return
 
     def settle(t, plane, h):
         cur, bank, new = f(plane, h, 1024, t, 8), f("pD", 2 + h), f("Ln%d" % t, h)

import numpy as np
from concourse.mybir import AluOpType as OP, ActivationFunctionType as AF

L, H, S, NM, RO, C0 = 256, 128, 2048, 4096, 4, 12
SW_ = S + L
VG = (0, 2)
SG = ((1, 2, 3), (0, 1, 2, 3))
EQS, SAME = (), (0, 0)
PARTS = MP = AMSG = NMSG = IDX = ((0, 128), (128, 256))
VD, FAST, LATE, Q2S = ((0,), (), (), ()), (0, 1), (1, 0, 0), ()
CY, WAKE, HOP, RATE, FX, GAT, SCA = 0.00083, 0.23, 1.7, 60e3, 0.0, 1.5, 3.6
PASSES, NOISE, WIN, PEC = 2000, 2.0, 1.5, 0.00055
SPANS, DBG, SLACK, MEAN = [], [], 0.1, 0.3
FASTA, FIRST = (1, 1), (0,)
LOADS, HALF = (0, "F", 1), 1.4
NLAST = ((0, 128), (128, 192), (192, 256))
ORDER = []

BIG, MID, OUT = 12582912.0, 8388608.0, -33554432.0
F32, BF, I32, U16, F16 = "float32", "bfloat16", "int32", "uint16", "float16"
WEIGHTS = {BF: [1.0, -1.0, -16.0, 8.0, 16.0, 2.0 ** 21, 2.0 ** 23, -2.0 ** 23, 2.0 ** 24, 2.0 ** 25, -2.0 ** 25, 2.0 ** 26, -2.0 ** 26,
                -2.0 ** 27, -7.0 * 2 ** 24, 3.0 * 2 ** 25],
           F32: [1.0, -1.0, -32.0]}
SCRATCH = {}
PART = {}
for _buf, _d, _parts in (
        ("KI", I32, (("c64 c64b", 64), ("j4", 32), ("jj j1 j2 j3", 8), ("pidx pm", 1))),
        ("KF", F32, (("DG", L), ("xp", H), ("P1 DGm LL l16", 16), ("wtF kapF pmF p0 an aq", 1), ("lc", 4))),
        ("TI", I32, (("s1 kd E2 E3 k4 sia za sib zb loa lob U1 U2 U3", L), ("ui sq s5 k5", 16))),
        ("TF", F32, (("n1 wi E1 c1 l1 an1 anum CP bN l1b b1 b1c bnum d0 ah big TT wd sc k0 PBf", L), ("KK128", H), ("KK64", 64))),
        ("TB", BF, (("same lose ow EQd oa KP EM", L), ("ONEB BDk", H), ("KC", 256), ("KD", 16), ("TG", 4 * H))),
        ("TH", F16, (("E16 PB", L), ("IDH", H))),
        ("TU", U16, (("idx EL", L), ("pl PL", 16), ("RU128 RK128", 8), ("RU64 RK64", 4), ("RC", 32)))):
    _o = 0
    for _names, _w in _parts:
        for _n in _names.split():
            PART[_n] = (_buf, _o, _w)
            _o += _w
    SCRATCH[_buf] = ("sbuf", [128, _o], _d)
for _names, _w, _d in (
        ("ENT", S, I32), ("Xp Ip", SW_, F32), ("OWN", SW_, BF), ("FT", NM + 16, BF), ("PI CC W1", S, F32), ("GS", 4096, F32),
        ("wtS kapS", 1, I32), ("ones B0 B1 ID SEL0 MK", 128, F32), ("SC SH WX", 2048, BF), ("GF YS D AB", 4096, BF), ("MB", 512, BF),
        ("OR", 1024, F32), ("LAM SIG IOT EM0", 2 * L, BF)):
    for _n in _names.split():
        SCRATCH[_n] = ("sbuf", [128, _w], _d)
for _n in "Q1 Q2".split():
    SCRATCH[_n] = ("sbuf", [128, 16, 16, 16], BF)
SCRATCH["EQ"] = ("sbuf", [128, 16, H], BF)
for _d in WEIGHTS:
    SCRATCH["W" + _d] = ("sbuf", [128, len(WEIGHTS[_d]), 128], _d)
for _n in "pU pA pW pZ pD pS0 pS1".split():
    SCRATCH[_n] = ("psum", [128, 512], F32)
SCRATCH["pO"] = ("psum", [128, 8, 4, 16], F32)
SEMAPHORES = ["sV", "sS", "sT", "sG", "dE0", "dE1", "dF", "dW", "dK", "dY0", "dY1", "dY2", "dY3"]
for _n, _w, _d in (("a", 16 + L, F32), ("u", 64, I32), ("n", L, F32), ("A", 4, F32)):
    SCRATCH["O" + _n] = ("sbuf", [128, _w], _d)
    for _t in range(RO - (_n == "A")):
        SCRATCH["L%s%d" % (_n, _t)] = ("sbuf", [128, _w], _d)
        for _h in range(1 if _n == "A" else 4):
            SEMAPHORES += ["r%s%d%d" % (_n, _t, _h), "l%s%d%d" % (_n, _t, _h)]


def is_psum(b):
    return b in SCRATCH and SCRATCH[b][0] == "psum"


def make_tools(g, T):
    queue = {"V": g.vector, "S": g.scalar, "T": g.tensor, "G": g, "Y": g.sync}
    qsem = {"V": "sV", "S": "sS", "T": "sT", "G": "sG"}
    nodes = []
    log, seen = {}, {}
    lastmm = {}
    kin, kinds, count = [], {}, {}
    now, early = [-1, 3], []

    def touch(i, rg, wr):
        q, deps = nodes[i][0], nodes[i][6]
        for (b, lo, hi) in rg:
            if is_psum(b):
                nodes[i][7].add(b)
                if q == "T":
                    if lastmm.get(b, i) != i:
                        deps[lastmm[b]] = deps.get(lastmm[b], False)
                    lastmm[b] = i
            for (l0, h0, j) in log.get(b, []) + (seen.get(b, []) if wr else []):
                if j != i and l0 < hi and lo < h0 and not (q == "T" and nodes[j][0] == "T"):
                    deps[j] = True

    def note(i, rg, wr):
        for (b, lo, hi) in rg:
            if wr:
                for d in (log, seen):
                    d[b] = [e for e in d.get(b, []) if not (lo <= e[0] and e[1] <= hi)]
            (log if wr else seen).setdefault(b, []).append((lo, hi, i))

    def run(q, fn, reads, writes, cost, sem=None, inc=1, lat=0.0, behind=None):
        nodes.append([q, fn, sem if sem else qsem[q], inc, cost, lat, {} if behind is None else {behind: False}, set()])
        i = len(nodes) - 1
        if now[1]:
            early.append((i, now[1]))
        name = (q, cost, tuple((b[:2], lo // 8, hi // 8) for b, lo, hi in writes[:1] + reads[:1]))
        count[name, now[0]] = count.get((name, now[0]), 0) + 1
        kin.append(kinds.setdefault((name, count[name, now[0]]), len(kinds)))
        touch(i, reads, False)
        touch(i, writes, True)
        note(i, reads, False)
        note(i, writes, True)
        return i

    def landed(rg, s, val, after, cost):
        nodes.append([None, None, s, val, cost, 0.0, {after: True}, set()])
        kin.append(kin[after])
        note(len(nodes) - 1, rg, True)

    def plan():
        n = len(nodes)
        before = [[(j, nodes[j][5] + (WAKE if nd[0] else 0.0) if w else 0.0) for j, w in nd[6].items()] for nd in nodes]
        after = [[] for _ in range(n)]
        for i in range(n):
            for j, d in before[i]:
                after[j].append((i, d))
        lat = [nd[5] for nd in nodes]
        way = [0.0] * n
        for i in range(n - 1, -1, -1):
            way[i] = nodes[i][4] + max([way[k] + d for k, d in after[i]] + [lat[i]])

        SPANS.append(max(way))
        DBG[:] = [nodes, after, way, kinds, kin]

        def first(lst, s):
            lo, hi = 0, len(lst)
            while lo < hi:
                m = (lo + hi) // 2
                if lst[m][1] <= s:
                    lo = m + 1
                else:
                    hi = m
            return lo

        def place(key, pre, post, tail):
            key = list(key)
            if pre is before:
                for i, k in early:
                    key[i] = -way[i] - 1000.0 * k
            for i in (range(n) if pre is before else range(n - 1, -1, -1)):
                for j, d in pre[i]:
                    if key[i] <= key[j]:
                        key[i] = key[j] + 1e-7
            at, end, why = list(tail), [0.0] * n, [(-1, False)] * n
            taken = {x: [] for x in places}
            for i in sorted(range(n), key=lambda k: key[k]):
                q, c, s, t = nodes[i][0], nodes[i][4], at[i], -1.0
                lists = [taken[x] for x in uses[i]]
                while s > t:
                    t = s
                    for lst in lists:
                        if lst and lst[-1][1] > s - WAKE:
                            k = first(lst, s - WAKE)
                            while k < len(lst) and lst[k][0] < s + c + WAKE:
                                pad = 0.0 if lst[k][2] == q else WAKE
                                if lst[k][0] < s + c + pad - 1e-9 and lst[k][1] + pad > s + 1e-9:
                                    s = lst[k][1] + pad
                                    why[i] = (lst[k][3], True)
                                k += 1
                for lst in lists:
                    if not lst or lst[-1][0] <= s:
                        lst.append((s, s + c, q, i))
                    else:
                        lst.insert(first(lst, s + 1e-9), (s, s + c, q, i))
                end[i] = s + c
                for k, d in post[i]:
                    if end[i] + d > at[k]:
                        at[k] = end[i] + d
                        why[k] = (i, False)
            return end, why
        uses = [[nd[0]] + sorted(nd[7]) for nd in nodes]
        places = {x for u in uses for x in u}
        like = {}
        for i in range(n):
            like.setdefault(kin[i], []).append(i)
        rng = np.random.default_rng(1)
        key, best, cur = [-x for x in way], None, None
        for p in range(PASSES):
            end, why = place(key, before, after, [0.0] * n)
            span = max(e + d for e, d in zip(end, lat)) + MEAN * sum(end) / n
            if cur is None or span <= cur[0] + SLACK * (1 - p / PASSES) * rng.random():
                cur = (span, end, why)
            if best is None or span <= best[0]:
                best = (span, end)
            SPANS.append(round(span, 1))
            key = [e - nd[4] for e, nd in zip(cur[1], nodes)]
            if p < 3 or p % 16 == 0:
                key = [-x for x in place([-x for x in cur[1]], after, before, lat)[0]]
            elif p % 4 == 0:
                mids = [cur[1][i] for i in like[kin[int(n * rng.random())]]]
                x = NOISE * rng.random() * (rng.random(n) - 0.5)
                key = [e + (x[k] if min(abs(e - m) for m in mids) < WIN else 0.0) for e, k in zip(key, kin)]
            else:
                i, held = max(range(n), key=lambda k: cur[1][k] + lat[k]), []
                while i >= 0:
                    j, by = cur[2][i]
                    if by:
                        held.append((i, j))
                    i = j
                i, j = held[int(len(held) * rng.random())]
                back = key[i] - key[j] + 1e-3 + rng.random() ** 2
                pull = rng.random() < 0.6
                for k in (like[kin[i if pull else j]] if rng.random() < 0.7 else [i if pull else j]):
                    key[k] += -back if pull else back
                if pull:
                    for k in range(n - 1, -1, -1):
                        for j, d in before[k]:
                            if key[j] >= key[k]:
                                key[j] = key[k] - 1e-7
        return sorted((i for i in range(n) if nodes[i][0]), key=lambda i: (best[1][i] - nodes[i][4], i))

    def issue():
        total, val, know, known = {}, {}, {}, {q: {} for q in queue}
        for i, nd in enumerate(nodes):
            if nd[0] is None:
                total[nd[2]] = total.get(nd[2], 0) + nd[3]
                val[i], know[i] = total[nd[2]], {}
        if not ORDER:
            ORDER.extend(plan())
        turn = {}
        for i in ORDER:
            q, fn, s, inc = nodes[i][:4]
            for b in nodes[i][7]:
                for p, j in turn.setdefault(b, {}).items():
                    if p != q:
                        nodes[i][6][j] = True
                turn[b][q] = i
            deps = [j for j, w in nodes[i][6].items() if w]
            best = {}
            for j in deps:
                sj = nodes[j][2]
                if known[q].get(sj, 0) < val[j]:
                    best[sj] = max(best.get(sj, 0), val[j])
            for j in deps:
                for sk, vk in know[j].items():
                    if best.get(nodes[j][2]) == val[j] and sk in best and sk != nodes[j][2] and best[sk] <= vk:
                        del best[sk]
            for sk, vk in best.items():
                queue[q].wait_ge(T.sem[sk], vk)
                known[q][sk] = max(known[q].get(sk, 0), vk)
            for j in deps:
                for sk, vk in know[j].items():
                    known[q][sk] = max(known[q].get(sk, 0), vk)
            total[s] = total.get(s, 0) + inc
            val[i] = total[s]
            ins = fn(queue[q])
            if ins is not None:
                ins.then_inc(T.sem[s], inc)
            know[i] = dict(known[q])
        for s, x in total.items():
            if known["G"].get(s, 0) < x:
                g.wait_ge(T.sem[s], x)
    return run, landed, issue, now


def rank_program(g, core, T, topo):
    rank = T.rank_of(core)
    if rank is None:
        return
    run, landed, issue, now = make_tools(g, T)
    cores = list(T.cores)

    def size(b):
        n = 1
        for d in SCRATCH[b][1][1:]:
            n *= d
        return n

    def v(b, lo=0, hi=None, st=1):
        if b in PART:
            b, o, w = PART[b]
            lo, hi = o + lo, o + (w if hi is None else hi)
        hi = size(b) if hi is None else hi
        rg = [(b, lo, hi)] if st <= 16 else [(b, k, k + 1) for k in range(lo, hi, st)]
        return (T[b][:, lo:hi] if st == 1 else T[b][:, lo:hi:st], rg, len(range(lo, hi, st)))

    def f(b, h, n=H, o=0, st=1):
        return v(b, n * h + o, n * h + n, st)

    def w(b, *ix):
        ix = tuple(slice(*k) if isinstance(k, tuple) else k for k in ix)
        flat = np.arange(size(b)).reshape(SCRATCH[b][1][1:])[ix].reshape(-1)
        cut = [0] + [int(k) + 1 for k in np.nonzero(np.diff(flat) > 16)[0]] + [len(flat)]
        return (T[b][(slice(None),) + ix], [(b, int(flat[a]), int(flat[z - 1]) + 1) for a, z in zip(cut, cut[1:])], len(flat))

    def at(win, o):
        return (win[0].indirect(o[0]), win[1] + o[1], 16 * o[2], True)

    def isv(x):
        return isinstance(x, tuple)

    def regs(*xs):
        out = []
        for x in xs:
            if isv(x):
                out += x[1]
        return out

    def ap(x):
        return x[0] if isv(x) else x

    def dtype(x):
        return SCRATCH[x[1][0][0]][2]

    def wide(*xs):
        return any(dtype(x) in (F32, I32) for x in xs)

    def vec(fn, o, ins, k):
        if len(o) > 3:
            run("V", fn, regs(*ins) + o[1][1:], o[1][:1], 0.05 + SCA * o[2] * CY)
        elif len(ins[0]) > 3:
            run("V", fn, regs(*ins), regs(o), 0.05 + GAT * o[2] * CY)
        else:
            run("V", fn, regs(*ins), regs(o), FX + max(64, o[2] * k) * CY)

    def ts(o, a, s1, op0, s2=None, op1=None):
        if op1 is None:
            fn = lambda e: e.tensor_scalar(out=o[0], in0=a[0], scalar1=ap(s1), scalar2=None, op0=op0)
        else:
            fn = lambda e: e.tensor_scalar(out=o[0], in0=a[0], scalar1=ap(s1), scalar2=ap(s2), op0=op0, op1=op1)
        vec(fn, o, [a, s1, s2], 1.0 if wide(o, a) else 0.5)

    def tt(o, a, b, op):
        vec(lambda e: e.tensor_tensor(out=o[0], in0=a[0], in1=b[0], op=op), o, [a, b], 1.0 if any(is_psum(x[1][0][0]) for x in (a, b)) else 2.0)

    def tc(o, a):
        vec(lambda e: e.tensor_copy(out=o[0], in_=a[0]), o, [a], 1.0 if wide(o, a) else 0.5)

    def fill(o, c):
        run("V", lambda e: e.memset(o[0], c), [], regs(o), FX + o[2] * CY * (1.0 if wide(o) else 0.5))

    def scan(o, m, a, op=OP.mult):
        vec(lambda e: e.tensor_tensor_scan(out=o[0], data0=m[0], data1=a[0], initial=0.0, op0=op, op1=OP.max), o, [m, a], 1.0 if wide(o, m, a) else 0.5)

    def act(o, a, func=AF.Identity, scale=1.0, bias=0.0, accum=None):
        b0, s0 = ap(bias), ap(scale)
        if accum is None:
            fn = lambda e: e.activation(out=o[0], in_=a[0], func=func, bias=b0, scale=s0)
        else:
            fn = lambda e: e.activation(out=o[0], in_=a[0], func=func, bias=b0, scale=s0, accum_out=accum[0])
        run("S", fn, regs(a, bias, scale), regs(o, accum), 0.065 + o[2] * GAT * CY if len(a) > 3 else FX + max(64, o[2]) * CY)

    def mm(o, lT, r, start, stop):
        k = 4.0 if dtype(lT) == F32 else 1.0
        run("T", lambda e: e.matmul(out=o[0], lhsT=lT[0], rhs=r[0], start=start, stop=stop), regs(lT, r), regs(o), PEC * k * max(64, o[2]))

    used = set()

    def diag(c, d=BF):
        k = WEIGHTS[d].index(c)
        if (k, d) not in used:
            used.add((k, d))
            act(w("W" + d, k), v("ID"), AF.Copy, scale=c)
        return w("W" + d, k)

    def total(o, terms):
        for k, (c, x) in enumerate(terms):
            mm(o, diag(c, dtype(x)), x, k == 0, k == len(terms) - 1)

    def iota(o, pattern, base, cm):
        if dtype(o) != I32:
            fn = lambda e: e.iota(o[0], pattern, base, cm, allow_small_or_imprecise_dtypes=True)
        else:
            fn = lambda e: e.iota(o[0], pattern, base, cm)
        run("G", fn, [], regs(o), 0.13 + 2 * o[2] * CY)

    def asel(o, a, pattern, cmp, base, cm, other=0.0):
        run("G", lambda e: e.affine_select(out=o[0], in_=a[0], pattern=pattern, compare_op=cmp, fill=other, base=base, channel_multiplier=cm), regs(a), regs(o), 0.17 + 2 * o[2] * CY)

    def send(kind, t, h, lo, hi, to, frm):
        rid, pid = topo.addr(to)[:2]
        m = topo.mask(core, to)
        src, dst, rs, ls = v("O" + kind, lo, hi), v("L%s%d" % (kind, t), lo, hi), "r%s%d%d" % (kind, t, h), "l%s%d%d" % (kind, t, h)

        def fn(e):
            e.remote_dma(out_ap=dst[0], in_ap=src[0], remote_sem=T.sem[rs], local_sem=T.sem[ls], pid=pid, routing_id=rid, dma_engine_mask=m)
        i = run("G", fn, src[1], [], max(0.1, 512 * (hi - lo) / RATE), sem=ls, inc=len(topo.engines(core, to)), lat=HOP)
        landed(dst[1], rs, len(topo.engines(frm, core)), i, 0.0)

    i = run("Y", lambda e: e.dma_start(T.kapS[:], T.kap[:]), [], regs(v("kapS")), 0.05, "dK", 16, 2.0)
    i = run("Y", lambda e: e.dma_start(T.wtS[:], T.wt[:]), [], regs(v("wtS")), 0.05, "dW", 16, 2.0, i)
    mb = 0
    for b in LOADS:
        mb += 2 if b == "F" else 1
        o, x = (v("FT", 16), T.feat[:]) if b == "F" else (f("ENT", b, 1024), T.ent[:, 1024 * b:1024 * b + 1024])
        i = run("Y", lambda e, o=o, x=x: e.dma_start(o[0], x), [], o[1], 0.05, "dF" if b == "F" else "dE%d" % b, 16, 2.0 + mb * HALF, i)

    fill(v("ones"), 1.0)
    fill(v("ONEB"), 1.0)
    fill(v("FT", 0, 16), 0.0)
    fill(v("SC"), 0.0)
    fill(v("WX"), 0.0)
    if Q2S:
        fill(v("SH"), 0.0)
    fill(v("MB"), 1.0)
    fill(v("MB", 0, 512, 16), 0.0)
    fill(v("OA"), 0.0)
    iota(v("pidx"), [[0, 1]], 0, 1)
    asel(v("B0"), v("ones"), [[-16, 8], [0, 16]], OP.is_ge, 0, 1)
    asel(v("B1"), v("B0"), [[16, 8], [0, 16]], OP.is_ge, 15, -1)
    asel(v("ID"), v("ones"), [[-1, 128]], OP.is_equal, 0, 1)
    iota(v("xp"), [[0, 8], [1, 16]], 0, 0)
    iota(v("jj"), [[16, 8]], 0, 0)
    iota(v("c64"), [[37, 64]], 0, 0)
    tc(v("wtF"), v("wtS"))
    tc(v("kapF"), v("kapS"))
    ts(v("pm"), v("pidx"), 15, OP.bitwise_and)
    tc(v("pmF"), v("pm"))
    ts(v("p0"), v("pmF"), 0.0, OP.is_equal)
    ts(v("SEL0"), v("ones"), v("p0"), OP.mult)
    for q in range(8):
        act(v("WX", 16 * q, 16 * q + 129 * 15 + 1, 129), f("B1", q, 16), AF.Copy, scale=v("wtF"))
        act(v("SC", 16 * q, 16 * q + 129 * 15 + 1, 129), f("B1", q, 16), AF.Copy, scale=32768.0)
        if Q2S:
            act(v("SH", 16 * q, 16 * q + 129 * 15 + 1, 129), f("B1", q, 16), AF.Copy, scale=16384.0)
    act(v("BDk"), v("B1"), AF.Copy, scale=4096.0)
    tc(v("IDH"), v("ID"))
    ts(v("DGm"), v("xp", 0, 16), v("pmF"), OP.is_equal)
    tri = v("pU", 384, 512)
    ts(tri, v("xp", 0, H), v("pmF"), OP.is_gt)
    ts(v("KD"), v("DGm", 0, 16), v("kapF"), OP.mult)
    mm(v("pZ", 0, 16), v("BDk"), v("KD"), True, True)
    act(v("Oa", 0, 16), v("pZ", 0, 16), AF.Copy, scale=2.0 ** -12)
    now[1] = 1
    ts(v("j1"), v("jj"), v("pmF"), OP.add)
    ts(v("j3"), v("j1"), 3, OP.bitwise_and)
    for n in sorted({hi - lo for lo, hi in PARTS}):
        j1, j2, j3 = [v(b, 0, n // 16) for b in ("j1", "j2", "j3")]
        ts(j2, j1, 2, OP.arith_shift_right, n // 16 - 1, OP.bitwise_and)
        tc(v("RU%d" % n), j2)
        ts(j2, j1, 1 + n // 64, OP.arith_shift_right, -4, OP.bitwise_and)
        tt(j2, j2, j3, OP.add)
        tc(v("RK%d" % n), j2)
    fill(v("Ou"), 0)
    iota(v("j4"), [[16, 8], [0, 4]], 0, 0)
    ts(v("RC"), v("j4"), v("pmF"), OP.add)
    ts(v("c64b"), v("c64"), 63, OP.bitwise_and)
    ts(v("CC", 0, 64), v("c64b"), 4096.0, OP.mult, -2033.0, OP.add)
    n = 64
    while n < S:
        act(v("CC", n, 2 * n), v("CC", 0, n), AF.Copy)
        n *= 2
    for c in WEIGHTS[BF]:
        diag(c)
    for b in ("Xp", "Ip"):
        for h in range(2):
            act(v(b, S + H * h, S + H * h + H), v("ones"), AF.Copy)
    ts(v("MK"), v("xp"), 1.0, OP.min)
    iota(v("l16"), [[16, 16]], S, 0)
    ts(v("LL"), v("l16"), v("pmF"), OP.add)
    for k in range(2):
        iota(f("KC", k, 64), [[0, 8], [-2048, 8]], 2048 * (15 - 8 * k), 0)
    iota(f("KC", 2, 64), [[1, 8], [0, 8]], 0, 0)
    if any(hi - lo < H for lo, hi in PARTS):
        iota(f("KC", 3, 64), [[0, 4], [-2048, 16]], 2048 * 15, 0)
    now[1] = 0
    for c in range(16):
        act(f("DG", c, 16), v("DGm"), AF.Copy, scale=f("LL", c, 1))
    for k in range(3):
        act(f("OWN", k, 768), f("FT", k, 768), AF.Copy, scale=0.0)
    for t in range(RO):
        act(f("TG", t), v("ONEB"), AF.Copy, scale=t + 1.0)
    for k in range(8):
        iota(f("PI", k, 256), [[1, 256]], 256 * k, 0)

    def entries(o, x, tmp, bank):
        ts(tmp, x, -1024.5, OP.add, 2048.0 * BIG, OP.add)
        act(bank, tmp, bias=2048.0 - MID - 2048.0 * BIG)
        tt(o, x, bank, OP.add)
    now[1] = 2
    for h in range(2):
        entries(v("Oa", 16 + H * h, 16 + H * h + H), f("ENT", h, 1024, 0, 8), f("n1", h), f("pA", h))
    now[1] = 0
    for k in range(4):
        entries(f("Xp", k, 512), f("ENT", k, 512), f("W1", k, 512), v(("pW", "pD", "pZ", "pD")[k]))

    def number(o, x, tmp, bank):
        act(tmp, x, scale=2.0 ** -12, bias=BIG)
        act(bank, tmp, scale=2048.0, bias=-2048.0 * BIG - MID / 2)
        tt(o, x, bank, OP.subtract)

    def settle(t, plane, lo, hi):
        cur, bank = v(plane, 8 * lo + t, 8 * hi, 8), v("pD", L + lo, L + hi)
        act(bank, cur, scale=-2.0, bias=OUT)
        tt(bank, v("Ln%d" % t, lo, hi), bank, OP.min)
        tt(cur, cur, bank, OP.max)

    for t in range(RO):
        clock = C0 + t
        now[0] = t
        thr = clock - 5
        last = t == RO - 1
        plane = "Ip" if last else "Xp"
        d = 1 + t % 3
        to, frm = cores[(rank + d) % 4], cores[(rank - d) % 4]

        now[1] = 2 * (t in FIRST)
        for k, (lo, hi) in enumerate(AMSG):
            if t:
                act(v("Oa", 16 + lo, 16 + hi), v("Xp", 8 * lo + t, 8 * hi, 8), AF.Copy)
            send("a", t, k, 16 + lo if lo else 0, 16 + hi, to, frm)
        for lo, hi in IDX:
            lanes = v("Xp", 8 * lo + t, 8 * hi, 8) if t else v("Oa", 16 + lo, 16 + hi)
            ts(v("s1", lo, hi), lanes if t else v("ENT", 8 * lo, 8 * hi, 8), -1.0, OP.add)
            act(v("n1", lo, hi), lanes, scale=2.0 ** -12, bias=BIG)
            act(v("pU", lo, hi), v("n1", lo, hi), scale=2.0 ** -9, bias=(2063 - BIG) / 512)
            ts(v("kd", lo, hi), v("s1", lo, hi), 16, OP.bitwise_and)
            tt(v("wi", lo, hi), v("pU", lo, hi), v("kd", lo, hi), OP.subtract)
            ts(v("idx", lo, hi), v("wi", lo, hi), 512.0, OP.mult, 0.0, OP.max)
        for p, (lo, hi) in enumerate(PARTS):
            c0, c1 = lo // 16, hi // 16
            for q in range(lo // 32, hi // 32):
                o, win = f("GF", q, 512), at(v("FT"), f("idx", q, 32))
                if q in VG:
                    tc(o, win)
                else:
                    act(o, win, AF.Copy)
                scan(f("YS", q, 512), v("MB"), o)
            u = v("pS%d" % (p % 2), 448 + c0, 448 + c1)
            for x in range(16):
                mm(u, f("WX", x), v("YS", 16 * lo + 16 * x + 15, 16 * hi, 256), x == 0, x == 15)
            um, s5 = v("Ou", 16 * p, 16 * p + c1 - c0), v("Ou", 16 * p + 8, 16 * p + 8 + c1 - c0)
            if LATE[p]:
                tc(um, u)
            else:
                tc(v("ui", c0, c1), u)
                ts(um, v("ui", c0, c1), 4095, OP.bitwise_and)
                tt(v("sq", c0, c1), um, um, OP.mult)
                ts(s5, v("sq", c0, c1), 5, OP.arith_shift_right)
            send("u", t, p, 16 * p, 16 * p + (8 if LATE[p] else 16), to, frm)
            now[1] = 0
        if t:
            for lo, hi in NMSG:
                settle(t - 1, "Xp", lo, hi)
        if last:
            for k in range(4):
                number(f("Ip", k, 512), f("Xp", k, 512), f("W1", k, 512), v("pS1" if k % 2 else "pD"))

        def side(b, lo, hi, s):
            return v(b, 2 * lo + s * (hi - lo), 2 * lo + (s + 1) * (hi - lo))

        for n in sorted({hi - lo for lo, hi in PARTS}):
            act(v("KK%d" % n), at(v("La%d" % t, 0, 16), v("RK%d" % n)), AF.Copy)
        for p, (lo, hi) in enumerate(PARTS):
            a, c1, l1 = v("La%d" % t, 16 + lo, 16 + hi), v("c1", lo, hi), v("l1", lo, hi)
            act(c1, a, scale=1 / 16, bias=7.5 / 16)
            act(c1, c1, bias=BIG)
            act(c1, c1, bias=-BIG)
            if VD[p]:
                act(v("OR", 4 * lo, 4 * hi), at(c1, v("RC", 0, (hi - lo) // 4)), scale=16.0, bias=-7.5)
        for lo, hi in MP:
            a, l1 = v("La%d" % t, 16 + lo, 16 + hi), v("l1", lo, hi)
            p0, p1, lam, keep = side("pW", lo, hi, 0), side("pW", lo, hi, 1), side("LAM", lo, hi, 0), v("KP", lo, hi)
            act(p1, v("CC", 8 * lo + t, 8 * hi, 8), AF.Copy)
            tt(v("sia", lo, hi), a, p1, OP.add)
            ts(v("za", lo, hi), v("sia", lo, hi), 7 << 15, OP.bitwise_and)
            if FASTA[lo // H]:
                ts(v("loa", lo, hi), v("sia", lo, hi), 31, OP.bitwise_and)
                ts(p1, v("loa", lo, hi), thr, OP.is_ge, 262144.0, OP.mult)
                ts(lam, v("loa", lo, hi), -15.0, OP.add)
            else:
                act(l1, a, scale=1 / 32, bias=-0.5 / 32)
                act(l1, l1, bias=BIG)
                act(p0, l1, scale=32.0, bias=-32.0 * BIG)
                tt(lam, a, p0, OP.subtract)
                act(p1, lam, AF.Relu, scale=262144.0, bias=262144.0 * (16 - thr))
            tt(keep, v("za", lo, hi), p1, OP.is_le)
            a1, a1N, one = v("pA", lo, hi), v("pA", L + lo, L + hi), v("ONEB", 0, hi - lo)
            total(a1, [(-MID, one), (2.0 ** 25, keep)])
            tt(a1, a, a1, OP.min)
            act(a1N, a1, bias=MID)
            if last:
                number(v("anum", lo, hi), a, v("an1", lo, hi), p0)
                total(a1, [(2.0 ** 25, keep)])
                tt(a1, v("anum", lo, hi), a1, OP.min)
            act(side("SIG", lo, hi, 0), lam, AF.Sign, bias=15.5 - thr)
            act(side("IOT", lo, hi, 1), lam, AF.Sign, bias=-0.5)
            act(side("EM0", lo, hi, 0), a, AF.Relu, scale=-1.0, bias=1.0 - MID)

        for p, (lo, hi) in enumerate(PARTS):
            bank, n, c0, c1 = "pS%d" % (p % 2), hi - lo, lo // 16, hi // 16

            def r(b, o=0, st=1):
                return v(b, lo + o, hi, st)
            um, s5 = at(f("Lu%d" % t, 2 * p, 8), v("RU%d" % n)), at(f("Lu%d" % t, 2 * p + 1, 8), v("RU%d" % n))
            if LATE[p]:
                ts(r("U1"), um, 4095, OP.bitwise_and)
                um, s5 = r("U1"), r("U3")
                tt(r("U2"), um, um, OP.mult)
                ts(s5, r("U2"), 5, OP.arith_shift_right)
            tt(r("E1"), um, v("KK%d" % n), OP.mult)
            e1 = r("E1")
            if t:
                e1 = v("pZ", 2 * lo, lo + hi) if LATE[p] else e1
                act(e1, r("E1"), bias=v("LA%d" % (t - 1), 0, 1))
            tt(r("E2"), s5, e1, OP.add)
            ts(r("E3"), r("E2"), 2047, OP.bitwise_and)
            tc(r("EL"), r("E3"))
            tc(r("E16"), r("E3"))
            rows = (0, 8) if n == H else (4 * (p % 2), 4 * (p % 2) + 4)
            if len(VD[p]) < 4:
                for m in range(4):
                    act(w("pO", rows, m), r("c1"), scale=16.0, bias=-7.5)
            step = 512 // (4 * n)
            for q in range(4):
                a = 16 * lo + 4 * n * q
                if q not in VD[p] and (q % step == 0 or q - 1 in VD[p]):
                    k = step - q % step
                    act(v("GS", a, a + 4 * n * k), at(v("Xp"), v("EL", lo + n * q // 4, lo + n * (q + k) // 4)), AF.Copy)
            for k in range(n // 64):
                g0, gm = 1024 // n * k, 1024 // n
                for q in range(g0 // 4, (g0 + gm) // 4):
                    a, ms = 16 * lo + 4 * n * q, (4 * q, 4 * q + 4)
                    o = v("D", a, a + 4 * n)
                    if q in VD[p]:
                        tt(o, at(v("Xp"), v("EL", lo + n * q // 4, lo + n * (q + 1) // 4)), v("OR", 4 * lo, 4 * hi), OP.subtract)
                    else:
                        tt(o, v("GS", a, a + 4 * n), w("pO", rows), OP.subtract)
                    ts(w("Q1", (c0, c1), ms), o, 4096.0 * (BIG + 1), OP.add, 4096.0 * (BIG + 1), OP.is_equal)
                    if (p, k) in Q2S:
                        act(v("AB", a, a + 4 * n), o, AF.Abs)
                        act(w("Q2", (c0, c1), ms), v("AB", a, a + 4 * n), AF.Sign, bias=-8.25)
                    else:
                        ts(w("Q2", (c0, c1), ms), o, 16.0 * BIG, OP.add, 16.0 * BIG, OP.not_equal)
                key = f(bank, k, 64)
                mm(key, diag(1.0), f("KC", k if n == H else 3, 64), True, False)
                if n == H:
                    mm(key, diag(2.0 ** 21), f("KC", 2, 64), False, False)
                for m in range(g0, g0 + gm):
                    a = lo + n // 4 * (m // 4)
                    mm(f(bank, k, 64, m - g0, gm), v("IDH"), v("E16", a + m % 4, a + n // 4, 4), False, False)
                if (p, k) in Q2S:
                    mm(key, diag(2.0 ** 18), v("ONEB", 0, 64), False, False)
                for Q in ("Q1", "Q2"):
                    for x in range(16):
                        mm(key, f("SH" if Q == "Q2" and (p, k) in Q2S else "SC", x), w(Q, (c0, c1), (g0, g0 + gm), x), False, Q == "Q2" and x == 15)
                if n == H and k == 0:
                    act(f("k0", p, 64), key, AF.Copy)
            if n == H:
                scan(f("k4", p, 64), f("k0", p, 64), f(bank, 1, 64), OP.max)
            else:
                scan(f("k4", p, 64), v("MK", 0, 64), f(bank, 0, 64))
            ts(v("k5", c0, c1), f("k4", p, 64, gm - 1, gm), 2047, OP.bitwise_and)
            if hi not in [b for a, b in MP]:
                continue
            p = [b for a, b in MP].index(hi)
            lo = MP[p][0]
            bank, n, c0 = "pS%d" % (p % 2), hi - lo, lo // 16
            pl = v("pl", c0, c1)
            tc(pl, v("k5", c0, c1))
            tc(v("P1", c0, c1), v("k5", c0, c1))
            tc(r("PB"), at(v("PI"), pl))
            act(r("CP"), at(v("CC"), pl), AF.Copy)
            act(r("bN"), at(v("Xp"), pl), bias=MID)
            tt(r("sib"), at(v("Xp"), pl), r("CP"), OP.add)
            if last:
                act(r("bnum"), at(v("Ip"), pl), AF.Copy)
            if p:
                act(r("ow"), at(v("OWN"), pl), AF.Relu, bias=-float(t))
            mine = [c for c in range(c0, c1) if c in EQS]
            if mine:
                act(v("PBf", 16 * mine[0], hi), at(v("PI"), v("pl", mine[0], c1)), AF.Copy)
            for c in range(c0, c1):
                eq = w("EQ", c, (0, hi - 16 * c))
                if c in mine:
                    act(eq, v("PBf", 16 * c, hi), AF.Abs, scale=-1.0, bias=f("P1", c, 1))
                    act(eq, eq, AF.Relu, scale=-1.0, bias=1.0)
                else:
                    ts(eq, v("PB", 16 * c, hi), f("P1", c, 1), OP.is_equal)
            tt(r("EQd"), w("EQ", (c0, c1), (0, 16)), v("pU", 384, 384 + n), OP.mult)
            cnt = r("pD")
            mm(cnt, v("IDH"), r("PB"), True, False)
            for c in range(c0, c1 - 1):
                mm(v("pD", 16 * c + 16, hi), v("BDk"), w("EQ", c, (16, hi - 16 * c)), False, False)
            if p:
                mm(cnt, v("BDk"), r("ow"), False, False)
            mm(cnt, v("BDk"), r("EQd"), False, True)
            tt(r("wd"), cnt, r("DG"), OP.min)
            act(r("lose"), cnt, AF.Sign, bias=-2047.5, accum=f("lc", p, 1))
            scan(r("sc"), v("MK", 0, n), r("wd"))
            tc(v("PL", c0, c1), r("sc", 15, 16))
            if hi < L:
                tc(at(v("OWN"), v("PL", c0, c1)), v("TG", H * t, H * t + n))
            lam, keep = side("LAM", lo, hi, 1), v(bank, 2 * H, 2 * H + n)
            ts(r("zb"), r("sib"), 7 << 15, OP.bitwise_and)
            if FAST[p]:
                ts(r("lob"), r("sib"), 31, OP.bitwise_and)
                ts(keep, r("lob"), thr, OP.is_ge, 262144.0, OP.mult)
                ts(lam, r("lob"), -15.0, OP.add)
            else:
                act(r("l1b"), at(v("Xp"), pl), scale=1 / 32, bias=-0.5 / 32)
                act(r("l1b"), r("l1b"), bias=BIG)
                act(v(bank, H, H + n), r("l1b"), scale=32.0, bias=MID - 32.0 * BIG)
                tt(lam, r("bN"), v(bank, H, H + n), OP.subtract)
                act(keep, lam, AF.Relu, scale=262144.0, bias=262144.0 * (16 - thr))
            tt(keep, r("zb"), keep, OP.is_le)
            tt(r("b1"), r("bN"), keep, OP.mult)
            if last:
                tt(r("b1c"), r("bnum"), keep, OP.mult)
            else:
                act(r("b1c"), r("b1"), bias=-MID)
            act(side("SIG", lo, hi, 1), lam, AF.Sign, bias=15.5 - thr)
            act(side("IOT", lo, hi, 0), lam, AF.Sign, bias=-0.5)
            act(side("EM0", lo, hi, 1), r("bN"), AF.Relu, scale=-1.0, bias=1.0)
            act(r("EM"), r("b1"), AF.Relu, scale=-1.0, bias=1.0)
            tt(r("d0"), r("b1"), v("pA", L + lo, L + hi), OP.subtract)
            if SAME[p]:
                act(r("d0"), r("d0"), AF.Abs)
                act(r("same"), r("d0"), AF.Sign, scale=-1.0, bias=2048.0)
            else:
                ts(r("same"), r("d0"), 4096.0 * BIG, OP.add, 4096.0 * BIG, OP.is_equal)
            oa, ob = side("pW", lo, hi, 0), side("pW", lo, hi, 1)
            for k, (c, b) in enumerate(((-1.0, "LAM"), (-16.0, "SIG"), (8.0, "IOT"))):
                mm(v("pW", 2 * lo, 2 * hi), diag(c), v(b, 2 * lo, 2 * hi), k == 0, k == 2 and not last)
            if last:
                mm(oa, diag(16.0), r("KP"), False, False)
                mm(ob, diag(-16.0), r("EM"), False, True)
            act(r("oa"), oa, AF.Relu, bias=clock - 39.0 - 16 * last)
            act(ob, ob, AF.Relu, bias=clock - 39.0)
            tt(r("ah"), r("oa"), r("pA"), OP.add)
            tt(ob, r("b1c"), ob, OP.add)
            tt(r("big"), r("ah"), ob, OP.max)
            zz, zk, one = side("pZ", lo, hi, 0), side("pZ", lo, hi, 1), v("ONEB", 0, n)
            total(zz, [(-2.0 ** 26 if SAME[p] else -7.0 * 2 ** 24, one), (2.0 ** 25, side("EM0", lo, hi, 0)), (2.0 ** 24, side("SIG", lo, hi, 0)), (-2.0 ** 26, r("KP")),
                       (-2.0 ** 25, side("EM0", lo, hi, 1)), (2.0 ** 24, side("SIG", lo, hi, 1)), (2.0 ** 26, r("EM")),
                       (3.0 * 2 ** (24 if SAME[p] else 25), r("same")), (-2.0 ** 27, r("lose"))])
            tt(r("TT"), r("big"), zz, OP.min)
            total(zk, [(2.0 ** (24 if last else 23), one), (2.0 ** 25, r("KP")), (2.0 ** 24, r("lose"))])
            tt(zk, r("anum") if last else v("La%d" % t, 16 + lo, 16 + hi), zk, OP.min)
            tt(r("On"), r("TT"), zk, OP.max)
        for k, (lo, hi) in enumerate(NLAST if last else NMSG):
            send("n", t, k, lo, hi, frm, to)
        mine = v(plane, t, S, 8)
        asel(mine, mine, [[0, L]], OP.is_gt, 0, 0, OUT)
        for lo, hi in MP:
            tt(at(v(plane), v("PL", lo // 16, hi // 16)), v("b1c", lo, hi), v("TT", lo, hi), OP.max)
        if not last:
            col = v("pU", 300, 301)
            for p in range(len(MP)):
                mm(col, v("SEL0"), f("lc", p, 1), p == 0, p == len(MP) - 1)
            act(v("an"), col, AF.Copy, scale=-0.5)
            act(v("aq"), v("an"), scale=1 / 32, bias=-15.5 / 32)
            act(v("aq"), v("aq"), bias=BIG)
            act(v("aq"), v("aq"), bias=-BIG)
            act(v("OA", 0, 1), v("aq"), scale=-32.0, bias=v("an"))
            dn = 1 + (t + 1) % 3
            send("A", t, 0, 0, 4, cores[(rank - d + dn) % 4], cores[(rank - dn + d) % 4])

    for k, (lo, hi) in enumerate(NLAST):
        settle(RO - 1, "Ip", lo, hi)
        o = v("Ip", 8 * lo, 8 * hi)
        run("Y", lambda e, o=o, lo=lo, hi=hi: e.dma_start(T.yent[:, 8 * lo:8 * hi], o[0]), o[1], [("yent", 8 * lo, 8 * hi)], 0.1, "dY%d" % k, 16, 2.0 + (hi - lo) / 80)
    issue()
    return

    def settle(t, plane, h):
        cur, bank, new = f(plane, h, 1024, t, 8), f("pD", 2 + h), f("Ln%d" % t, h)
        if PE1[h]:
            act(f("pen", h), cur, AF.Relu, bias=2 * MID)
            total(bank, [(-8.0, f("pen", h)), (1.0, new)])
        else:
            act(bank, cur, scale=-2.0, bias=OUT)
            tt(bank, new, bank, OP.min)
        tt(cur, cur, bank, OP.max)

    for t in range(RO):
        clock = C0 + t
        now[0] = t
        thr = clock - 5
        last = t == RO - 1
        plane = "Ip" if last else "Xp"
        d = 1 + t % 3
        to, frm = cores[(rank + d) % 4], cores[(rank - d) % 4]

        for h in range(2):
            ab = v("Oa", 16 + H * h, 16 + H * h + H)
            lanes = f("Xp", h, 1024, t, 8) if t else ab
            ts(f("s1", h), lanes if t else f("ENT", h, 1024, 0, 8), -1.0, OP.add)
            act(f("n1", h), lanes, scale=2.0 ** -12, bias=BIG)
            act(f("pU", h), f("n1", h), scale=2.0 ** -9, bias=(2063 - BIG) / 512)
            if t and GAB:
                asel(ab, lanes, [[0, H]], OP.is_ge, 0, 0)
            elif t:
                act(ab, lanes, AF.Copy)
            send("a", t, h, (16 + H) * h, 16 + H * h + H, to, frm)
            ts(f("kd", h), f("s1", h), 16, OP.bitwise_and)
            tt(f("wi", h), f("pU", h), f("kd", h), OP.subtract)
            ts(f("idx", h), f("wi", h), 512.0, OP.mult, 0.0, OP.max)
        for h in range(2):
            for q in range(4 * h, 4 * h + 4):
                o, win = f("GF", q, 512), at(v("FT"), f("idx", q, 32))
                if q in VG:
                    tc(o, win)
                else:
                    act(o, win, AF.Copy)
                scan(f("YS", q, 512), v("MB"), o)
            u = v("pU", L + 8 * h, L + 8 * h + 8)
            for x in range(16):
                mm(u, f("WX", x), f("YS", h, 2048, 16 * x + 15, 256), x == 0, x == 15)
            tc(f("ui", h, 8), u)
            um, s5 = f("Ou", 2 * h, 8), f("Ou", 2 * h + 1, 8)
            ts(um, f("ui", h, 8), 4095, OP.bitwise_and)
            tt(f("sq", h, 8), um, um, OP.mult)
            ts(f("s5", h, 8) if t else s5, f("sq", h, 8), 5, OP.arith_shift_right)
            if t:
                ts(s5, f("s5", h, 8), v("LA%d" % (t - 1), 0, 1), OP.add)
            send("u", t, h, 16 * h, 16 * h + 16, to, frm)
        if t:
            for h in range(2):
                settle(t - 1, "Xp", h)
        if last:
            for k in range(4):
                number(f("Ip", k, 512), f("Xp", k, 512), f("W1", k, 512), v("pS1" if k % 2 else "pD"))

        def alone(h, s, x, l2, z, p0, p1, x1, num, n1, k0, k1):
            lam, keep = f("LAM", 2 * h + s), f("KP", 2 * h + s)
            if PE2[2 * h + s]:
                total(p0, [(32 * BIG, one), (-32.0, l2), (1.0, x)])
                act(p1, p0, AF.Relu, scale=262144.0, bias=262144.0 * (16 - thr))
                act(lam, p0, AF.Copy)
            else:
                act(p0, l2, scale=32.0, bias=-32.0 * BIG)
                tt(lam, x, p0, OP.subtract)
                act(p1, lam, AF.Relu, scale=262144.0, bias=262144.0 * (16 - thr))
            tt(keep, z, p1, OP.is_le)
            total(k0, [(-MID, one), (2.0 ** 25, keep)])
            tt(x1, x, k0, OP.min)
            if last:
                total(k1, [(2.0 ** 25, keep)])
                tt(n1, num, k1, OP.min)
            act(f("SIG", 2 * h + s), lam, AF.Sign, bias=15.5 - thr)
            act(f("IOT", 2 * h + 1 - s), lam, AF.Sign, bias=-0.5)
            act(f("EM0", 2 * h + s), x, AF.Relu, scale=-1.0, bias=1.0 - MID)

        act(v("KK"), at(v("La%d" % t, 0, 16), v("RK")), AF.Copy)
        lane = [v("La%d" % t, 16 + H * h, 16 + H * h + H) for h in range(2)]
        a1c = [f("a1c", h) if PE3[h] else f("pA", h) for h in range(2)]
        a1n = [(f("a1n", h) if PE3[h] else f("pA", 2 + h)) if last else a1c[h] for h in range(2)]
        for h in range(2):
            a = lane[h]
            act(f("c1", h), a, scale=1 / 16, bias=7.5 / 16)
            act(f("c1", h), f("c1", h), bias=BIG)
            act(f("c1", h), f("c1", h), bias=-BIG)
            if len(SG[h]) < 4:
                act(f("OR", h, 512), at(f("c1", h), v("RC")), scale=16.0, bias=-7.5)
            p0, p1 = f("pW", 2 * h), f("pW", 2 * h + 1)
            act(p1, f("CC", h, 1024, t, 8), AF.Copy)
            act(f("l1", h), a, scale=1 / 32, bias=-0.5 / 32)
            act(f("l1", h), f("l1", h), bias=BIG)
            tt(f("sia", h), a, p1, OP.add)
            ts(f("za", h), f("sia", h), 7 << 15, OP.bitwise_and)
            if last:
                number(f("anum", h), a, f("an1", h), f("pA", 2 + h))
            alone(h, 0, a, f("l1", h), f("za", h), p0, p1, a1c[h], f("anum", h), a1n[h], f("pA", h), f("pA", 2 + h))

        for h in range(2):
            bank = "pS%d" % h
            tt(f("E1", h), at(f("Lu%d" % t, 2 * h, 8), v("RU")), v("KK"), OP.mult)
            tt(f("E2", h), at(f("Lu%d" % t, 2 * h + 1, 8), v("RU")), f("E1", h), OP.add)
            ts(f("E3", h), f("E2", h), 2047, OP.bitwise_and)
            tc(f("EL", h), f("E3", h))
            tc(f("E16", h), f("EL" if E16U else "E3", h))
            if SG[h]:
                for m in range(4):
                    act(w("pO", (0, 8), m), f("c1", h), scale=16.0, bias=-7.5)
            blk = (8 * h, 8 * h + 8)
            for k in range(2):
                for q in (2 * k, 2 * k + 1):
                    ms = (4 * q, 4 * q + 4)
                    o, win = f("D", 4 * h + q, 512), at(v("Xp"), f("EL", 4 * h + q, 32))
                    if q in SG[h]:
                        act(f("GS", 4 * h + q, 512), win, AF.Copy)
                        tt(o, f("GS", 4 * h + q, 512), w("pO"), OP.subtract)
                    else:
                        tt(o, win, f("OR", h, 512), OP.subtract)
                    ts(w("Q1", blk, ms), o, 4096.0 * (BIG + 1), OP.add, 4096.0 * (BIG + 1), OP.is_equal)
                    ts(w("Q2", blk, ms), o, 16.0 * BIG, OP.add, 16.0 * BIG, OP.not_equal)
                ms = (8 * k, 8 * k + 8)
                key = f(bank, k, 64)
                mm(key, diag(1.0), f("KC", k, 64), True, False)
                mm(key, diag(2.0 ** 21), f("KC", 2, 64), False, False)
                for m in range(8):
                    mm(f(bank, k, 64, m, 8), v("IDH"), f("E16", 4 * h + 2 * k + m // 4, 32, m % 4, 4), False, False)
                for Q in ("Q1", "Q2"):
                    for x in range(16):
                        mm(key, f("SC", x), w(Q, blk, ms, x), False, Q == "Q2" and x == 15)
                if k == 0:
                    act(f("k0", h, 64), key, AF.Copy)
            scan(f("k4", h, 64), f("k0", h, 64), f(bank, 1, 64), OP.max)
            ts(f("k5", h, 8), f("k4", h, 64, 7, 8), 2047, OP.bitwise_and)
            pl = f("pl", h, 8)
            tc(pl, f("k5", h, 8))
            tc(f("P1", h, 8), f("k5", h, 8))
            tc(f("PB", h), at(v("PI"), pl))
            act(f("l1b", h), at(v("Xp"), pl), scale=1 / 32, bias=-0.5 / 32)
            act(f("CP", h), at(v("CC"), pl), AF.Copy)
            act(f("bX", h), at(v("Xp"), pl), AF.Copy)
            tt(f("sib", h), at(v("Xp"), pl), f("CP", h), OP.add)
            if last:
                act(f("bnum", h), at(v("Ip"), pl), AF.Copy)
            if h:
                act(f("ow", h), at(v("OWN"), pl), AF.Relu, bias=-float(t))
            hi = H * h + H
            mine = [c for c in range(*blk) if c in EQS]
            if mine:
                act(v("PBf", 16 * mine[0], hi), at(v("PI"), v("pl", mine[0], blk[1])), AF.Copy)
            for c in range(*blk):
                eq = w("EQ", c, (0, hi - 16 * c))
                if c in mine:
                    act(eq, v("PBf", 16 * c, hi), AF.Abs, scale=-1.0, bias=f("P1", c, 1))
                    act(eq, eq, AF.Relu, scale=-1.0, bias=1.0)
                else:
                    ts(eq, v("PB", 16 * c, hi), f("P1", c, 1), OP.is_equal)
            tt(f("EQd", h), w("EQ", blk, (0, 16)), tri, OP.mult)
            cnt = f("pD", h)
            mm(cnt, v("IDH"), f("PB", h), True, False)
            if h:
                mm(cnt, v("BDk"), f("ow", h), False, False)
            for c in range(blk[0], blk[1] - 1):
                mm(v("pD", 16 * c + 16, hi), v("BDk"), w("EQ", c, (16, hi - 16 * c)), False, False)
            mm(cnt, v("BDk"), f("EQd", h), False, True)
            tt(f("wd", h), cnt, f("DG", h), OP.min)
            act(f("lose", h), cnt, AF.Sign, bias=-2047.5, accum=f("lc", h, 1))
            scan(f("sc", h), v("MK"), f("wd", h))
            tc(f("PL", h, 8), f("sc", h, H, 15, 16))
            if h == 0:
                tc(at(v("OWN"), f("PL", h, 8)), f("TG", t))
            b1c, b1n = f("b1c", h), f("b1n" if last else "b1c", h)
            act(f("l1b", h), f("l1b", h), bias=BIG)
            ts(f("zb", h), f("sib", h), 7 << 15, OP.bitwise_and)
            alone(h, 1, f("bX", h), f("l1b", h), f("zb", h), f(bank, 1), f(bank, 2), b1c, f("bnum", h), b1n, f(bank, 1), f(bank, 2))
            if PE3[h]:
                d0 = f(bank, 3)
                total(d0, [(-1.0, a1c[h]), (1.0, b1c)])
            else:
                d0 = f("d0", h)
                tt(d0, b1c, a1c[h], OP.subtract)
            if SAME[h]:
                act(d0, d0, AF.Abs)
                act(f("same", h), d0, AF.Sign, scale=-1.0, bias=2048.0)
            else:
                ts(f("same", h), d0, 4096.0 * BIG, OP.add, 4096.0 * BIG, OP.is_equal)
            total(f("pW", h, L), [(c, f(b, h, L)) for c, b in [(-1.0, "LAM"), (-16.0, "SIG"), (8.0, "IOT")] + [(16.0, "KP")] * last])
            oa, ob = f("pW", 2 * h), f("pW", 2 * h + 1)
            act(f("oa", h), oa, AF.Relu, bias=clock - 39.0 - 16 * last)
            act(ob, ob, AF.Relu, bias=clock - 39.0 - 16 * last)
            if PE3[h]:
                total(f("pA", h), [(1.0, a1n[h]), (1.0, f("oa", h))])
                tt(f("ah", h), b1n, ob, OP.add)
                tt(f("big", h), f("ah", h), f("pA", h), OP.max)
            else:
                tt(f("ah", h), f("oa", h), a1n[h], OP.add)
                tt(ob, b1n, ob, OP.add)
                tt(f("big", h), f("ah", h), ob, OP.max)
            zz, zk = f("pZ", 2 * h), f("pZ", 2 * h + 1)
            total(zz, [(-3.0 * 2 ** 24, one)] * (not SAME[h])
                  + [(c, f(b, 2 * h + s)) for s in range(2) for c, b in ((2.0 ** 25, "EM0"), (2.0 ** 24, "SIG"), (-2.0 ** 26, "KP"))]
                  + [(3.0 * 2 ** (24 if SAME[h] else 25), f("same", h)), (-2.0 ** 27, f("lose", h))])
            tt(f("TT", h), f("big", h), zz, OP.min)
            total(zk, [(2.0 ** (24 if last else 23), one), (2.0 ** 25, f("KP", 2 * h)), (2.0 ** 24, f("lose", h))])
            tt(zk, f("anum", h) if last else lane[h], zk, OP.min)
            tt(f("On", h), f("TT", h), zk, OP.max)
            send("n", t, h, H * h, H * h + H, frm, to)
        mine = v(plane, t, S, 8)
        asel(mine, mine, [[0, L]], OP.is_gt, 0, 0, OUT)
        for h in range(2):
            tt(at(v(plane), f("PL", h, 8)), f("b1n" if last else "b1c", h), f("TT", h), OP.max)
        if not last:
            col = v("pU", 300, 301)
            for h in range(2):
                mm(col, v("SEL0"), f("lc", h, 1), h == 0, h == 1)
            act(v("an"), col, AF.Copy, scale=-0.5)
            act(v("aq"), v("an"), scale=1 / 32, bias=-15.5 / 32)
            act(v("aq"), v("aq"), bias=BIG)
            act(v("aq"), v("aq"), bias=-BIG)
            act(v("OA", 0, 1), v("aq"), scale=-32.0, bias=v("an"))
            send("A", t, 0, 0, 4, frm, to)

    for h in range(2):
        settle(RO - 1, "Ip", h)
        lo, hi = 1024 * h, 1024 * h + 1024
        run("Y", lambda e, lo=lo, hi=hi: e.dma_start(T.yent[:, lo:hi], T.Ip[:, lo:hi]), regs(v("Ip", lo, hi)), [("yent", lo, hi)], 0.1, "dY%d" % h, 16, 4.0)
    issue()
